import numpy as np
import ml_dtypes


def mxq(x, axis, fmt="e4m3"):
    dtype, down = {"e4m3": (ml_dtypes.float8_e4m3fn, 7), "e5m2": (ml_dtypes.float8_e5m2, 14)}[fmt]
    v = np.moveaxis(np.asarray(x, np.float32).astype(ml_dtypes.bfloat16).astype(np.float64), axis, -1)
    blocks = v.reshape(v.shape[:-1] + (-1, 32))
    amax = np.abs(blocks).max(-1, keepdims=True)
    byte = np.maximum(np.where(amax > 0, np.frexp(amax)[1] - 1 + 127, 0) - down, 1)
    scale = np.exp2(byte - 127.0)
    codes = (blocks / scale).astype(np.float32).astype(dtype).astype(np.float64)
    return np.moveaxis((codes * scale).reshape(v.shape), -1, axis)


WIDE = False


def mx_kscale(k):
    if not WIDE:
        return np.ones(k)
    levels = np.array([24, -24, 12, -12, 0])
    if k % 512:
        return np.exp2(np.random.permutation(np.resize(levels, k // 32))).repeat(32)
    a = np.empty((k // 512, 16))
    for p in range(k // 512):
        a[p, :8] = np.random.permutation(np.resize(levels, 8))
        for g in range(8):
            far = levels[np.abs(levels - a[p, g]) >= 10]
            a[p, g + 8] = far[np.random.randint(len(far))]
    return np.exp2(a.ravel()).repeat(32)


def f64(x):
    return np.asarray(x).astype(np.float64)


def striped(idx):
    return np.tile(idx.reshape(-1, 16).T, (8, 1)).astype(np.uint16)


def unstriped(offs):
    return offs[:16].T.reshape(-1).astype(np.int64)


E2M1 = np.array([0.0, 0.5, 1.0, 1.5, 2.0, 3.0, 4.0, 6.0, -0.0, -0.5, -1.0, -1.5, -2.0, -3.0, -4.0, -6.0])


def pack_weight(w, fmt):
    k, n = w.shape
    w = f64(np.asarray(w, np.float32).astype(ml_dtypes.bfloat16)).reshape(k // 32, 32, n)
    amax = np.abs(w).max(1)
    if fmt == "e4m3":
        byte = np.frexp(amax)[1] - 1 + 127 - 7
    else:
        mant, ex = np.frexp(amax / 6.0)
        byte = np.where(mant > 0.5, ex, ex - 1) + 127
    byte = np.clip(np.where(amax > 0, byte, 1), 1, 254)
    scaled = (w * np.exp2(127.0 - byte)[:, None, :]).reshape(k, n).astype(np.float32)
    by_word = np.ascontiguousarray(scaled.reshape(k // 512, 128, 4, n).transpose(0, 1, 3, 2))
    if fmt == "e4m3":
        words = by_word.astype(ml_dtypes.float8_e4m3fn).view(np.uint8)
    else:
        c = by_word.astype(ml_dtypes.float4_e2m1fn).view(np.uint8) & 0xF
        words = (c[..., 0::2] | (c[..., 1::2] << 4)).reshape(k // 512, 128, 2 * n)
    return np.ascontiguousarray(words), np.ascontiguousarray(byte.astype(np.uint8).reshape(k // 512, 16, n))


def unpack_weight(words, scales, fmt):
    g, _, n = scales.shape
    words = np.ascontiguousarray(words).reshape(g, 128, n, -1)
    if fmt == "e4m3":
        vals = words.view(ml_dtypes.float8_e4m3fn).astype(np.float64)
    else:
        nib = np.empty((g, 128, n, 4), np.uint8)
        nib[..., 0::2] = words & 0xF
        nib[..., 1::2] = words >> 4
        vals = E2M1[nib]
    vals = vals * np.repeat(np.exp2(scales.astype(np.float64) - 127.0), 8, axis=1)[..., None]
    return vals.transpose(0, 1, 3, 2).reshape(g * 512, n)


def pack_table4(v):
    words, scales = pack_weight(v, "e2m1")
    g, t = words.shape[0] // 2, v.shape[1]
    return np.ascontiguousarray(words.reshape(g, 2, 128, t, 2).transpose(0, 2, 3, 1, 4).reshape(g, 128, t, 4)), scales


def unpack_table4(words, scales):
    g, _, t, _ = words.shape
    return unpack_weight(words.reshape(g, 128, t, 2, 2).transpose(0, 3, 1, 2, 4).reshape(2 * g, 128, 2 * t), scales, "e2m1")


def silu(f):
    return f / (1.0 + np.exp(-np.maximum(f, -700.0)))


def sigm(f):
    return 1.0 / (1.0 + np.exp(-np.maximum(f, -700.0)))


K, L, N, T, J = 1024, 512, 512, 2048, 1024


def setup_inputs():
    n = np.random.standard_normal
    s = mx_kscale(K)[:, None]
    s2 = mx_kscale(L)[:, None]
    p_tab = pack_table4(n((K, T)) * s)
    p_tab2 = pack_weight(n((L, T)) * s2, "e4m3")
    p_wv = pack_weight(n((K, N)) / np.sqrt(K) / s, "e4m3")
    p_wt = pack_weight(n((L, N)) / np.sqrt(L) / s2, "e2m1")
    return {
        "tab_words": p_tab[0],
        "tab_scales": p_tab[1],
        "tab2_words": p_tab2[0],
        "tab2_scales": p_tab2[1],
        "zv": (n((K, N)) / np.sqrt(K) / s).astype(np.float32),
        "zt": (n((L, N)) / np.sqrt(L) / s2).astype(np.float32),
        "b": (0.3 * n(N)).astype(np.float32),
        "wv_words": p_wv[0],
        "wv_scales": p_wv[1],
        "wt_words": p_wt[0],
        "wt_scales": p_wt[1],
        "wgo": np.tile(np.random.uniform(0.5, 2.0, J), (128, 1)).astype(np.float32),
        "offs": striped(np.random.permutation(T)[:J]),
        "offs2": striped(np.random.permutation(T)[:J]),
    }


def reference(tab_words, tab_scales, tab2_words, tab2_scales, zv, zt, b, wv_words, wv_scales, wt_words, wt_scales, wgo, offs, offs2):
    idx = unstriped(offs)
    idx2 = unstriped(offs2)
    tab_ = unpack_table4(tab_words, tab_scales)[:, idx]
    tab2_ = unpack_weight(tab2_words, tab2_scales, "e4m3")[:, idx2]
    zv_ = mxq(f64(zv), 0, "e4m3")
    zt_ = mxq(f64(zt), 0, "e4m3")
    z = zv_.T @ tab_ + zt_.T @ tab2_
    gate = sigm(z + f64(b)[:, None])
    wv_ = unpack_weight(wv_words, wv_scales, "e4m3")
    wt_ = unpack_weight(wt_words, wt_scales, "e2m1")
    hv = wv_.T @ tab_
    ht = wt_.T @ tab2_
    av = silu(hv)
    at = silu(ht)
    out = np.zeros((N, T))
    out[:, idx] = f64(wgo)[0] * (at + gate * (av - at))
    return out

@@ -1,0 +1,241 @@
+from contextlib import ExitStack
+
+import concourse.mybir as mybir
+from concourse.masks import make_identity
+
+K, L, N, T, J = 1024, 512, 512, 2048, 1024
+FLOPS = 2 * 2 * (K + L) * N * J
+
+F32 = mybir.dt.float32
+BF16 = mybir.dt.bfloat16
+I32 = mybir.dt.int32
+U32 = mybir.dt.uint32
+U16 = mybir.dt.uint16
+U8 = mybir.dt.uint8
+FP8X4 = mybir.dt.float8_e4m3fn_x4
+FP4X4 = mybir.dt.float4_e2m1fn_x4
+ACT = mybir.ActivationFunctionType
+ALU = mybir.AluOpType
+
+P = 128
+PACK = 4
+HALF = 512
+LIST_COLS = HALF // 16
+Z_LOADS = (((0, 0, 256), (1, 0, 128), (2, 0, 128)), ((1, 128, 256), (2, 128, 256)), ((0, 256, 512), (1, 256, 512), (2, 256, 512)))
+Z_QUANT = (((0, 0), (1, 0), (0, 1), (0, 2)), ((1, 1), (1, 2)), ((2, 0), (3, 0), (2, 1), (2, 2)), ((3, 1), (3, 2)))
+CHUNKS = [(nt, h) for nt in range(N // P) for h in range(J // HALF)]
+STEPS = ("vvvv",) + ("gggv",) * 7
+
+
+def tile_list_gmu_silu_scat_kernel(
+    tc, tab_words, tab_scales, tab2_words, tab2_scales, zv, zt, b, wv_words, wv_scales, wt_words, wt_scales, wgo, offs, offs2, out
+):
+    nc = tc.nc
+    with ExitStack() as ctx:
+        keep = ctx.enter_context(tc.tile_pool(name="keep", bufs=1))
+        work = ctx.enter_context(tc.tile_pool(name="work", bufs=4))
+        psum = ctx.enter_context(tc.psum_pool(name="psum", bufs=2))
+        psum_keep = ctx.enter_context(tc.psum_pool(name="psum_keep", bufs=1))
+
+        list1 = keep.tile([P, J // 16], U16, name="list1")
+        list2 = keep.tile([P, J // 16], U16, name="list2")
+        tabw = keep.tile([P, T], U32, name="tabw")
+        tab2w = keep.tile([P, T], U32, name="tab2w")
+        tabs = keep.tile([P, T], U8, name="tabs")
+        tab2s = keep.tile([P, T], U8, name="tab2s")
+        vs0 = keep.tile([P, J], U8, name="vs0", align_bytes=64)
+        vs1 = keep.tile([P, J], U8, name="vs1", align_bytes=64)
+        ts = [keep.tile([P, HALF], U8, name=f"ts{h}", align_bytes=64) for h in range(2)]
+        wvs = keep.tile([P, 2, N], U8, name="wvs", align_bytes=64)
+        wts = keep.tile([P, N], U8, name="wts", align_bytes=64)
+        wvw = keep.tile([P, 2, N], U32, name="wvw", align_bytes=64)
+        wtw = keep.tile([P, 2 * N], U8, name="wtw", align_bytes=64)
+        wgo_col = keep.tile([P, 2, 4], F32, name="wgo_col")
+        ident = keep.tile([P, P], F32, name="ident")
+        wgo_ps = [psum_keep.tile([P, HALF], F32, name=f"wgo_ps{h}") for h in range(2)]
+        bias = keep.tile([P, N // P], F32, name="bias")
+        half_bias = keep.tile([P, N // P], F32, name="half_bias")
+        warm_in = keep.tile([P, 1], F32, name="warm_in")
+        warm_out = keep.tile([P, 1], F32, name="warm_out")
+        windows = [keep.tile([P, T], F32, name=f"window{i}") for i in range(2)]
+
+        nc.vector.memset(tabs[:].bitcast(I32), 0)
+        nc.vector.memset(warm_in[:], 0.0)
+        nc.scalar.activation(out=warm_out[:], in_=warm_in[:], func=ACT.Silu)
+        nc.vector.memset(vs1[:].bitcast(I32), 0)
+        nc.vector.memset(wvs[:].rearrange("p a n -> p (a n)").bitcast(I32), 0)
+        nc.vector.memset(windows[0][:], 0.0)
+        nc.gpsimd.memset(tab2s[:].bitcast(I32), 0)
+        nc.gpsimd.memset(wts[:].bitcast(I32), 0)
+        for q in range(4):
+            nc.gpsimd.dma_start(out=tab2s[32 * q : 32 * q + 4, :].bitcast(I32), in_=tab2_scales[0, 4 * q : 4 * q + 4, :].bitcast(I32))
+
+        z_raw = {}
+
+        def load_z(stage_no):
+            for a, n0, n1 in Z_LOADS[stage_no]:
+                tile = keep.tile([P, PACK, n1 - n0], F32, name=f"z_raw{a}_{n0}")
+                rows = zv[512 * a : 512 * (a + 1), n0:n1] if a < 2 else zt[:, n0:n1]
+                nc.sync.dma_start(out=tile[:], in_=rows.rearrange("(p i) n -> p i n", i=PACK))
+                for nt in range(n0 // P, n1 // P):
+                    z_raw[(nt, a)] = tile[:, :, P * nt - n0 : P * (nt + 1) - n0]
+
+        nc.sync.dma_start(list1[:], offs)
+        for q in range(4):
+            nc.sync.dma_start(out=tabs[32 * q : 32 * q + 8, :].bitcast(I32), in_=tab_scales[:, 4 * q : 4 * q + 4, :].bitcast(I32))
+        nc.sync.dma_start(out=tabw[:].bitcast(I32), in_=tab_words[0].rearrange("p t i -> p (t i)").bitcast(I32))
+        with nc.allow_non_contiguous_dma(reason="one value a partition"):
+            nc.sync.dma_start(out=bias[:], in_=b.rearrange("(c p) -> p c", p=P))
+        nc.sync.dma_start(out=wgo_col[:], in_=wgo[0].rearrange("(h p c) -> p h c", p=P, c=4))
+        nc.sync.dma_start(list2[:], offs2)
+        load_z(0)
+        nc.sync.dma_start(out=tab2w[:].bitcast(I32), in_=tab2_words[0].rearrange("p t i -> p (t i)").bitcast(I32))
+        nc.sync.dma_start(out=wvw[:].bitcast(I32), in_=wv_words.rearrange("a p n i -> p a (n i)").bitcast(I32))
+        nc.sync.dma_start(out=wtw[:].bitcast(I32), in_=wt_words[0].bitcast(I32))
+        for q in range(4):
+            nc.sync.dma_start(
+                out=wvs[32 * q : 32 * q + 4, :, :].bitcast(I32),
+                in_=wv_scales[:, 4 * q : 4 * q + 4, :].rearrange("a r n -> r a n").bitcast(I32),
+            )
+        load_z(1)
+        load_z(2)
+
+        z_codes = [keep.tile([P, len(u), P], U32, name=f"z_codes{g}", align_bytes=64) for g, u in enumerate(Z_QUANT)]
+        z_scales = [keep.tile([P, len(u), P], U8, name=f"z_scales{g}", align_bytes=64) for g, u in enumerate(Z_QUANT)]
+        z_bf = [keep.tile([P, len(u), P, PACK], BF16, name=f"z_bf{g}", align_bytes=64) for g, u in enumerate(Z_QUANT)]
+        z_place = {unit: (g, slot) for g, units in enumerate(Z_QUANT) for slot, unit in enumerate(units)}
+
+        def quantize_z(g):
+            for slot, unit in enumerate(Z_QUANT[g]):
+                nc.scalar.activation(out=z_bf[g][:, slot, :, :], in_=z_raw[unit].rearrange("p i n -> p n i"), func=ACT.Copy)
+            nc.vector.quantize_mx(
+                out=z_codes[g][:].rearrange("p s n -> p (s n)").bitcast(FP8X4),
+                scales=z_scales[g][:].rearrange("p s n -> p (s n)"),
+                in_=z_bf[g][:].rearrange("p s n i -> p (s n i)"),
+            )
+
+        vw = [keep.tile([P, 2, 2 * HALF], U8, name=f"vw{h}", align_bytes=64) for h in range(2)]
+        tw = [keep.tile([P, HALF], U32, name=f"tw{h}", align_bytes=64) for h in range(2)]
+        pairs = [keep.tile([P, HALF], U32, name=f"pairs{h}") for h in range(2)]
+
+        def list_half(tile, h):
+            return tile[:, LIST_COLS * h : LIST_COLS * (h + 1)]
+
+        def gather_v(h):
+            nc.vector.tensor_copy(pairs[h][:], tabw[:].indirect(list_half(list1, h)))
+
+        def part_v(h):
+            nc.vector.tensor_copy(vw[h][:].bitcast(U16), pairs[h][:].bitcast(U16).rearrange("p (j d) -> p d j", d=2))
+
+        def gather_t(h):
+            nc.vector.tensor_copy(tw[h][:], tab2w[:].indirect(list_half(list2, h)))
+
+        def gather_ts(h):
+            nc.vector.tensor_copy(ts[h][:], tab2s[:].indirect(list_half(list2, h)))
+
+        stage = {}
+
+        def front(c):
+            nt, h = CHUNKS[c]
+            jc = slice(HALF * h, HALF * (h + 1))
+            ncols = slice(P * nt, P * (nt + 1))
+            v_ops = [(vw[h][:, 0, :].bitcast(FP4X4), vs0[:, jc]), (vw[h][:, 1, :].bitcast(FP4X4), vs1[:, jc])]
+            t_op = (tw[h][:].bitcast(FP8X4), ts[h][:])
+            hv = psum.tile([P, HALF], F32, name="hv")
+            ht = psum.tile([P, HALF], F32, name="ht")
+            z = psum.tile([P, HALF], F32, name="z")
+            for a in range(2):
+                nc.tensor.matmul_mx(
+                    out=hv[:], lhsT=wvw[:, a, ncols].bitcast(FP8X4), lhsT_scale=wvs[:, a, ncols],
+                    rhs=v_ops[a][0], rhs_scale=v_ops[a][1], start=(a == 0), stop=(a == 1),
+                )
+            nc.tensor.matmul_mx(
+                out=ht[:], lhsT=wtw[:, 2 * P * nt : 2 * P * (nt + 1)].bitcast(FP4X4), lhsT_scale=wts[:, ncols],
+                rhs=t_op[0], rhs_scale=t_op[1], start=True, stop=True,
+            )
+            for a, (codes, scales) in enumerate(v_ops + [t_op]):
+                g, slot = z_place[(nt, a)]
+                nc.tensor.matmul_mx(
+                    out=z[:], lhsT=z_codes[g][:, slot, :].bitcast(FP8X4), lhsT_scale=z_scales[g][:, slot, :],
+                    rhs=codes, rhs_scale=scales, start=(a == 0), stop=(a == 2),
+                )
+            av = work.tile([P, HALF], F32, name="av")
+            at = work.tile([P, HALF], F32, name="at")
+            th = work.tile([P, HALF], F32, name="th")
+            gate = work.tile([P, HALF], F32, name="gate")
+            nc.scalar.activation(out=av[:], in_=hv[:], func=ACT.Silu)
+            nc.scalar.activation(out=at[:], in_=ht[:], func=ACT.Silu)
+            nc.scalar.activation(out=th[:], in_=z[:], func=ACT.Tanh, bias=half_bias[:, nt : nt + 1], scale=0.5)
+            nc.scalar.activation(out=gate[:], in_=th[:], func=ACT.Copy, bias=0.5, scale=0.5)
+            stage[c] = {"av": av, "at": at, "gate": gate}
+
+        def step(c, s):
+            kind = STEPS[c][s]
+            eng = nc.vector if kind == "v" else nc.gpsimd
+            st = stage[c]
+            h = CHUNKS[c][1]
+            res = work.tile([P, HALF], F32, name=f"step{s}")
+            if s == 0:
+                eng.tensor_tensor(res[:], st["av"][:], st["at"][:], ALU.subtract)
+            elif s == 1:
+                eng.tensor_tensor(res[:], st["last"][:], st["gate"][:], ALU.mult)
+            elif s == 2:
+                eng.tensor_tensor(res[:], st["last"][:], st["at"][:], ALU.add)
+            else:
+                eng.tensor_tensor(
+                    res[:].rearrange("n (p c) -> n p c", c=4),
+                    st["last"][:].rearrange("n (p c) -> n p c", c=4),
+                    wgo_ps[h][:].rearrange("n (c p) -> n p c", c=4),
+                    ALU.mult,
+                )
+            st["last"] = res
+
+        def scatter(c):
+            nt, h = CHUNKS[c]
+            window = windows[nt % 2]
+            target = window[:].indirect(list_half(list1, h))
+            nc.vector.tensor_copy(target, stage[c]["last"][:])
+            if h == 1:
+                nc.sync.dma_start(out=out[P * nt : P * (nt + 1), :], in_=window[:])
+
+        nc.vector.tensor_copy(vs0[:], tabs[:].indirect(list1[:]))
+        nc.gpsimd.dma_start(out=vs1[0:112, :].bitcast(I32), in_=vs0[4:116, :].bitcast(I32))
+        for q in range(4):
+            nc.gpsimd.dma_start(out=wts[32 * q : 32 * q + 4, :].bitcast(I32), in_=wt_scales[0, 4 * q : 4 * q + 4, :].bitcast(I32))
+        make_identity(nc, ident[:])
+        for q in range(4):
+            nc.gpsimd.memset(windows[1][:, HALF * q : HALF * (q + 1)], 0.0)
+        gather_v(0)
+        gather_ts(0)
+        part_v(0)
+        quantize_z(0)
+        gather_t(0)
+        nc.scalar.activation(out=half_bias[:], in_=bias[:], func=ACT.Copy, scale=0.5)
+        gather_v(1)
+        front(0)
+        for c in range(J // P):
+            nc.tensor.transpose(wgo_ps[c // 4][:, P * (c % 4) : P * (c % 4 + 1)], wgo_col[:, c // 4, c % 4 : c % 4 + 1].to_broadcast([P, P]), ident[:])
+        step(0, 0)
+        gather_ts(1)
+        part_v(1)
+        gather_t(1)
+        front(1)
+        quantize_z(1)
+        for s in (1, 2, 3):
+            step(0, s)
+        step(1, 0)
+        front(2)
+        last = len(CHUNKS) - 1
+        for c in range(len(CHUNKS)):
+            if c < last:
+                step(c + 1, 1)
+            if c + 1 < last:
+                step(c + 2, 0)
+            if c < last:
+                step(c + 1, 2)
+                step(c + 1, 3)
+            scatter(c)
+            if c in (0, 2):
+                quantize_z(2 + c // 2)
+            if c + 2 < last:
+                front(c + 3)

@@ -1,7 +1,6 @@
 from contextlib import ExitStack
 
 import concourse.mybir as mybir
-from concourse.masks import make_identity
 
 K, L, N, T, J = 1024, 512, 512, 2048, 1024
 FLOPS = 2 * 2 * (K + L) * N * J
@@ -24,7 +23,6 @@ LIST_COLS = HALF // 16
 Z_LOADS = (((0, 0, 256), (1, 0, 128), (2, 0, 128)), ((1, 128, 256), (2, 128, 256)), ((0, 256, 512), (1, 256, 512), (2, 256, 512)))
 Z_QUANT = (((0, 0), (1, 0), (0, 1), (0, 2)), ((1, 1), (1, 2)), ((2, 0), (3, 0), (2, 1), (2, 2)), ((3, 1), (3, 2)))
 CHUNKS = [(nt, h) for nt in range(N // P) for h in range(J // HALF)]
-STEPS = ("vvvv",) + ("gggv",) * 7
 
 
 def tile_list_gmu_silu_scat_kernel(
@@ -35,11 +33,10 @@ def tile_list_gmu_silu_scat_kernel(
         keep = ctx.enter_context(tc.tile_pool(name="keep", bufs=1))
         work = ctx.enter_context(tc.tile_pool(name="work", bufs=4))
         psum = ctx.enter_context(tc.psum_pool(name="psum", bufs=2))
-        psum_keep = ctx.enter_context(tc.psum_pool(name="psum_keep", bufs=1))
 
         list1 = keep.tile([P, J // 16], U16, name="list1")
         list2 = keep.tile([P, J // 16], U16, name="list2")
-        tabw = keep.tile([P, T], U32, name="tabw")
+        tabw = keep.tile([P, T], U32, name="tabw", tag="shared")
         tab2w = keep.tile([P, T], U32, name="tab2w")
         tabs = keep.tile([P, T], U8, name="tabs")
         tab2s = keep.tile([P, T], U8, name="tab2s")
@@ -50,25 +47,23 @@ def tile_list_gmu_silu_scat_kernel(
         wts = keep.tile([P, N], U8, name="wts", align_bytes=64)
         wvw = keep.tile([P, 2, N], U32, name="wvw", align_bytes=64)
         wtw = keep.tile([P, 2 * N], U8, name="wtw", align_bytes=64)
-        wgo_col = keep.tile([P, 2, 4], F32, name="wgo_col")
-        ident = keep.tile([P, P], F32, name="ident")
-        wgo_ps = [psum_keep.tile([P, HALF], F32, name=f"wgo_ps{h}") for h in range(2)]
+        wgo_sb = keep.tile([P, J], F32, name="wgo_sb")
         bias = keep.tile([P, N // P], F32, name="bias")
         half_bias = keep.tile([P, N // P], F32, name="half_bias")
         warm_in = keep.tile([P, 1], F32, name="warm_in")
         warm_out = keep.tile([P, 1], F32, name="warm_out")
-        windows = [keep.tile([P, T], F32, name=f"window{i}") for i in range(2)]
+        windows = [keep.tile([P, T], F32, name="window0")]
 
         nc.vector.memset(tabs[:].bitcast(I32), 0)
-        nc.vector.memset(warm_in[:], 0.0)
+        nc.vector.memset(wts[:].bitcast(I32), 0)
+        nc.vector.memset(tab2s[:].bitcast(I32), 0)
+        nc.gpsimd.memset(warm_in[:], 0.0)
         nc.scalar.activation(out=warm_out[:], in_=warm_in[:], func=ACT.Silu)
-        nc.vector.memset(vs1[:].bitcast(I32), 0)
         nc.vector.memset(wvs[:].rearrange("p a n -> p (a n)").bitcast(I32), 0)
+        nc.vector.memset(vs1[:].bitcast(I32), 0)
         nc.vector.memset(windows[0][:], 0.0)
-        nc.gpsimd.memset(tab2s[:].bitcast(I32), 0)
-        nc.gpsimd.memset(wts[:].bitcast(I32), 0)
         for q in range(4):
-            nc.gpsimd.dma_start(out=tab2s[32 * q : 32 * q + 4, :].bitcast(I32), in_=tab2_scales[0, 4 * q : 4 * q + 4, :].bitcast(I32))
+            nc.gpsimd.dma_start(out=wts[32 * q : 32 * q + 4, :].bitcast(I32), in_=wt_scales[0, 4 * q : 4 * q + 4, :].bitcast(I32))
 
         z_raw = {}
 
@@ -86,18 +81,20 @@ def tile_list_gmu_silu_scat_kernel(
         nc.sync.dma_start(out=tabw[:].bitcast(I32), in_=tab_words[0].rearrange("p t i -> p (t i)").bitcast(I32))
         with nc.allow_non_contiguous_dma(reason="one value a partition"):
             nc.sync.dma_start(out=bias[:], in_=b.rearrange("(c p) -> p c", p=P))
-        nc.sync.dma_start(out=wgo_col[:], in_=wgo[0].rearrange("(h p c) -> p h c", p=P, c=4))
         nc.sync.dma_start(list2[:], offs2)
+        for q in range(4):
+            nc.scalar.dma_start(out=tab2s[32 * q : 32 * q + 4, :].bitcast(I32), in_=tab2_scales[0, 4 * q : 4 * q + 4, :].bitcast(I32))
         load_z(0)
         nc.sync.dma_start(out=tab2w[:].bitcast(I32), in_=tab2_words[0].rearrange("p t i -> p (t i)").bitcast(I32))
-        nc.sync.dma_start(out=wvw[:].bitcast(I32), in_=wv_words.rearrange("a p n i -> p a (n i)").bitcast(I32))
-        nc.sync.dma_start(out=wtw[:].bitcast(I32), in_=wt_words[0].bitcast(I32))
         for q in range(4):
-            nc.sync.dma_start(
+            nc.scalar.dma_start(
                 out=wvs[32 * q : 32 * q + 4, :, :].bitcast(I32),
                 in_=wv_scales[:, 4 * q : 4 * q + 4, :].rearrange("a r n -> r a n").bitcast(I32),
             )
+        nc.sync.dma_start(out=wvw[:].bitcast(I32), in_=wv_words.rearrange("a p n i -> p a (n i)").bitcast(I32))
+        nc.sync.dma_start(out=wtw[:].bitcast(I32), in_=wt_words[0].bitcast(I32))
         load_z(1)
+        nc.sync.dma_start(out=wgo_sb[:], in_=wgo)
         load_z(2)
 
         z_codes = [keep.tile([P, len(u), P], U32, name=f"z_codes{g}", align_bytes=64) for g, u in enumerate(Z_QUANT)]
@@ -162,68 +159,51 @@ def tile_list_gmu_silu_scat_kernel(
             av = work.tile([P, HALF], F32, name="av")
             at = work.tile([P, HALF], F32, name="at")
             th = work.tile([P, HALF], F32, name="th")
-            gate = work.tile([P, HALF], F32, name="gate")
             nc.scalar.activation(out=av[:], in_=hv[:], func=ACT.Silu)
             nc.scalar.activation(out=at[:], in_=ht[:], func=ACT.Silu)
             nc.scalar.activation(out=th[:], in_=z[:], func=ACT.Tanh, bias=half_bias[:, nt : nt + 1], scale=0.5)
-            nc.scalar.activation(out=gate[:], in_=th[:], func=ACT.Copy, bias=0.5, scale=0.5)
-            stage[c] = {"av": av, "at": at, "gate": gate}
+            stage[c] = {"av": av, "at": at, "th": th}
 
         def step(c, s):
-            kind = STEPS[c][s]
-            eng = nc.vector if kind == "v" else nc.gpsimd
             st = stage[c]
-            h = CHUNKS[c][1]
             res = work.tile([P, HALF], F32, name=f"step{s}")
             if s == 0:
-                eng.tensor_tensor(res[:], st["av"][:], st["at"][:], ALU.subtract)
+                nc.vector.tensor_tensor(res[:], st["av"][:], st["at"][:], ALU.subtract)
             elif s == 1:
-                eng.tensor_tensor(res[:], st["last"][:], st["gate"][:], ALU.mult)
-            elif s == 2:
-                eng.tensor_tensor(res[:], st["last"][:], st["at"][:], ALU.add)
+                nc.vector.scalar_tensor_tensor(res[:], st["th"][:], 1.0, st["last"][:], ALU.add, ALU.mult)
             else:
-                eng.tensor_tensor(
-                    res[:].rearrange("n (p c) -> n p c", c=4),
-                    st["last"][:].rearrange("n (p c) -> n p c", c=4),
-                    wgo_ps[h][:].rearrange("n (c p) -> n p c", c=4),
-                    ALU.mult,
-                )
+                nc.vector.scalar_tensor_tensor(res[:], st["last"][:], 0.5, st["at"][:], ALU.mult, ALU.add)
             st["last"] = res
 
         def scatter(c):
             nt, h = CHUNKS[c]
             window = windows[nt % 2]
             target = window[:].indirect(list_half(list1, h))
-            nc.vector.tensor_copy(target, stage[c]["last"][:])
+            nc.vector.tensor_tensor(target, stage[c]["last"][:], wgo_sb[:, HALF * h : HALF * (h + 1)], ALU.mult)
             if h == 1:
                 nc.sync.dma_start(out=out[P * nt : P * (nt + 1), :], in_=window[:])
 
         nc.vector.tensor_copy(vs0[:], tabs[:].indirect(list1[:]))
-        nc.gpsimd.dma_start(out=vs1[0:112, :].bitcast(I32), in_=vs0[4:116, :].bitcast(I32))
-        for q in range(4):
-            nc.gpsimd.dma_start(out=wts[32 * q : 32 * q + 4, :].bitcast(I32), in_=wt_scales[0, 4 * q : 4 * q + 4, :].bitcast(I32))
-        make_identity(nc, ident[:])
-        for q in range(4):
-            nc.gpsimd.memset(windows[1][:, HALF * q : HALF * (q + 1)], 0.0)
+        nc.scalar.dma_start(out=vs1[0:112, :].bitcast(I32), in_=vs0[4:116, :].bitcast(I32))
         gather_v(0)
         gather_ts(0)
         part_v(0)
+        nc.scalar.activation(out=half_bias[:], in_=bias[:], func=ACT.Copy, scale=0.5)
         quantize_z(0)
         gather_t(0)
-        nc.scalar.activation(out=half_bias[:], in_=bias[:], func=ACT.Copy, scale=0.5)
         gather_v(1)
         front(0)
-        for c in range(J // P):
-            nc.tensor.transpose(wgo_ps[c // 4][:, P * (c % 4) : P * (c % 4 + 1)], wgo_col[:, c // 4, c % 4 : c % 4 + 1].to_broadcast([P, P]), ident[:])
-        step(0, 0)
         gather_ts(1)
         part_v(1)
         gather_t(1)
         front(1)
+        windows.append(keep.tile([P, T], F32, name="window1", tag="shared"))
+        nc.vector.memset(windows[1][:], 0.0)
+        step(0, 0)
         quantize_z(1)
-        for s in (1, 2, 3):
-            step(0, s)
+        step(0, 1)
         step(1, 0)
+        step(0, 2)
         front(2)
         last = len(CHUNKS) - 1
         for c in range(len(CHUNKS)):
@@ -233,7 +213,6 @@ def tile_list_gmu_silu_scat_kernel(
                 step(c + 2, 0)
             if c < last:
                 step(c + 1, 2)
-                step(c + 1, 3)
             scatter(c)
             if c in (0, 2):
                 quantize_z(2 + c // 2)

@@ -1,6 +1,7 @@
 from contextlib import ExitStack
 
 import concourse.mybir as mybir
+from concourse.masks import make_identity
 
 K, L, N, T, J = 1024, 512, 512, 2048, 1024
 FLOPS = 2 * 2 * (K + L) * N * J
@@ -19,10 +20,12 @@ ALU = mybir.AluOpType
 P = 128
 PACK = 4
 HALF = 512
+BLOCKS = HALF // P
 LIST_COLS = HALF // 16
-Z_LOADS = (((0, 0, 256), (1, 0, 128), (2, 0, 128)), ((1, 128, 256), (2, 128, 256)), ((0, 256, 512), (1, 256, 512), (2, 256, 512)))
-Z_QUANT = (((0, 0), (1, 0), (0, 1), (0, 2)), ((1, 1), (1, 2)), ((2, 0), (3, 0), (2, 1), (2, 2)), ((3, 1), (3, 2)))
-CHUNKS = [(nt, h) for nt in range(N // P) for h in range(J // HALF)]
+TILES = N // P
+AV_SLOTS = (8192, 11264, 14336)
+BANK = 2048
+CHUNKS = [(nt, h) for nt in range(TILES) for h in range(J // HALF)]
 
 
 def tile_list_gmu_silu_scat_kernel(
@@ -31,89 +34,102 @@ def tile_list_gmu_silu_scat_kernel(
     nc = tc.nc
     with ExitStack() as ctx:
         keep = ctx.enter_context(tc.tile_pool(name="keep", bufs=1))
-        work = ctx.enter_context(tc.tile_pool(name="work", bufs=4))
-        psum = ctx.enter_context(tc.psum_pool(name="psum", bufs=2))
+        reuse = ctx.enter_context(tc.tile_pool(name="reuse", bufs=1))
+        work = ctx.enter_context(tc.tile_pool(name="work", bufs=3))
+        psum = ctx.enter_context(tc.psum_pool(name="psum", bufs=1))
 
         list1 = keep.tile([P, J // 16], U16, name="list1")
         list2 = keep.tile([P, J // 16], U16, name="list2")
         tabw = keep.tile([P, T], U32, name="tabw", tag="shared")
         tab2w = keep.tile([P, T], U32, name="tab2w")
-        tabs = keep.tile([P, T], U8, name="tabs")
+        tabs = reuse.tile([P, T], U8, name="tabs", align_bytes=64, offset=22528)
         tab2s = keep.tile([P, T], U8, name="tab2s")
         vs0 = keep.tile([P, J], U8, name="vs0", align_bytes=64)
         vs1 = keep.tile([P, J], U8, name="vs1", align_bytes=64)
-        ts = [keep.tile([P, HALF], U8, name=f"ts{h}", align_bytes=64) for h in range(2)]
         wvs = keep.tile([P, 2, N], U8, name="wvs", align_bytes=64)
         wts = keep.tile([P, N], U8, name="wts", align_bytes=64)
-        wvw = keep.tile([P, 2, N], U32, name="wvw", align_bytes=64)
         wtw = keep.tile([P, 2 * N], U8, name="wtw", align_bytes=64)
-        wgo_sb = keep.tile([P, J], F32, name="wgo_sb")
-        bias = keep.tile([P, N // P], F32, name="bias")
-        half_bias = keep.tile([P, N // P], F32, name="half_bias")
-        warm_in = keep.tile([P, 1], F32, name="warm_in")
-        warm_out = keep.tile([P, 1], F32, name="warm_out")
-        windows = [keep.tile([P, T], F32, name="window0")]
+        rows = keep.tile([P, P], F32, name="rows")
+        ident = keep.tile([P, P], F32, name="ident")
+        halves = keep.tile([P, J // P + TILES], F32, name="halves")
+        neg_half_w = keep.tile([P, J // P], F32, name="neg_half_w")
+        windows = []
 
         nc.vector.memset(tabs[:].bitcast(I32), 0)
-        nc.vector.memset(wts[:].bitcast(I32), 0)
         nc.vector.memset(tab2s[:].bitcast(I32), 0)
-        nc.gpsimd.memset(warm_in[:], 0.0)
-        nc.scalar.activation(out=warm_out[:], in_=warm_in[:], func=ACT.Silu)
+        nc.vector.memset(rows[:], 0.0)
+        nc.vector.memset(wts[:].bitcast(I32), 0)
         nc.vector.memset(wvs[:].rearrange("p a n -> p (a n)").bitcast(I32), 0)
         nc.vector.memset(vs1[:].bitcast(I32), 0)
-        nc.vector.memset(windows[0][:], 0.0)
-        for q in range(4):
-            nc.gpsimd.dma_start(out=wts[32 * q : 32 * q + 4, :].bitcast(I32), in_=wt_scales[0, 4 * q : 4 * q + 4, :].bitcast(I32))
+        make_identity(nc, ident[:])
 
         z_raw = {}
 
-        def load_z(stage_no):
-            for a, n0, n1 in Z_LOADS[stage_no]:
+        wv_cols = {}
+
+        def load_wv(n0, n1):
+            tile = keep.tile([P, 2, n1 - n0], U32, name=f"wvw{n0}", align_bytes=64)
+            nc.sync.dma_start(out=tile[:].bitcast(I32), in_=wv_words[:, :, n0:n1, :].rearrange("a p n i -> p a (n i)").bitcast(I32))
+            for nt in range(n0 // P, n1 // P):
+                wv_cols[nt] = tile[:, :, P * nt - n0 : P * (nt + 1) - n0]
+
+        def load_z(n0, n1, passes):
+            for a in passes:
                 tile = keep.tile([P, PACK, n1 - n0], F32, name=f"z_raw{a}_{n0}")
-                rows = zv[512 * a : 512 * (a + 1), n0:n1] if a < 2 else zt[:, n0:n1]
-                nc.sync.dma_start(out=tile[:], in_=rows.rearrange("(p i) n -> p i n", i=PACK))
+                src = zv[512 * a : 512 * (a + 1), n0:n1] if a < 2 else zt[:, n0:n1]
+                nc.sync.dma_start(out=tile[:], in_=src.rearrange("(p i) n -> p i n", i=PACK))
                 for nt in range(n0 // P, n1 // P):
                     z_raw[(nt, a)] = tile[:, :, P * nt - n0 : P * (nt + 1) - n0]
 
         nc.sync.dma_start(list1[:], offs)
+        nc.sync.dma_start(list2[:], offs2)
+        nc.sync.dma_start(out=wtw[:].bitcast(I32), in_=wt_words[0].bitcast(I32))
         for q in range(4):
             nc.sync.dma_start(out=tabs[32 * q : 32 * q + 8, :].bitcast(I32), in_=tab_scales[:, 4 * q : 4 * q + 4, :].bitcast(I32))
         nc.sync.dma_start(out=tabw[:].bitcast(I32), in_=tab_words[0].rearrange("p t i -> p (t i)").bitcast(I32))
-        with nc.allow_non_contiguous_dma(reason="one value a partition"):
-            nc.sync.dma_start(out=bias[:], in_=b.rearrange("(c p) -> p c", p=P))
-        nc.sync.dma_start(list2[:], offs2)
         for q in range(4):
-            nc.scalar.dma_start(out=tab2s[32 * q : 32 * q + 4, :].bitcast(I32), in_=tab2_scales[0, 4 * q : 4 * q + 4, :].bitcast(I32))
-        load_z(0)
+            nc.gpsimd.dma_start(out=wts[32 * q : 32 * q + 4, :].bitcast(I32), in_=wt_scales[0, 4 * q : 4 * q + 4, :].bitcast(I32))
+        for q in range(4):
+            nc.sync.dma_start(out=tab2s[32 * q : 32 * q + 4, :].bitcast(I32), in_=tab2_scales[0, 4 * q : 4 * q + 4, :].bitcast(I32))
         nc.sync.dma_start(out=tab2w[:].bitcast(I32), in_=tab2_words[0].rearrange("p t i -> p (t i)").bitcast(I32))
+        load_z(0, P, (0, 1, 2))
+        load_wv(0, P)
+        nc.sync.dma_start(out=rows[0 : J // P, :], in_=wgo[0].rearrange("(r c) -> r c", c=P))
+        nc.sync.dma_start(out=rows[J // P : J // P + TILES, :], in_=b.rearrange("(r c) -> r c", c=P))
         for q in range(4):
-            nc.scalar.dma_start(
+            nc.sync.dma_start(
                 out=wvs[32 * q : 32 * q + 4, :, :].bitcast(I32),
                 in_=wv_scales[:, 4 * q : 4 * q + 4, :].rearrange("a r n -> r a n").bitcast(I32),
             )
-        nc.sync.dma_start(out=wvw[:].bitcast(I32), in_=wv_words.rearrange("a p n i -> p a (n i)").bitcast(I32))
-        nc.sync.dma_start(out=wtw[:].bitcast(I32), in_=wt_words[0].bitcast(I32))
-        load_z(1)
-        nc.sync.dma_start(out=wgo_sb[:], in_=wgo)
-        load_z(2)
+        load_z(P, 2 * P, (0, 1, 2))
+        load_wv(P, N)
+        load_z(2 * P, N, (0, 1, 2))
 
-        z_codes = [keep.tile([P, len(u), P], U32, name=f"z_codes{g}", align_bytes=64) for g, u in enumerate(Z_QUANT)]
-        z_scales = [keep.tile([P, len(u), P], U8, name=f"z_scales{g}", align_bytes=64) for g, u in enumerate(Z_QUANT)]
-        z_bf = [keep.tile([P, len(u), P, PACK], BF16, name=f"z_bf{g}", align_bytes=64) for g, u in enumerate(Z_QUANT)]
-        z_place = {unit: (g, slot) for g, units in enumerate(Z_QUANT) for slot, unit in enumerate(units)}
+        z_codes = {}
+        z_scales = [keep.tile([P, 3, P], U8, name=f"z_scales{nt}", align_bytes=64) for nt in range(TILES)]
+        z_bf = {}
 
-        def quantize_z(g):
-            for slot, unit in enumerate(Z_QUANT[g]):
-                nc.scalar.activation(out=z_bf[g][:, slot, :, :], in_=z_raw[unit].rearrange("p i n -> p n i"), func=ACT.Copy)
-            nc.vector.quantize_mx(
-                out=z_codes[g][:].rearrange("p s n -> p (s n)").bitcast(FP8X4),
-                scales=z_scales[g][:].rearrange("p s n -> p (s n)"),
-                in_=z_bf[g][:].rearrange("p s n i -> p (s n i)"),
-            )
+        def cast_z(nt):
+            z_bf[nt] = reuse.tile([P, 3, P, PACK], BF16, name=f"z_bf{nt}", align_bytes=64, offset=(0, 5 * HALF, AV_SLOTS[0], AV_SLOTS[2])[nt])
+            for a in range(3):
+                if nt != 1:
+                    nc.scalar.activation(out=z_bf[nt][:, a, :, :], in_=z_raw[(nt, a)].rearrange("p i n -> p n i"), func=ACT.Copy)
+                else:
+                    nc.vector.tensor_copy(z_bf[nt][:, a, :, :], z_raw[(nt, a)].rearrange("p i n -> p n i"))
+
+        def quantize_z(nt):
+            z_codes[nt] = keep.tile([P, 3, P], U32, name=f"z_codes{nt}", align_bytes=64)
+            for a0, a1 in ((0, 2), (2, 3)):
+                nc.vector.quantize_mx(
+                    out=z_codes[nt][:, a0:a1, :].rearrange("p s n -> p (s n)").bitcast(FP8X4),
+                    scales=z_scales[nt][:, a0:a1, :].rearrange("p s n -> p (s n)"),
+                    in_=z_bf[nt][:, a0:a1, :, :].rearrange("p s n i -> p (s n i)"),
+                )
 
         vw = [keep.tile([P, 2, 2 * HALF], U8, name=f"vw{h}", align_bytes=64) for h in range(2)]
-        tw = [keep.tile([P, HALF], U32, name=f"tw{h}", align_bytes=64) for h in range(2)]
-        pairs = [keep.tile([P, HALF], U32, name=f"pairs{h}") for h in range(2)]
+        tw = [keep.tile([P, HALF], U32, name="tw0", align_bytes=64)]
+        ts = [keep.tile([P, HALF], U8, name="ts0", align_bytes=64)]
+        pairs = []
 
         def list_half(tile, h):
             return tile[:, LIST_COLS * h : LIST_COLS * (h + 1)]
@@ -132,89 +148,135 @@ def tile_list_gmu_silu_scat_kernel(
 
         stage = {}
 
-        def front(c):
+        def products(c):
             nt, h = CHUNKS[c]
             jc = slice(HALF * h, HALF * (h + 1))
             ncols = slice(P * nt, P * (nt + 1))
-            v_ops = [(vw[h][:, 0, :].bitcast(FP4X4), vs0[:, jc]), (vw[h][:, 1, :].bitcast(FP4X4), vs1[:, jc])]
-            t_op = (tw[h][:].bitcast(FP8X4), ts[h][:])
-            hv = psum.tile([P, HALF], F32, name="hv")
-            ht = psum.tile([P, HALF], F32, name="ht")
-            z = psum.tile([P, HALF], F32, name="z")
-            for a in range(2):
+            hv = psum.tile([P, BLOCKS, P], F32, name=f"hv{c}", offset=BANK * 0)
+            ht = psum.tile([P, BLOCKS, P], F32, name=f"ht{c}", offset=BANK * 1)
+            z = psum.tile([P, HALF], F32, name=f"z{c}", offset=BANK * (4 if c == 1 else 2 + c % 2))
+            for blk in range(BLOCKS):
                 nc.tensor.matmul_mx(
-                    out=hv[:], lhsT=wvw[:, a, ncols].bitcast(FP8X4), lhsT_scale=wvs[:, a, ncols],
-                    rhs=v_ops[a][0], rhs_scale=v_ops[a][1], start=(a == 0), stop=(a == 1),
+                    out=ht[:, blk, :], lhsT=tw[h][:, P * blk : P * (blk + 1)].bitcast(FP8X4), lhsT_scale=ts[h][:, P * blk : P * (blk + 1)],
+                    rhs=wtw[:, 2 * P * nt : 2 * P * (nt + 1)].bitcast(FP4X4), rhs_scale=wts[:, ncols], start=True, stop=True,
                 )
-            nc.tensor.matmul_mx(
-                out=ht[:], lhsT=wtw[:, 2 * P * nt : 2 * P * (nt + 1)].bitcast(FP4X4), lhsT_scale=wts[:, ncols],
-                rhs=t_op[0], rhs_scale=t_op[1], start=True, stop=True,
-            )
-            for a, (codes, scales) in enumerate(v_ops + [t_op]):
-                g, slot = z_place[(nt, a)]
+            for blk in range(BLOCKS):
+                j0 = HALF * h + P * blk
+                for a, plane in enumerate((vs0, vs1)):
+                    nc.tensor.matmul_mx(
+                        out=hv[:, blk, :], lhsT=vw[h][:, a, 2 * P * blk : 2 * P * (blk + 1)].bitcast(FP4X4), lhsT_scale=plane[:, j0 : j0 + P],
+                        rhs=wv_cols[nt][:, a, :].bitcast(FP8X4), rhs_scale=wvs[:, a, ncols], start=(a == 0), stop=(a == 1),
+                    )
+            moving = [
+                (vw[h][:, 0, :].bitcast(FP4X4), vs0[:, jc]),
+                (vw[h][:, 1, :].bitcast(FP4X4), vs1[:, jc]),
+                (tw[h][:].bitcast(FP8X4), ts[h][:]),
+            ]
+            for a, (codes, scales) in enumerate(moving):
                 nc.tensor.matmul_mx(
-                    out=z[:], lhsT=z_codes[g][:, slot, :].bitcast(FP8X4), lhsT_scale=z_scales[g][:, slot, :],
+                    out=z[:], lhsT=z_codes[nt][:, a, :].bitcast(FP8X4), lhsT_scale=z_scales[nt][:, a, :],
                     rhs=codes, rhs_scale=scales, start=(a == 0), stop=(a == 2),
                 )
-            av = work.tile([P, HALF], F32, name="av")
-            at = work.tile([P, HALF], F32, name="at")
-            th = work.tile([P, HALF], F32, name="th")
-            nc.scalar.activation(out=av[:], in_=hv[:], func=ACT.Silu)
-            nc.scalar.activation(out=at[:], in_=ht[:], func=ACT.Silu)
-            nc.scalar.activation(out=th[:], in_=z[:], func=ACT.Tanh, bias=half_bias[:, nt : nt + 1], scale=0.5)
-            stage[c] = {"av": av, "at": at, "th": th}
+            stage[c] = {"hv": hv, "ht": ht, "z": z}
 
-        def step(c, s):
+        def activations(c):
+            nt, h = CHUNKS[c]
             st = stage[c]
-            res = work.tile([P, HALF], F32, name=f"step{s}")
-            if s == 0:
-                nc.vector.tensor_tensor(res[:], st["av"][:], st["at"][:], ALU.subtract)
-            elif s == 1:
-                nc.vector.scalar_tensor_tensor(res[:], st["th"][:], 1.0, st["last"][:], ALU.add, ALU.mult)
-            else:
-                nc.vector.scalar_tensor_tensor(res[:], st["last"][:], 0.5, st["at"][:], ALU.mult, ALU.add)
-            st["last"] = res
+            av = work.tile([P, BLOCKS, P], F32, name="av", bufs=1)
+            at = work.tile([P, BLOCKS, P], F32, name="at", bufs=1)
+            wav = work.tile([P, BLOCKS, P], F32, name="wav")
+            wat = work.tile([P, BLOCKS, P], F32, name="wat")
+            th = work.tile([P, HALF], F32, name="th")
+            sides = [(st["ht"], at, wat, neg_half_w), (st["hv"], av, wav, halves)]
+            if c > 0:
+                sides = sides[::-1]
+            for bank, act, weighted, factor in sides:
+                nc.scalar.activation(out=act[:], in_=bank[:], func=ACT.Silu)
+            for bank, act, weighted, factor in sides:
+                for blk in range(BLOCKS):
+                    col = BLOCKS * h + blk
+                    nc.scalar.activation(out=weighted[:, blk, :], in_=act[:, blk, :], func=ACT.Copy, scale=factor[:, col : col + 1])
+            col = J // P + nt
+            nc.scalar.activation(out=th[:], in_=st["z"][:], func=ACT.Tanh, bias=halves[:, col : col + 1], scale=0.5)
+            st.update({"wav": wav, "wat": wat, "th": th})
+
+        def turn(c):
+            st = stage[c]
+            base = psum.tile([P, BLOCKS, P], F32, name=f"base{c}", offset=BANK * (4 + c % 2))
+            diff = psum.tile([P, BLOCKS, P], F32, name=f"diff{c}", offset=BANK * (6 + c % 2))
+            first, second = ("wav", "wat") if c == 0 else ("wat", "wav")
+            for blk in reversed(range(BLOCKS)):
+                nc.tensor.matmul(diff[:, blk, :], st[first][:, blk, :], ident[:], start=True, stop=False, is_transpose=True)
+                nc.tensor.matmul(diff[:, blk, :], st[second][:, blk, :], ident[:], start=False, stop=True, is_transpose=True)
+            for blk in reversed(range(BLOCKS)):
+                nc.tensor.transpose(base[:, blk, :], st["wat"][:, blk, :], ident[:])
+            st.update({"base": base, "diff": diff})
+
+        def unload(c):
+            st = stage[c]
+            base_sb = work.tile([P, HALF], F32, name="base_sb")
+            nc.scalar.activation(out=base_sb[:], in_=st["base"][:].rearrange("p b j -> p (b j)"), func=ACT.Copy, scale=-2.0)
+            st["base_sb"] = base_sb
+
+        def gate(c):
+            st = stage[c]
+            gated = reuse.tile([P, HALF], F32, name=f"gated{c}", align_bytes=64, offset=AV_SLOTS[c % 3])
+            nc.vector.scalar_tensor_tensor(gated[:], st["th"][:], 1.0, st["diff"][:].rearrange("p b j -> p (b j)"), ALU.add, ALU.mult)
+            st["gated"] = gated
 
         def scatter(c):
             nt, h = CHUNKS[c]
             window = windows[nt % 2]
-            target = window[:].indirect(list_half(list1, h))
-            nc.vector.tensor_tensor(target, stage[c]["last"][:], wgo_sb[:, HALF * h : HALF * (h + 1)], ALU.mult)
+            nc.vector.tensor_tensor(window[:].indirect(list_half(list1, h)), stage[c]["gated"][:], stage[c]["base_sb"][:], ALU.add)
             if h == 1:
                 nc.sync.dma_start(out=out[P * nt : P * (nt + 1), :], in_=window[:])
 
         nc.vector.tensor_copy(vs0[:], tabs[:].indirect(list1[:]))
         nc.scalar.dma_start(out=vs1[0:112, :].bitcast(I32), in_=vs0[4:116, :].bitcast(I32))
+        pairs.append(reuse.tile([P, HALF], U32, name="pairs0", align_bytes=64, offset=22528))
         gather_v(0)
-        gather_ts(0)
         part_v(0)
-        nc.scalar.activation(out=half_bias[:], in_=bias[:], func=ACT.Copy, scale=0.5)
-        quantize_z(0)
+        windows.append(reuse.tile([P, T], F32, name="window0", align_bytes=64, offset=22528))
+        for part in range(4):
+            nc.gpsimd.memset(windows[0][:, HALF * part : HALF * (part + 1)], 0.0)
+        gather_ts(0)
         gather_t(0)
+        cast_z(0)
+        turned = psum.tile([P, BLOCKS, P], F32, name="turned", offset=BANK * 5)
+        nc.tensor.transpose(turned[:, 0, :], rows[:], ident[:])
+        nc.scalar.activation(out=halves[:], in_=turned[:, 0, 0 : J // P + TILES], func=ACT.Copy, scale=0.5)
+        nc.scalar.activation(out=neg_half_w[:], in_=turned[:, 0, 0 : J // P], func=ACT.Copy, scale=-0.5)
+        quantize_z(0)
+        products(0)
+        ts.append(reuse.tile([P, HALF], U8, name="ts1", align_bytes=64, offset=0))
+        tw.append(reuse.tile([P, HALF], U32, name="tw1", align_bytes=64, offset=HALF))
+        pairs.append(reuse.tile([P, HALF], U32, name="pairs1", align_bytes=64, offset=5 * HALF))
         gather_v(1)
-        front(0)
-        gather_ts(1)
+        activations(0)
         part_v(1)
+        gather_ts(1)
         gather_t(1)
-        front(1)
-        windows.append(keep.tile([P, T], F32, name="window1", tag="shared"))
-        nc.vector.memset(windows[1][:], 0.0)
-        step(0, 0)
+        cast_z(1)
         quantize_z(1)
-        step(0, 1)
-        step(1, 0)
-        step(0, 2)
-        front(2)
+        windows.append(keep.tile([P, T], F32, name="window1", tag="shared"))
+        for part in range(4):
+            nc.gpsimd.memset(windows[1][:, HALF * part : HALF * (part + 1)], 0.0)
+        turn(0)
         last = len(CHUNKS) - 1
         for c in range(len(CHUNKS)):
+            nt, h = CHUNKS[c]
+            if 0 < c < last:
+                products(c + 1)
+            unload(c)
+            gate(c)
+            if c == 0:
+                products(1)
             if c < last:
-                step(c + 1, 1)
-            if c + 1 < last:
-                step(c + 2, 0)
-            if c < last:
-                step(c + 1, 2)
+                activations(c + 1)
+            if h == 1 and nt + 2 < TILES:
+                cast_z(nt + 2)
             scatter(c)
-            if c in (0, 2):
-                quantize_z(2 + c // 2)
-            if c + 2 < last:
-                front(c + 3)
+            if h == 1 and nt + 2 < TILES:
+                quantize_z(nt + 2)
+            if c < last:
+                turn(c + 1)

@@ -40,7 +40,7 @@ def tile_list_gmu_silu_scat_kernel(
 
         list1 = keep.tile([P, J // 16], U16, name="list1")
         list2 = keep.tile([P, J // 16], U16, name="list2")
-        tabw = keep.tile([P, T], U32, name="tabw", tag="shared")
+        tabw = keep.tile([P, T], U32, name="tabw")
         tab2w = keep.tile([P, T], U32, name="tab2w")
         tabs = reuse.tile([P, T], U8, name="tabs", align_bytes=64, offset=22528)
         tab2s = keep.tile([P, T], U8, name="tab2s")
@@ -53,7 +53,7 @@ def tile_list_gmu_silu_scat_kernel(
         ident = keep.tile([P, P], F32, name="ident")
         halves = keep.tile([P, J // P + TILES], F32, name="halves")
         neg_half_w = keep.tile([P, J // P], F32, name="neg_half_w")
-        windows = []
+        windows = [keep.tile([P, T], F32, name="window0")]
 
         nc.vector.memset(tabs[:].bitcast(I32), 0)
         nc.vector.memset(tab2s[:].bitcast(I32), 0)
@@ -61,6 +61,7 @@ def tile_list_gmu_silu_scat_kernel(
         nc.vector.memset(wts[:].bitcast(I32), 0)
         nc.vector.memset(wvs[:].rearrange("p a n -> p (a n)").bitcast(I32), 0)
         nc.vector.memset(vs1[:].bitcast(I32), 0)
+        nc.vector.memset(windows[0][:], 0.0)
         make_identity(nc, ident[:])
 
         z_raw = {}
@@ -93,14 +94,14 @@ def tile_list_gmu_silu_scat_kernel(
             nc.sync.dma_start(out=tab2s[32 * q : 32 * q + 4, :].bitcast(I32), in_=tab2_scales[0, 4 * q : 4 * q + 4, :].bitcast(I32))
         nc.sync.dma_start(out=tab2w[:].bitcast(I32), in_=tab2_words[0].rearrange("p t i -> p (t i)").bitcast(I32))
         load_z(0, P, (0, 1, 2))
-        load_wv(0, P)
-        nc.sync.dma_start(out=rows[0 : J // P, :], in_=wgo[0].rearrange("(r c) -> r c", c=P))
-        nc.sync.dma_start(out=rows[J // P : J // P + TILES, :], in_=b.rearrange("(r c) -> r c", c=P))
         for q in range(4):
             nc.sync.dma_start(
                 out=wvs[32 * q : 32 * q + 4, :, :].bitcast(I32),
                 in_=wv_scales[:, 4 * q : 4 * q + 4, :].rearrange("a r n -> r a n").bitcast(I32),
             )
+        load_wv(0, P)
+        nc.sync.dma_start(out=rows[0 : J // P, :], in_=wgo[0].rearrange("(r c) -> r c", c=P))
+        nc.sync.dma_start(out=rows[J // P : J // P + TILES, :], in_=b.rearrange("(r c) -> r c", c=P))
         load_z(P, 2 * P, (0, 1, 2))
         load_wv(P, N)
         load_z(2 * P, N, (0, 1, 2))
@@ -154,7 +155,7 @@ def tile_list_gmu_silu_scat_kernel(
             ncols = slice(P * nt, P * (nt + 1))
             hv = psum.tile([P, BLOCKS, P], F32, name=f"hv{c}", offset=BANK * 0)
             ht = psum.tile([P, BLOCKS, P], F32, name=f"ht{c}", offset=BANK * 1)
-            z = psum.tile([P, HALF], F32, name=f"z{c}", offset=BANK * (4 if c == 1 else 2 + c % 2))
+            z = psum.tile([P, HALF], F32, name=f"z{c}", offset=BANK * (4 if c == 1 else 2))
             for blk in range(BLOCKS):
                 nc.tensor.matmul_mx(
                     out=ht[:, blk, :], lhsT=tw[h][:, P * blk : P * (blk + 1)].bitcast(FP8X4), lhsT_scale=ts[h][:, P * blk : P * (blk + 1)],
@@ -186,18 +187,28 @@ def tile_list_gmu_silu_scat_kernel(
             at = work.tile([P, BLOCKS, P], F32, name="at", bufs=1)
             wav = work.tile([P, BLOCKS, P], F32, name="wav")
             wat = work.tile([P, BLOCKS, P], F32, name="wat")
-            th = work.tile([P, HALF], F32, name="th")
+            if c == 0:
+                th = reuse.tile([P, HALF], F32, name="th0", align_bytes=64, offset=24576)
+            else:
+                th = work.tile([P, HALF], F32, name="th")
+
+            def tanh():
+                col = J // P + nt
+                nc.scalar.activation(out=th[:], in_=st["z"][:], func=ACT.Tanh, bias=halves[:, col : col + 1], scale=0.5)
+
             sides = [(st["ht"], at, wat, neg_half_w), (st["hv"], av, wav, halves)]
             if c > 0:
                 sides = sides[::-1]
             for bank, act, weighted, factor in sides:
                 nc.scalar.activation(out=act[:], in_=bank[:], func=ACT.Silu)
-            for bank, act, weighted, factor in sides:
+            for side, (bank, act, weighted, factor) in enumerate(sides):
+                if side == (1 if c > 1 else 2):
+                    tanh()
                 for blk in range(BLOCKS):
                     col = BLOCKS * h + blk
                     nc.scalar.activation(out=weighted[:, blk, :], in_=act[:, blk, :], func=ACT.Copy, scale=factor[:, col : col + 1])
-            col = J // P + nt
-            nc.scalar.activation(out=th[:], in_=st["z"][:], func=ACT.Tanh, bias=halves[:, col : col + 1], scale=0.5)
+            if c <= 1:
+                tanh()
             st.update({"wav": wav, "wat": wat, "th": th})
 
         def turn(c):
@@ -236,9 +247,6 @@ def tile_list_gmu_silu_scat_kernel(
         pairs.append(reuse.tile([P, HALF], U32, name="pairs0", align_bytes=64, offset=22528))
         gather_v(0)
         part_v(0)
-        windows.append(reuse.tile([P, T], F32, name="window0", align_bytes=64, offset=22528))
-        for part in range(4):
-            nc.gpsimd.memset(windows[0][:, HALF * part : HALF * (part + 1)], 0.0)
         gather_ts(0)
         gather_t(0)
         cast_z(0)
@@ -258,9 +266,6 @@ def tile_list_gmu_silu_scat_kernel(
         gather_t(1)
         cast_z(1)
         quantize_z(1)
-        windows.append(keep.tile([P, T], F32, name="window1", tag="shared"))
-        for part in range(4):
-            nc.gpsimd.memset(windows[1][:, HALF * part : HALF * (part + 1)], 0.0)
         turn(0)
         last = len(CHUNKS) - 1
         for c in range(len(CHUNKS)):
@@ -271,6 +276,8 @@ def tile_list_gmu_silu_scat_kernel(
             gate(c)
             if c == 0:
                 products(1)
+                windows.append(reuse.tile([P, T], F32, name="window1", align_bytes=64, offset=24576))
+                nc.gpsimd.memset(windows[1][:], 0.0)
             if c < last:
                 activations(c + 1)
             if h == 1 and nt + 2 < TILES:

@@ -23,8 +23,10 @@ HALF = 512
 BLOCKS = HALF // P
 LIST_COLS = HALF // 16
 TILES = N // P
-AV_SLOTS = (8192, 11264, 14336)
+TH_AT = 8192
+WINDOW_AT = 45056
 BANK = 2048
+LATE_CASTS = {1: ((2, 0), (2, 1), (2, 2)), 3: ((3, 0), (3, 1), (3, 2))}
 CHUNKS = [(nt, h) for nt in range(TILES) for h in range(J // HALF)]
 
 
@@ -42,7 +44,7 @@ def tile_list_gmu_silu_scat_kernel(
         list2 = keep.tile([P, J // 16], U16, name="list2")
         tabw = keep.tile([P, T], U32, name="tabw")
         tab2w = keep.tile([P, T], U32, name="tab2w")
-        tabs = reuse.tile([P, T], U8, name="tabs", align_bytes=64, offset=22528)
+        tabs = reuse.tile([P, T], U8, name="tabs", align_bytes=64, offset=43008)
         tab2s = keep.tile([P, T], U8, name="tab2s")
         vs0 = keep.tile([P, J], U8, name="vs0", align_bytes=64)
         vs1 = keep.tile([P, J], U8, name="vs1", align_bytes=64)
@@ -111,7 +113,7 @@ def tile_list_gmu_silu_scat_kernel(
         z_bf = {}
 
         def cast_z(nt):
-            z_bf[nt] = reuse.tile([P, 3, P, PACK], BF16, name=f"z_bf{nt}", align_bytes=64, offset=(0, 5 * HALF, AV_SLOTS[0], AV_SLOTS[2])[nt])
+            z_bf[nt] = reuse.tile([P, 3, P, PACK], BF16, name=f"z_bf{nt}", align_bytes=64, offset=(0, 5 * HALF)[nt])
             for a in range(3):
                 if nt != 1:
                     nc.scalar.activation(out=z_bf[nt][:, a, :, :], in_=z_raw[(nt, a)].rearrange("p i n -> p n i"), func=ACT.Copy)
@@ -119,12 +121,28 @@ def tile_list_gmu_silu_scat_kernel(
                     nc.vector.tensor_copy(z_bf[nt][:, a, :, :], z_raw[(nt, a)].rearrange("p i n -> p n i"))
 
         def quantize_z(nt):
-            z_codes[nt] = keep.tile([P, 3, P], U32, name=f"z_codes{nt}", align_bytes=64)
+            z_codes[nt] = reuse.tile([P, 3, P], U32, name=f"z_codes{nt}", align_bytes=64, offset=(40960, TH_AT + 1024)[nt])
             for a0, a1 in ((0, 2), (2, 3)):
                 nc.vector.quantize_mx(
                     out=z_codes[nt][:, a0:a1, :].rearrange("p s n -> p (s n)").bitcast(FP8X4),
                     scales=z_scales[nt][:, a0:a1, :].rearrange("p s n -> p (s n)"),
                     in_=z_bf[nt][:, a0:a1, :, :].rearrange("p s n i -> p (s n i)"),
+                )
+
+        late_bf = {}
+
+        def cast_late(nt, a, offset):
+            late_bf[(nt, a)] = reuse.tile([P, P, PACK], BF16, name=f"z_bf{nt}_{a}", align_bytes=64, offset=offset)
+            if a < 2:
+                nc.vector.tensor_copy(late_bf[(nt, a)][:], z_raw[(nt, a)].rearrange("p i n -> p n i"))
+            else:
+                nc.scalar.activation(out=late_bf[(nt, a)][:], in_=z_raw[(nt, a)].rearrange("p i n -> p n i"), func=ACT.Copy)
+
+        def quantize_late(nt, offset):
+            z_codes[nt] = reuse.tile([P, 3, P], U32, name=f"z_codes{nt}", align_bytes=64, offset=offset)
+            for a in range(3):
+                nc.vector.quantize_mx(
+                    out=z_codes[nt][:, a, :].bitcast(FP8X4), scales=z_scales[nt][:, a, :], in_=late_bf[(nt, a)][:].rearrange("p n i -> p (n i)")
                 )
 
         vw = [keep.tile([P, 2, 2 * HALF], U8, name=f"vw{h}", align_bytes=64) for h in range(2)]
@@ -154,8 +172,8 @@ def tile_list_gmu_silu_scat_kernel(
             jc = slice(HALF * h, HALF * (h + 1))
             ncols = slice(P * nt, P * (nt + 1))
             hv = psum.tile([P, BLOCKS, P], F32, name=f"hv{c}", offset=BANK * 0)
-            ht = psum.tile([P, BLOCKS, P], F32, name=f"ht{c}", offset=BANK * 1)
-            z = psum.tile([P, HALF], F32, name=f"z{c}", offset=BANK * (4 if c == 1 else 2))
+            ht = psum.tile([P, BLOCKS, P], F32, name=f"ht{c}", offset=BANK * (4 if c == 1 else 1))
+            z = psum.tile([P, HALF], F32, name=f"z{c}", offset=BANK * (6 if c == 1 else 2))
             for blk in range(BLOCKS):
                 nc.tensor.matmul_mx(
                     out=ht[:, blk, :], lhsT=tw[h][:, P * blk : P * (blk + 1)].bitcast(FP8X4), lhsT_scale=ts[h][:, P * blk : P * (blk + 1)],
@@ -187,10 +205,7 @@ def tile_list_gmu_silu_scat_kernel(
             at = work.tile([P, BLOCKS, P], F32, name="at", bufs=1)
             wav = work.tile([P, BLOCKS, P], F32, name="wav")
             wat = work.tile([P, BLOCKS, P], F32, name="wat")
-            if c == 0:
-                th = reuse.tile([P, HALF], F32, name="th0", align_bytes=64, offset=24576)
-            else:
-                th = work.tile([P, HALF], F32, name="th")
+            th = reuse.tile([P, HALF], F32, name=f"th{c}", align_bytes=64, offset=TH_AT + 4096 * c + 512)
 
             def tanh():
                 col = J // P + nt
@@ -231,7 +246,10 @@ def tile_list_gmu_silu_scat_kernel(
 
         def gate(c):
             st = stage[c]
-            gated = reuse.tile([P, HALF], F32, name=f"gated{c}", align_bytes=64, offset=AV_SLOTS[c % 3])
+            if c == 0:
+                gated = reuse.tile([P, HALF], F32, name="gated0", align_bytes=64, offset=WINDOW_AT)
+            else:
+                gated = work.tile([P, HALF], F32, name="gated")
             nc.vector.scalar_tensor_tensor(gated[:], st["th"][:], 1.0, st["diff"][:].rearrange("p b j -> p (b j)"), ALU.add, ALU.mult)
             st["gated"] = gated
 
@@ -244,7 +262,7 @@ def tile_list_gmu_silu_scat_kernel(
 
         nc.vector.tensor_copy(vs0[:], tabs[:].indirect(list1[:]))
         nc.scalar.dma_start(out=vs1[0:112, :].bitcast(I32), in_=vs0[4:116, :].bitcast(I32))
-        pairs.append(reuse.tile([P, HALF], U32, name="pairs0", align_bytes=64, offset=22528))
+        pairs.append(reuse.tile([P, HALF], U32, name="pairs0", align_bytes=64, offset=43008))
         gather_v(0)
         part_v(0)
         gather_ts(0)
@@ -265,7 +283,6 @@ def tile_list_gmu_silu_scat_kernel(
         gather_ts(1)
         gather_t(1)
         cast_z(1)
-        quantize_z(1)
         turn(0)
         last = len(CHUNKS) - 1
         for c in range(len(CHUNKS)):
@@ -276,14 +293,17 @@ def tile_list_gmu_silu_scat_kernel(
             gate(c)
             if c == 0:
                 products(1)
-                windows.append(reuse.tile([P, T], F32, name="window1", align_bytes=64, offset=24576))
-                nc.gpsimd.memset(windows[1][:], 0.0)
             if c < last:
                 activations(c + 1)
-            if h == 1 and nt + 2 < TILES:
-                cast_z(nt + 2)
+            for slot, (znt, a) in enumerate(LATE_CASTS.get(c, ())):
+                cast_late(znt, a, TH_AT + 4096 * c + 1024 * slot)
+            if c == 0:
+                quantize_z(1)
+            if c in (2, 4):
+                quantize_late(1 + c // 2, TH_AT + 4096 * c + 1024)
             scatter(c)
-            if h == 1 and nt + 2 < TILES:
-                quantize_z(nt + 2)
+            if c == 0:
+                windows.append(reuse.tile([P, T], F32, name="window1", align_bytes=64, offset=WINDOW_AT))
+                nc.gpsimd.memset(windows[1][:], 0.0)
             if c < last:
                 turn(c + 1)

@@ -24,9 +24,8 @@ BLOCKS = HALF // P
 LIST_COLS = HALF // 16
 TILES = N // P
 TH_AT = 8192
-WINDOW_AT = 45056
+WINDOW_AT = 49152
 BANK = 2048
-LATE_CASTS = {1: ((2, 0), (2, 1), (2, 2)), 3: ((3, 0), (3, 1), (3, 2))}
 CHUNKS = [(nt, h) for nt in range(TILES) for h in range(J // HALF)]
 
 
@@ -57,13 +56,15 @@ def tile_list_gmu_silu_scat_kernel(
         neg_half_w = keep.tile([P, J // P], F32, name="neg_half_w")
         windows = [keep.tile([P, T], F32, name="window0")]
 
+        nc.gpsimd.memset(tab2s[:].bitcast(I32), 0)
         nc.vector.memset(tabs[:].bitcast(I32), 0)
-        nc.vector.memset(tab2s[:].bitcast(I32), 0)
-        nc.vector.memset(rows[:], 0.0)
         nc.vector.memset(wts[:].bitcast(I32), 0)
+        nc.vector.memset(rows[:], 0.0)
         nc.vector.memset(wvs[:].rearrange("p a n -> p (a n)").bitcast(I32), 0)
         nc.vector.memset(vs1[:].bitcast(I32), 0)
         nc.vector.memset(windows[0][:], 0.0)
+        for q in range(4):
+            nc.gpsimd.dma_start(out=tab2s[32 * q : 32 * q + 4, :].bitcast(I32), in_=tab2_scales[0, 4 * q : 4 * q + 4, :].bitcast(I32))
         make_identity(nc, ident[:])
 
         z_raw = {}
@@ -84,26 +85,24 @@ def tile_list_gmu_silu_scat_kernel(
                 for nt in range(n0 // P, n1 // P):
                     z_raw[(nt, a)] = tile[:, :, P * nt - n0 : P * (nt + 1) - n0]
 
-        nc.sync.dma_start(list1[:], offs)
         nc.sync.dma_start(list2[:], offs2)
+        nc.sync.dma_start(list1[:], offs)
+        nc.sync.dma_start(out=tab2w[:].bitcast(I32), in_=tab2_words[0].rearrange("p t i -> p (t i)").bitcast(I32))
+        nc.sync.dma_start(out=tabw[:].bitcast(I32), in_=tab_words[0].rearrange("p t i -> p (t i)").bitcast(I32))
         nc.sync.dma_start(out=wtw[:].bitcast(I32), in_=wt_words[0].bitcast(I32))
         for q in range(4):
-            nc.sync.dma_start(out=tabs[32 * q : 32 * q + 8, :].bitcast(I32), in_=tab_scales[:, 4 * q : 4 * q + 4, :].bitcast(I32))
-        nc.sync.dma_start(out=tabw[:].bitcast(I32), in_=tab_words[0].rearrange("p t i -> p (t i)").bitcast(I32))
+            nc.scalar.dma_start(out=tabs[32 * q : 32 * q + 8, :].bitcast(I32), in_=tab_scales[:, 4 * q : 4 * q + 4, :].bitcast(I32))
         for q in range(4):
-            nc.gpsimd.dma_start(out=wts[32 * q : 32 * q + 4, :].bitcast(I32), in_=wt_scales[0, 4 * q : 4 * q + 4, :].bitcast(I32))
+            nc.scalar.dma_start(out=wts[32 * q : 32 * q + 4, :].bitcast(I32), in_=wt_scales[0, 4 * q : 4 * q + 4, :].bitcast(I32))
+        nc.scalar.dma_start(out=rows[0 : J // P, :], in_=wgo[0].rearrange("(r c) -> r c", c=P))
+        nc.scalar.dma_start(out=rows[J // P : J // P + TILES, :], in_=b.rearrange("(r c) -> r c", c=P))
         for q in range(4):
-            nc.sync.dma_start(out=tab2s[32 * q : 32 * q + 4, :].bitcast(I32), in_=tab2_scales[0, 4 * q : 4 * q + 4, :].bitcast(I32))
-        nc.sync.dma_start(out=tab2w[:].bitcast(I32), in_=tab2_words[0].rearrange("p t i -> p (t i)").bitcast(I32))
-        load_z(0, P, (0, 1, 2))
-        for q in range(4):
-            nc.sync.dma_start(
+            nc.scalar.dma_start(
                 out=wvs[32 * q : 32 * q + 4, :, :].bitcast(I32),
                 in_=wv_scales[:, 4 * q : 4 * q + 4, :].rearrange("a r n -> r a n").bitcast(I32),
             )
         load_wv(0, P)
-        nc.sync.dma_start(out=rows[0 : J // P, :], in_=wgo[0].rearrange("(r c) -> r c", c=P))
-        nc.sync.dma_start(out=rows[J // P : J // P + TILES, :], in_=b.rearrange("(r c) -> r c", c=P))
+        load_z(0, P, (0, 1, 2))
         load_z(P, 2 * P, (0, 1, 2))
         load_wv(P, N)
         load_z(2 * P, N, (0, 1, 2))
@@ -112,16 +111,18 @@ def tile_list_gmu_silu_scat_kernel(
         z_scales = [keep.tile([P, 3, P], U8, name=f"z_scales{nt}", align_bytes=64) for nt in range(TILES)]
         z_bf = {}
 
-        def cast_z(nt):
-            z_bf[nt] = reuse.tile([P, 3, P, PACK], BF16, name=f"z_bf{nt}", align_bytes=64, offset=(0, 5 * HALF)[nt])
+        def cast_z(nt, offset):
+            z_bf[nt] = reuse.tile([P, 3, P, PACK], BF16, name=f"z_bf{nt}", align_bytes=64, offset=offset)
             for a in range(3):
-                if nt != 1:
-                    nc.scalar.activation(out=z_bf[nt][:, a, :, :], in_=z_raw[(nt, a)].rearrange("p i n -> p n i"), func=ACT.Copy)
+                dst = z_bf[nt][:, a, :, :].rearrange("p (c u) i -> p c i u", u=4)
+                src = z_raw[(nt, a)].rearrange("p i (c u) -> p c i u", u=4)
+                if nt == 0:
+                    nc.scalar.copy(dst, src)
                 else:
-                    nc.vector.tensor_copy(z_bf[nt][:, a, :, :], z_raw[(nt, a)].rearrange("p i n -> p n i"))
+                    nc.vector.tensor_copy(dst, src)
 
-        def quantize_z(nt):
-            z_codes[nt] = reuse.tile([P, 3, P], U32, name=f"z_codes{nt}", align_bytes=64, offset=(40960, TH_AT + 1024)[nt])
+        def quantize_z(nt, offset):
+            z_codes[nt] = reuse.tile([P, 3, P], U32, name=f"z_codes{nt}", align_bytes=64, offset=offset)
             for a0, a1 in ((0, 2), (2, 3)):
                 nc.vector.quantize_mx(
                     out=z_codes[nt][:, a0:a1, :].rearrange("p s n -> p (s n)").bitcast(FP8X4),
@@ -129,25 +130,9 @@ def tile_list_gmu_silu_scat_kernel(
                     in_=z_bf[nt][:, a0:a1, :, :].rearrange("p s n i -> p (s n i)"),
                 )
 
-        late_bf = {}
-
-        def cast_late(nt, a, offset):
-            late_bf[(nt, a)] = reuse.tile([P, P, PACK], BF16, name=f"z_bf{nt}_{a}", align_bytes=64, offset=offset)
-            if a < 2:
-                nc.vector.tensor_copy(late_bf[(nt, a)][:], z_raw[(nt, a)].rearrange("p i n -> p n i"))
-            else:
-                nc.scalar.activation(out=late_bf[(nt, a)][:], in_=z_raw[(nt, a)].rearrange("p i n -> p n i"), func=ACT.Copy)
-
-        def quantize_late(nt, offset):
-            z_codes[nt] = reuse.tile([P, 3, P], U32, name=f"z_codes{nt}", align_bytes=64, offset=offset)
-            for a in range(3):
-                nc.vector.quantize_mx(
-                    out=z_codes[nt][:, a, :].bitcast(FP8X4), scales=z_scales[nt][:, a, :], in_=late_bf[(nt, a)][:].rearrange("p n i -> p (n i)")
-                )
-
         vw = [keep.tile([P, 2, 2 * HALF], U8, name=f"vw{h}", align_bytes=64) for h in range(2)]
         tw = [keep.tile([P, HALF], U32, name="tw0", align_bytes=64)]
-        ts = [keep.tile([P, HALF], U8, name="ts0", align_bytes=64)]
+        ts = []
         pairs = []
 
         def list_half(tile, h):
@@ -216,6 +201,9 @@ def tile_list_gmu_silu_scat_kernel(
                 sides = sides[::-1]
             for bank, act, weighted, factor in sides:
                 nc.scalar.activation(out=act[:], in_=bank[:], func=ACT.Silu)
+                if c == 0 and act is at:
+                    nc.scalar.activation(out=neg_half_w[:], in_=turned[:, 0, 0 : J // P], func=ACT.Copy, scale=-0.5)
+                    nc.scalar.activation(out=halves[:], in_=turned[:, 0, 0 : J // P + TILES], func=ACT.Copy, scale=0.5)
             for side, (bank, act, weighted, factor) in enumerate(sides):
                 if side == (1 if c > 1 else 2):
                     tanh()
@@ -246,10 +234,7 @@ def tile_list_gmu_silu_scat_kernel(
 
         def gate(c):
             st = stage[c]
-            if c == 0:
-                gated = reuse.tile([P, HALF], F32, name="gated0", align_bytes=64, offset=WINDOW_AT)
-            else:
-                gated = work.tile([P, HALF], F32, name="gated")
+            gated = work.tile([P, HALF], F32, name="gated")
             nc.vector.scalar_tensor_tensor(gated[:], st["th"][:], 1.0, st["diff"][:].rearrange("p b j -> p (b j)"), ALU.add, ALU.mult)
             st["gated"] = gated
 
@@ -260,47 +245,39 @@ def tile_list_gmu_silu_scat_kernel(
             if h == 1:
                 nc.sync.dma_start(out=out[P * nt : P * (nt + 1), :], in_=window[:])
 
+        gather_t(0)
         nc.vector.tensor_copy(vs0[:], tabs[:].indirect(list1[:]))
         nc.scalar.dma_start(out=vs1[0:112, :].bitcast(I32), in_=vs0[4:116, :].bitcast(I32))
-        pairs.append(reuse.tile([P, HALF], U32, name="pairs0", align_bytes=64, offset=43008))
-        gather_v(0)
-        part_v(0)
+        ts.append(reuse.tile([P, HALF], U8, name="ts0", align_bytes=64, offset=43008))
         gather_ts(0)
-        gather_t(0)
-        cast_z(0)
+        for h in range(2):
+            pairs.append(reuse.tile([P, HALF], U32, name=f"pairs{h}", align_bytes=64, offset=4096))
+            gather_v(h)
+            part_v(h)
+        cast_z(0, WINDOW_AT - 5 * HALF)
         turned = psum.tile([P, BLOCKS, P], F32, name="turned", offset=BANK * 5)
         nc.tensor.transpose(turned[:, 0, :], rows[:], ident[:])
-        nc.scalar.activation(out=halves[:], in_=turned[:, 0, 0 : J // P + TILES], func=ACT.Copy, scale=0.5)
-        nc.scalar.activation(out=neg_half_w[:], in_=turned[:, 0, 0 : J // P], func=ACT.Copy, scale=-0.5)
-        quantize_z(0)
+        quantize_z(0, 40960)
         products(0)
-        ts.append(reuse.tile([P, HALF], U8, name="ts1", align_bytes=64, offset=0))
-        tw.append(reuse.tile([P, HALF], U32, name="tw1", align_bytes=64, offset=HALF))
-        pairs.append(reuse.tile([P, HALF], U32, name="pairs1", align_bytes=64, offset=5 * HALF))
-        gather_v(1)
+        ts.append(reuse.tile([P, HALF], U8, name="ts1", align_bytes=64, offset=WINDOW_AT - 5 * HALF))
+        tw.append(reuse.tile([P, HALF], U32, name="tw1", align_bytes=64, offset=WINDOW_AT - 4 * HALF))
         activations(0)
-        part_v(1)
-        gather_ts(1)
         gather_t(1)
-        cast_z(1)
+        gather_ts(1)
+        cast_z(1, WINDOW_AT)
         turn(0)
         last = len(CHUNKS) - 1
         for c in range(len(CHUNKS)):
             nt, h = CHUNKS[c]
-            if 0 < c < last:
-                products(c + 1)
             unload(c)
             gate(c)
-            if c == 0:
-                products(1)
+            if c in (1, 3):
+                cast_z(2 + c // 2, TH_AT + 4096 * c)
+            if c in (0, 2, 4):
+                quantize_z(1 + c // 2, TH_AT + 4096 * c + 1024)
             if c < last:
+                products(c + 1)
                 activations(c + 1)
-            for slot, (znt, a) in enumerate(LATE_CASTS.get(c, ())):
-                cast_late(znt, a, TH_AT + 4096 * c + 1024 * slot)
-            if c == 0:
-                quantize_z(1)
-            if c in (2, 4):
-                quantize_late(1 + c // 2, TH_AT + 4096 * c + 1024)
             scatter(c)
             if c == 0:
                 windows.append(reuse.tile([P, T], F32, name="window1", align_bytes=64, offset=WINDOW_AT))

@@ -197,7 +197,7 @@ def tile_list_gmu_silu_scat_kernel(
                 nc.scalar.activation(out=th[:], in_=st["z"][:], func=ACT.Tanh, bias=halves[:, col : col + 1], scale=0.5)
 
             sides = [(st["ht"], at, wat, neg_half_w), (st["hv"], av, wav, halves)]
-            if c > 0:
+            if c == 1:
                 sides = sides[::-1]
             for bank, act, weighted, factor in sides:
                 nc.scalar.activation(out=act[:], in_=bank[:], func=ACT.Silu)
@@ -205,25 +205,21 @@ def tile_list_gmu_silu_scat_kernel(
                     nc.scalar.activation(out=neg_half_w[:], in_=turned[:, 0, 0 : J // P], func=ACT.Copy, scale=-0.5)
                     nc.scalar.activation(out=halves[:], in_=turned[:, 0, 0 : J // P + TILES], func=ACT.Copy, scale=0.5)
             for side, (bank, act, weighted, factor) in enumerate(sides):
-                if side == (1 if c > 1 else 2):
-                    tanh()
                 for blk in range(BLOCKS):
                     col = BLOCKS * h + blk
                     nc.scalar.activation(out=weighted[:, blk, :], in_=act[:, blk, :], func=ACT.Copy, scale=factor[:, col : col + 1])
-            if c <= 1:
-                tanh()
+            tanh()
             st.update({"wav": wav, "wat": wat, "th": th})
 
         def turn(c):
             st = stage[c]
             base = psum.tile([P, BLOCKS, P], F32, name=f"base{c}", offset=BANK * (4 + c % 2))
             diff = psum.tile([P, BLOCKS, P], F32, name=f"diff{c}", offset=BANK * (6 + c % 2))
-            first, second = ("wav", "wat") if c == 0 else ("wat", "wav")
-            for blk in reversed(range(BLOCKS)):
-                nc.tensor.matmul(diff[:, blk, :], st[first][:, blk, :], ident[:], start=True, stop=False, is_transpose=True)
-                nc.tensor.matmul(diff[:, blk, :], st[second][:, blk, :], ident[:], start=False, stop=True, is_transpose=True)
-            for blk in reversed(range(BLOCKS)):
+            for blk in range(BLOCKS):
                 nc.tensor.transpose(base[:, blk, :], st["wat"][:, blk, :], ident[:])
+            for blk in range(BLOCKS):
+                nc.tensor.matmul(diff[:, blk, :], st["wat"][:, blk, :], ident[:], start=True, stop=False, is_transpose=True)
+                nc.tensor.matmul(diff[:, blk, :], st["wav"][:, blk, :], ident[:], start=False, stop=True, is_transpose=True)
             st.update({"base": base, "diff": diff})
 
         def unload(c):
@@ -278,9 +274,8 @@ def tile_list_gmu_silu_scat_kernel(
             if c < last:
                 products(c + 1)
                 activations(c + 1)
+                turn(c + 1)
             scatter(c)
             if c == 0:
                 windows.append(reuse.tile([P, T], F32, name="window1", align_bytes=64, offset=WINDOW_AT))
                 nc.gpsimd.memset(windows[1][:], 0.0)
-            if c < last:
-                turn(c + 1)

@@ -26,6 +26,8 @@ TILES = N // P
 TH_AT = 8192
 WINDOW_AT = 49152
 BANK = 2048
+LATE_CASTS = {0: ((2, 0),), 1: ((2, 1),), 2: ((2, 2), (3, 0)), 3: ((3, 1),), 4: ((3, 2),)}
+LATE_QUANTS = {2: ((2, 0),), 3: ((2, 1), (2, 2)), 4: ((3, 0),), 5: ((3, 1), (3, 2))}
 CHUNKS = [(nt, h) for nt in range(TILES) for h in range(J // HALF)]
 
 
@@ -111,24 +113,33 @@ def tile_list_gmu_silu_scat_kernel(
         z_scales = [keep.tile([P, 3, P], U8, name=f"z_scales{nt}", align_bytes=64) for nt in range(TILES)]
         z_bf = {}
 
+        def cast_pass(engine_copy, dst, nt, a):
+            engine_copy(dst.rearrange("p (c u) i -> p c i u", u=2), z_raw[(nt, a)].rearrange("p i (c u) -> p c i u", u=2))
+
         def cast_z(nt, offset):
             z_bf[nt] = reuse.tile([P, 3, P, PACK], BF16, name=f"z_bf{nt}", align_bytes=64, offset=offset)
             for a in range(3):
-                dst = z_bf[nt][:, a, :, :].rearrange("p (c u) i -> p c i u", u=4)
-                src = z_raw[(nt, a)].rearrange("p i (c u) -> p c i u", u=4)
-                if nt == 0:
-                    nc.scalar.copy(dst, src)
-                else:
-                    nc.vector.tensor_copy(dst, src)
+                cast_pass(nc.scalar.copy if nt == 0 else nc.vector.tensor_copy, z_bf[nt][:, a, :, :], nt, a)
 
         def quantize_z(nt, offset):
-            z_codes[nt] = reuse.tile([P, 3, P], U32, name=f"z_codes{nt}", align_bytes=64, offset=offset)
+            codes = reuse.tile([P, 3, P], U32, name=f"z_codes{nt}", align_bytes=64, offset=offset)
             for a0, a1 in ((0, 2), (2, 3)):
                 nc.vector.quantize_mx(
-                    out=z_codes[nt][:, a0:a1, :].rearrange("p s n -> p (s n)").bitcast(FP8X4),
+                    out=codes[:, a0:a1, :].rearrange("p s n -> p (s n)").bitcast(FP8X4),
                     scales=z_scales[nt][:, a0:a1, :].rearrange("p s n -> p (s n)"),
                     in_=z_bf[nt][:, a0:a1, :, :].rearrange("p s n i -> p (s n i)"),
                 )
+            for a in range(3):
+                z_codes[(nt, a)] = codes[:, a, :]
+
+        def cast_late(nt, a, offset):
+            z_bf[(nt, a)] = reuse.tile([P, P, PACK], BF16, name=f"z_bf{nt}_{a}", align_bytes=64, offset=offset)
+            cast_pass(nc.scalar.copy, z_bf[(nt, a)][:], nt, a)
+
+        def quantize_late(nt, a, offset):
+            codes = reuse.tile([P, P], U32, name=f"z_codes{nt}_{a}", align_bytes=64, offset=offset)
+            nc.vector.quantize_mx(out=codes[:].bitcast(FP8X4), scales=z_scales[nt][:, a, :], in_=z_bf[(nt, a)][:].rearrange("p n i -> p (n i)"))
+            z_codes[(nt, a)] = codes[:]
 
         vw = [keep.tile([P, 2, 2 * HALF], U8, name=f"vw{h}", align_bytes=64) for h in range(2)]
         tw = [keep.tile([P, HALF], U32, name="tw0", align_bytes=64)]
@@ -178,7 +189,7 @@ def tile_list_gmu_silu_scat_kernel(
             ]
             for a, (codes, scales) in enumerate(moving):
                 nc.tensor.matmul_mx(
-                    out=z[:], lhsT=z_codes[nt][:, a, :].bitcast(FP8X4), lhsT_scale=z_scales[nt][:, a, :],
+                    out=z[:], lhsT=z_codes[(nt, a)].bitcast(FP8X4), lhsT_scale=z_scales[nt][:, a, :],
                     rhs=codes, rhs_scale=scales, start=(a == 0), stop=(a == 2),
                 )
             stage[c] = {"hv": hv, "ht": ht, "z": z}
@@ -267,14 +278,16 @@ def tile_list_gmu_silu_scat_kernel(
             nt, h = CHUNKS[c]
             unload(c)
             gate(c)
-            if c in (1, 3):
-                cast_z(2 + c // 2, TH_AT + 4096 * c)
-            if c in (0, 2, 4):
-                quantize_z(1 + c // 2, TH_AT + 4096 * c + 1024)
+            if c == 0:
+                quantize_z(1, TH_AT + 512)
+            for slot, (znt, a) in enumerate(LATE_QUANTS.get(c, ())):
+                quantize_late(znt, a, TH_AT + 4096 * c + 1024 + HALF * slot)
             if c < last:
                 products(c + 1)
                 activations(c + 1)
                 turn(c + 1)
+            for slot, (znt, a) in enumerate(LATE_CASTS.get(c, ())):
+                cast_late(znt, a, TH_AT + 4096 * c + (0 if c > 0 and slot == 0 else 2560 - 64))
             scatter(c)
             if c == 0:
                 windows.append(reuse.tile([P, T], F32, name="window1", align_bytes=64, offset=WINDOW_AT))

@@ -24,10 +24,11 @@ BLOCKS = HALF // P
 LIST_COLS = HALF // 16
 TILES = N // P
 TH_AT = 8192
-WINDOW_AT = 49152
 BANK = 2048
-LATE_CASTS = {0: ((2, 0),), 1: ((2, 1),), 2: ((2, 2), (3, 0)), 3: ((3, 1),), 4: ((3, 2),)}
-LATE_QUANTS = {2: ((2, 0),), 3: ((2, 1), (2, 2)), 4: ((3, 0),), 5: ((3, 1), (3, 2))}
+WAV_AT = 49152
+RAW_AT = 0
+ROUNDED_AT = 65536
+PARTS = ((0, 2), (2, 3))
 CHUNKS = [(nt, h) for nt in range(TILES) for h in range(J // HALF)]
 
 
@@ -45,7 +46,7 @@ def tile_list_gmu_silu_scat_kernel(
         list2 = keep.tile([P, J // 16], U16, name="list2")
         tabw = keep.tile([P, T], U32, name="tabw")
         tab2w = keep.tile([P, T], U32, name="tab2w")
-        tabs = reuse.tile([P, T], U8, name="tabs", align_bytes=64, offset=43008)
+        tabs = keep.tile([P, T], U8, name="tabs")
         tab2s = keep.tile([P, T], U8, name="tab2s")
         vs0 = keep.tile([P, J], U8, name="vs0", align_bytes=64)
         vs1 = keep.tile([P, J], U8, name="vs1", align_bytes=64)
@@ -56,17 +57,16 @@ def tile_list_gmu_silu_scat_kernel(
         ident = keep.tile([P, P], F32, name="ident")
         halves = keep.tile([P, J // P + TILES], F32, name="halves")
         neg_half_w = keep.tile([P, J // P], F32, name="neg_half_w")
-        windows = [keep.tile([P, T], F32, name="window0")]
+        windows = [keep.tile([P, T], F32, name=f"window{i}") for i in range(2)]
 
-        nc.gpsimd.memset(tab2s[:].bitcast(I32), 0)
-        nc.vector.memset(tabs[:].bitcast(I32), 0)
+        nc.gpsimd.memset(tabs[:].bitcast(I32), 0)
+        nc.vector.memset(tab2s[:].bitcast(I32), 0)
         nc.vector.memset(wts[:].bitcast(I32), 0)
         nc.vector.memset(rows[:], 0.0)
         nc.vector.memset(wvs[:].rearrange("p a n -> p (a n)").bitcast(I32), 0)
         nc.vector.memset(vs1[:].bitcast(I32), 0)
-        nc.vector.memset(windows[0][:], 0.0)
-        for q in range(4):
-            nc.gpsimd.dma_start(out=tab2s[32 * q : 32 * q + 4, :].bitcast(I32), in_=tab2_scales[0, 4 * q : 4 * q + 4, :].bitcast(I32))
+        for window in windows:
+            nc.vector.memset(window[:], 0.0)
         make_identity(nc, ident[:])
 
         z_raw = {}
@@ -81,7 +81,10 @@ def tile_list_gmu_silu_scat_kernel(
 
         def load_z(n0, n1, passes):
             for a in passes:
-                tile = keep.tile([P, PACK, n1 - n0], F32, name=f"z_raw{a}_{n0}")
+                if n0 == 0:
+                    tile = reuse.tile([P, PACK, P], F32, name=f"z_raw{a}_{n0}", align_bytes=64, offset=RAW_AT + 2048 * a)
+                else:
+                    tile = keep.tile([P, PACK, n1 - n0], F32, name=f"z_raw{a}_{n0}")
                 src = zv[512 * a : 512 * (a + 1), n0:n1] if a < 2 else zt[:, n0:n1]
                 nc.sync.dma_start(out=tile[:], in_=src.rearrange("(p i) n -> p i n", i=PACK))
                 for nt in range(n0 // P, n1 // P):
@@ -90,24 +93,22 @@ def tile_list_gmu_silu_scat_kernel(
         nc.sync.dma_start(list2[:], offs2)
         nc.sync.dma_start(list1[:], offs)
         nc.sync.dma_start(out=tab2w[:].bitcast(I32), in_=tab2_words[0].rearrange("p t i -> p (t i)").bitcast(I32))
+        for q in range(4):
+            nc.sync.dma_start(out=tabs[32 * q : 32 * q + 8, :].bitcast(I32), in_=tab_scales[:, 4 * q : 4 * q + 4, :].bitcast(I32))
         nc.sync.dma_start(out=tabw[:].bitcast(I32), in_=tab_words[0].rearrange("p t i -> p (t i)").bitcast(I32))
         nc.sync.dma_start(out=wtw[:].bitcast(I32), in_=wt_words[0].bitcast(I32))
         for q in range(4):
-            nc.scalar.dma_start(out=tabs[32 * q : 32 * q + 8, :].bitcast(I32), in_=tab_scales[:, 4 * q : 4 * q + 4, :].bitcast(I32))
+            nc.scalar.dma_start(out=tab2s[32 * q : 32 * q + 4, :].bitcast(I32), in_=tab2_scales[0, 4 * q : 4 * q + 4, :].bitcast(I32))
         for q in range(4):
             nc.scalar.dma_start(out=wts[32 * q : 32 * q + 4, :].bitcast(I32), in_=wt_scales[0, 4 * q : 4 * q + 4, :].bitcast(I32))
-        nc.scalar.dma_start(out=rows[0 : J // P, :], in_=wgo[0].rearrange("(r c) -> r c", c=P))
-        nc.scalar.dma_start(out=rows[J // P : J // P + TILES, :], in_=b.rearrange("(r c) -> r c", c=P))
         for q in range(4):
             nc.scalar.dma_start(
                 out=wvs[32 * q : 32 * q + 4, :, :].bitcast(I32),
                 in_=wv_scales[:, 4 * q : 4 * q + 4, :].rearrange("a r n -> r a n").bitcast(I32),
             )
         load_wv(0, P)
-        load_z(0, P, (0, 1, 2))
-        load_z(P, 2 * P, (0, 1, 2))
-        load_wv(P, N)
-        load_z(2 * P, N, (0, 1, 2))
+        nc.sync.dma_start(out=rows[0 : J // P, :], in_=wgo[0].rearrange("(r c) -> r c", c=P))
+        nc.sync.dma_start(out=rows[J // P : J // P + TILES, :], in_=b.rearrange("(r c) -> r c", c=P))
 
         z_codes = {}
         z_scales = [keep.tile([P, 3, P], U8, name=f"z_scales{nt}", align_bytes=64) for nt in range(TILES)]
@@ -116,35 +117,27 @@ def tile_list_gmu_silu_scat_kernel(
         def cast_pass(engine_copy, dst, nt, a):
             engine_copy(dst.rearrange("p (c u) i -> p c i u", u=2), z_raw[(nt, a)].rearrange("p i (c u) -> p c i u", u=2))
 
-        def cast_z(nt, offset):
-            z_bf[nt] = reuse.tile([P, 3, P, PACK], BF16, name=f"z_bf{nt}", align_bytes=64, offset=offset)
-            for a in range(3):
-                cast_pass(nc.scalar.copy if nt == 0 else nc.vector.tensor_copy, z_bf[nt][:, a, :, :], nt, a)
+        def cast_z(engine_copy, nt, a0, a1, offset):
+            tile = reuse.tile([P, a1 - a0, P, PACK], BF16, name=f"z_bf{nt}_{a0}", align_bytes=64, offset=offset)
+            for a in range(a0, a1):
+                cast_pass(engine_copy, tile[:, a - a0, :, :], nt, a)
+                z_bf[(nt, a)] = (tile, a - a0)
 
-        def quantize_z(nt, offset):
-            codes = reuse.tile([P, 3, P], U32, name=f"z_codes{nt}", align_bytes=64, offset=offset)
-            for a0, a1 in ((0, 2), (2, 3)):
-                nc.vector.quantize_mx(
-                    out=codes[:, a0:a1, :].rearrange("p s n -> p (s n)").bitcast(FP8X4),
-                    scales=z_scales[nt][:, a0:a1, :].rearrange("p s n -> p (s n)"),
-                    in_=z_bf[nt][:, a0:a1, :, :].rearrange("p s n i -> p (s n i)"),
-                )
-            for a in range(3):
-                z_codes[(nt, a)] = codes[:, a, :]
-
-        def cast_late(nt, a, offset):
-            z_bf[(nt, a)] = reuse.tile([P, P, PACK], BF16, name=f"z_bf{nt}_{a}", align_bytes=64, offset=offset)
-            cast_pass(nc.scalar.copy, z_bf[(nt, a)][:], nt, a)
-
-        def quantize_late(nt, a, offset):
-            codes = reuse.tile([P, P], U32, name=f"z_codes{nt}_{a}", align_bytes=64, offset=offset)
-            nc.vector.quantize_mx(out=codes[:].bitcast(FP8X4), scales=z_scales[nt][:, a, :], in_=z_bf[(nt, a)][:].rearrange("p n i -> p (n i)"))
-            z_codes[(nt, a)] = codes[:]
+        def quantize_z(nt, a0, a1, offset):
+            codes = reuse.tile([P, a1 - a0, P], U32, name=f"z_codes{nt}_{a0}", align_bytes=64, offset=offset)
+            tile, first = z_bf[(nt, a0)]
+            nc.vector.quantize_mx(
+                out=codes[:].rearrange("p s n -> p (s n)").bitcast(FP8X4),
+                scales=z_scales[nt][:, a0:a1, :].rearrange("p s n -> p (s n)"),
+                in_=tile[:, first : first + a1 - a0, :, :].rearrange("p s n i -> p (s n i)"),
+            )
+            for a in range(a0, a1):
+                z_codes[(nt, a)] = codes[:, a - a0, :]
 
         vw = [keep.tile([P, 2, 2 * HALF], U8, name=f"vw{h}", align_bytes=64) for h in range(2)]
         tw = [keep.tile([P, HALF], U32, name="tw0", align_bytes=64)]
-        ts = []
-        pairs = []
+        ts = [keep.tile([P, HALF], U8, name="ts0", align_bytes=64)]
+        pairs = [keep.tile([P, HALF], U32, name=f"pairs{h}", align_bytes=64) for h in range(2)]
 
         def list_half(tile, h):
             return tile[:, LIST_COLS * h : LIST_COLS * (h + 1)]
@@ -199,7 +192,7 @@ def tile_list_gmu_silu_scat_kernel(
             st = stage[c]
             av = work.tile([P, BLOCKS, P], F32, name="av", bufs=1)
             at = work.tile([P, BLOCKS, P], F32, name="at", bufs=1)
-            wav = work.tile([P, BLOCKS, P], F32, name="wav")
+            wav = reuse.tile([P, BLOCKS, P], F32, name=f"wav{c}", align_bytes=64, offset=WAV_AT + 2048 * c)
             wat = work.tile([P, BLOCKS, P], F32, name="wat")
             th = reuse.tile([P, HALF], F32, name=f"th{c}", align_bytes=64, offset=TH_AT + 4096 * c + 512)
 
@@ -254,41 +247,39 @@ def tile_list_gmu_silu_scat_kernel(
 
         gather_t(0)
         nc.vector.tensor_copy(vs0[:], tabs[:].indirect(list1[:]))
-        nc.scalar.dma_start(out=vs1[0:112, :].bitcast(I32), in_=vs0[4:116, :].bitcast(I32))
-        ts.append(reuse.tile([P, HALF], U8, name="ts0", align_bytes=64, offset=43008))
+        load_z(0, P, (0, 1, 2))
+        nc.sync.dma_start(out=vs1[0:112, :].bitcast(I32), in_=vs0[4:116, :].bitcast(I32))
+        load_z(P, 2 * P, (0, 1, 2))
+        load_wv(P, N)
+        load_z(2 * P, N, (0, 1, 2))
         gather_ts(0)
         for h in range(2):
-            pairs.append(reuse.tile([P, HALF], U32, name=f"pairs{h}", align_bytes=64, offset=4096))
             gather_v(h)
+        for h in range(2):
             part_v(h)
-        cast_z(0, WINDOW_AT - 5 * HALF)
+        cast_z(nc.scalar.copy, 0, 0, 3, ROUNDED_AT)
         turned = psum.tile([P, BLOCKS, P], F32, name="turned", offset=BANK * 5)
         nc.tensor.transpose(turned[:, 0, :], rows[:], ident[:])
-        quantize_z(0, 40960)
-        products(0)
-        ts.append(reuse.tile([P, HALF], U8, name="ts1", align_bytes=64, offset=WINDOW_AT - 5 * HALF))
-        tw.append(reuse.tile([P, HALF], U32, name="tw1", align_bytes=64, offset=WINDOW_AT - 4 * HALF))
-        activations(0)
-        gather_t(1)
+        for a0, a1 in PARTS:
+            quantize_z(0, a0, a1, 40960 + HALF * a0)
+        ts.append(reuse.tile([P, HALF], U8, name="ts1", align_bytes=64, offset=RAW_AT + 2048))
+        tw.append(reuse.tile([P, HALF], U32, name="tw1", align_bytes=64, offset=RAW_AT + 4096))
         gather_ts(1)
-        cast_z(1, WINDOW_AT)
+        gather_t(1)
+        cast_z(nc.vector.tensor_copy, 1, 0, 3, ROUNDED_AT + 5 * HALF)
+        products(0)
+        activations(0)
         turn(0)
         last = len(CHUNKS) - 1
         for c in range(len(CHUNKS)):
-            nt, h = CHUNKS[c]
             unload(c)
             gate(c)
-            if c == 0:
-                quantize_z(1, TH_AT + 512)
-            for slot, (znt, a) in enumerate(LATE_QUANTS.get(c, ())):
-                quantize_late(znt, a, TH_AT + 4096 * c + 1024 + HALF * slot)
+            if c < 6:
+                quantize_z(1 + c // 2, *PARTS[c % 2], WAV_AT + 2048 * c)
             if c < last:
                 products(c + 1)
                 activations(c + 1)
                 turn(c + 1)
-            for slot, (znt, a) in enumerate(LATE_CASTS.get(c, ())):
-                cast_late(znt, a, TH_AT + 4096 * c + (0 if c > 0 and slot == 0 else 2560 - 64))
+            if c < 4:
+                cast_z(nc.scalar.copy, 2 + c // 2, *PARTS[c % 2], TH_AT + 4096 * c + 2048)
             scatter(c)
-            if c == 0:
-                windows.append(reuse.tile([P, T], F32, name="window1", align_bytes=64, offset=WINDOW_AT))
-                nc.gpsimd.memset(windows[1][:], 0.0)

@@ -168,22 +168,24 @@ def tile_list_gmu_silu_scat_kernel(
                     out=ht[:, blk, :], lhsT=tw[h][:, P * blk : P * (blk + 1)].bitcast(FP8X4), lhsT_scale=ts[h][:, P * blk : P * (blk + 1)],
                     rhs=wtw[:, 2 * P * nt : 2 * P * (nt + 1)].bitcast(FP4X4), rhs_scale=wts[:, ncols], start=True, stop=True,
                 )
-            for blk in range(BLOCKS):
-                j0 = HALF * h + P * blk
-                for a, plane in enumerate((vs0, vs1)):
+            for a, plane in enumerate((vs0, vs1)):
+                for blk in range(BLOCKS):
+                    j0 = HALF * h + P * blk
                     nc.tensor.matmul_mx(
                         out=hv[:, blk, :], lhsT=vw[h][:, a, 2 * P * blk : 2 * P * (blk + 1)].bitcast(FP4X4), lhsT_scale=plane[:, j0 : j0 + P],
-                        rhs=wv_cols[nt][:, a, :].bitcast(FP8X4), rhs_scale=wvs[:, a, ncols], start=(a == 0), stop=(a == 1),
+                        rhs=wv_cols[nt][:, a, :].bitcast(FP8X4), rhs_scale=wvs[:, a, ncols],
+                        start=(a == 0 and blk == 0), stop=(a == 1 and blk == BLOCKS - 1),
                     )
             moving = [
                 (vw[h][:, 0, :].bitcast(FP4X4), vs0[:, jc]),
                 (vw[h][:, 1, :].bitcast(FP4X4), vs1[:, jc]),
                 (tw[h][:].bitcast(FP8X4), ts[h][:]),
             ]
-            for a, (codes, scales) in enumerate(moving):
+            for a in (0, 2, 1):
+                codes, scales = moving[a]
                 nc.tensor.matmul_mx(
                     out=z[:], lhsT=z_codes[(nt, a)].bitcast(FP8X4), lhsT_scale=z_scales[nt][:, a, :],
-                    rhs=codes, rhs_scale=scales, start=(a == 0), stop=(a == 2),
+                    rhs=codes, rhs_scale=scales, start=(a == 0), stop=(a == 1),
                 )
             stage[c] = {"hv": hv, "ht": ht, "z": z}
 
@@ -245,6 +247,7 @@ def tile_list_gmu_silu_scat_kernel(
             if h == 1:
                 nc.sync.dma_start(out=out[P * nt : P * (nt + 1), :], in_=window[:])
 
+        gather_ts(0)
         gather_t(0)
         nc.vector.tensor_copy(vs0[:], tabs[:].indirect(list1[:]))
         load_z(0, P, (0, 1, 2))
@@ -252,7 +255,6 @@ def tile_list_gmu_silu_scat_kernel(
         load_z(P, 2 * P, (0, 1, 2))
         load_wv(P, N)
         load_z(2 * P, N, (0, 1, 2))
-        gather_ts(0)
         for h in range(2):
             gather_v(h)
         for h in range(2):

@@ -27,6 +27,7 @@ TH_AT = 8192
 BANK = 2048
 WAV_AT = 49152
 RAW_AT = 0
+SPARE_AT = 73728
 ROUNDED_AT = 65536
 PARTS = ((0, 2), (2, 3))
 CHUNKS = [(nt, h) for nt in range(TILES) for h in range(J // HALF)]
@@ -46,7 +47,7 @@ def tile_list_gmu_silu_scat_kernel(
         list2 = keep.tile([P, J // 16], U16, name="list2")
         tabw = keep.tile([P, T], U32, name="tabw")
         tab2w = keep.tile([P, T], U32, name="tab2w")
-        tabs = keep.tile([P, T], U8, name="tabs")
+        tabs = reuse.tile([P, T], U8, name="tabs", offset=SPARE_AT)
         tab2s = keep.tile([P, T], U8, name="tab2s")
         vs0 = keep.tile([P, J], U8, name="vs0", align_bytes=64)
         vs1 = keep.tile([P, J], U8, name="vs1", align_bytes=64)
@@ -57,7 +58,7 @@ def tile_list_gmu_silu_scat_kernel(
         ident = keep.tile([P, P], F32, name="ident")
         halves = keep.tile([P, J // P + TILES], F32, name="halves")
         neg_half_w = keep.tile([P, J // P], F32, name="neg_half_w")
-        windows = [keep.tile([P, T], F32, name=f"window{i}") for i in range(2)]
+        windows = [keep.tile([P, T], F32, name="window0")]
 
         nc.gpsimd.memset(tabs[:].bitcast(I32), 0)
         nc.vector.memset(tab2s[:].bitcast(I32), 0)
@@ -65,8 +66,7 @@ def tile_list_gmu_silu_scat_kernel(
         nc.vector.memset(rows[:], 0.0)
         nc.vector.memset(wvs[:].rearrange("p a n -> p (a n)").bitcast(I32), 0)
         nc.vector.memset(vs1[:].bitcast(I32), 0)
-        for window in windows:
-            nc.vector.memset(window[:], 0.0)
+        nc.vector.memset(windows[0][:], 0.0)
         make_identity(nc, ident[:])
 
         z_raw = {}
@@ -250,6 +250,8 @@ def tile_list_gmu_silu_scat_kernel(
         gather_ts(0)
         gather_t(0)
         nc.vector.tensor_copy(vs0[:], tabs[:].indirect(list1[:]))
+        windows.append(reuse.tile([P, T], F32, name="window1", offset=SPARE_AT))
+        nc.gpsimd.memset(windows[1][:], 0.0)
         load_z(0, P, (0, 1, 2))
         nc.sync.dma_start(out=vs1[0:112, :].bitcast(I32), in_=vs0[4:116, :].bitcast(I32))
         load_z(P, 2 * P, (0, 1, 2))

@@ -19,18 +19,30 @@ ALU = mybir.AluOpType
 
 P = 128
 PACK = 4
+PASS = P * PACK
+Z_PASSES = (K + L) // PASS
+QUADRANTS = 4
 HALF = 512
 BLOCKS = HALF // P
 LIST_COLS = HALF // 16
 TILES = N // P
-TH_AT = 8192
-BANK = 2048
-WAV_AT = 49152
-RAW_AT = 0
-SPARE_AT = 73728
-ROUNDED_AT = 65536
-PARTS = ((0, 2), (2, 3))
+W_COLS = J // P
 CHUNKS = [(nt, h) for nt in range(TILES) for h in range(J // HALF)]
+PARTS = ((0, 2), (2, 3))
+PLANE_ROWS = 32 * (QUADRANTS - 1) + 4
+
+TILE_BYTES = 4 * HALF
+ROUNDED_BYTES = 2 * PACK * P * Z_PASSES
+RAW_AT = 0
+TH_AT = 8192
+CODES_AT = 40960
+WAV_AT = 49152
+ROUNDED_AT = 65536
+TABS_AT = 73728
+
+BANK = 2048
+HV_BANK, HT_BANK, Z_BANK = 0, 1, 2
+BASE_BANKS, DIFF_BANKS = (4, 5), (6, 7)
 
 
 def tile_list_gmu_silu_scat_kernel(
@@ -47,7 +59,7 @@ def tile_list_gmu_silu_scat_kernel(
         list2 = keep.tile([P, J // 16], U16, name="list2")
         tabw = keep.tile([P, T], U32, name="tabw")
         tab2w = keep.tile([P, T], U32, name="tab2w")
-        tabs = reuse.tile([P, T], U8, name="tabs", offset=SPARE_AT)
+        tabs = reuse.tile([P, T], U8, name="tabs", offset=TABS_AT)
         tab2s = keep.tile([P, T], U8, name="tab2s")
         vs0 = keep.tile([P, J], U8, name="vs0", align_bytes=64)
         vs1 = keep.tile([P, J], U8, name="vs1", align_bytes=64)
@@ -56,8 +68,8 @@ def tile_list_gmu_silu_scat_kernel(
         wtw = keep.tile([P, 2 * N], U8, name="wtw", align_bytes=64)
         rows = keep.tile([P, P], F32, name="rows")
         ident = keep.tile([P, P], F32, name="ident")
-        halves = keep.tile([P, J // P + TILES], F32, name="halves")
-        neg_half_w = keep.tile([P, J // P], F32, name="neg_half_w")
+        halves = keep.tile([P, W_COLS + TILES], F32, name="halves")
+        neg_half_w = keep.tile([P, W_COLS], F32, name="neg_half_w")
         windows = [keep.tile([P, T], F32, name="window0")]
 
         nc.gpsimd.memset(tabs[:].bitcast(I32), 0)
@@ -70,7 +82,6 @@ def tile_list_gmu_silu_scat_kernel(
         make_identity(nc, ident[:])
 
         z_raw = {}
-
         wv_cols = {}
 
         def load_wv(n0, n1):
@@ -79,13 +90,13 @@ def tile_list_gmu_silu_scat_kernel(
             for nt in range(n0 // P, n1 // P):
                 wv_cols[nt] = tile[:, :, P * nt - n0 : P * (nt + 1) - n0]
 
-        def load_z(n0, n1, passes):
-            for a in passes:
+        def load_z(n0, n1):
+            for a in range(Z_PASSES):
                 if n0 == 0:
-                    tile = reuse.tile([P, PACK, P], F32, name=f"z_raw{a}_{n0}", align_bytes=64, offset=RAW_AT + 2048 * a)
+                    tile = reuse.tile([P, PACK, P], F32, name=f"z_raw{a}_{n0}", align_bytes=64, offset=RAW_AT + TILE_BYTES * a)
                 else:
                     tile = keep.tile([P, PACK, n1 - n0], F32, name=f"z_raw{a}_{n0}")
-                src = zv[512 * a : 512 * (a + 1), n0:n1] if a < 2 else zt[:, n0:n1]
+                src = zv[PASS * a : PASS * (a + 1), n0:n1] if a < K // PASS else zt[:, n0:n1]
                 nc.sync.dma_start(out=tile[:], in_=src.rearrange("(p i) n -> p i n", i=PACK))
                 for nt in range(n0 // P, n1 // P):
                     z_raw[(nt, a)] = tile[:, :, P * nt - n0 : P * (nt + 1) - n0]
@@ -93,34 +104,33 @@ def tile_list_gmu_silu_scat_kernel(
         nc.sync.dma_start(list2[:], offs2)
         nc.sync.dma_start(list1[:], offs)
         nc.sync.dma_start(out=tab2w[:].bitcast(I32), in_=tab2_words[0].rearrange("p t i -> p (t i)").bitcast(I32))
-        for q in range(4):
+        for q in range(QUADRANTS):
             nc.sync.dma_start(out=tabs[32 * q : 32 * q + 8, :].bitcast(I32), in_=tab_scales[:, 4 * q : 4 * q + 4, :].bitcast(I32))
         nc.sync.dma_start(out=tabw[:].bitcast(I32), in_=tab_words[0].rearrange("p t i -> p (t i)").bitcast(I32))
         nc.sync.dma_start(out=wtw[:].bitcast(I32), in_=wt_words[0].bitcast(I32))
-        for q in range(4):
+        for q in range(QUADRANTS):
             nc.scalar.dma_start(out=tab2s[32 * q : 32 * q + 4, :].bitcast(I32), in_=tab2_scales[0, 4 * q : 4 * q + 4, :].bitcast(I32))
-        for q in range(4):
+        for q in range(QUADRANTS):
             nc.scalar.dma_start(out=wts[32 * q : 32 * q + 4, :].bitcast(I32), in_=wt_scales[0, 4 * q : 4 * q + 4, :].bitcast(I32))
-        for q in range(4):
+        for q in range(QUADRANTS):
             nc.scalar.dma_start(
                 out=wvs[32 * q : 32 * q + 4, :, :].bitcast(I32),
                 in_=wv_scales[:, 4 * q : 4 * q + 4, :].rearrange("a r n -> r a n").bitcast(I32),
             )
         load_wv(0, P)
-        nc.sync.dma_start(out=rows[0 : J // P, :], in_=wgo[0].rearrange("(r c) -> r c", c=P))
-        nc.sync.dma_start(out=rows[J // P : J // P + TILES, :], in_=b.rearrange("(r c) -> r c", c=P))
+        nc.sync.dma_start(out=rows[0:W_COLS, :], in_=wgo[0].rearrange("(r c) -> r c", c=P))
+        nc.sync.dma_start(out=rows[W_COLS : W_COLS + TILES, :], in_=b.rearrange("(r c) -> r c", c=P))
 
         z_codes = {}
-        z_scales = [keep.tile([P, 3, P], U8, name=f"z_scales{nt}", align_bytes=64) for nt in range(TILES)]
+        z_scales = [keep.tile([P, Z_PASSES, P], U8, name=f"z_scales{nt}", align_bytes=64) for nt in range(TILES)]
         z_bf = {}
-
-        def cast_pass(engine_copy, dst, nt, a):
-            engine_copy(dst.rearrange("p (c u) i -> p c i u", u=2), z_raw[(nt, a)].rearrange("p i (c u) -> p c i u", u=2))
 
         def cast_z(engine_copy, nt, a0, a1, offset):
             tile = reuse.tile([P, a1 - a0, P, PACK], BF16, name=f"z_bf{nt}_{a0}", align_bytes=64, offset=offset)
             for a in range(a0, a1):
-                cast_pass(engine_copy, tile[:, a - a0, :, :], nt, a)
+                engine_copy(
+                    tile[:, a - a0, :, :].rearrange("p (c u) i -> p c i u", u=2), z_raw[(nt, a)].rearrange("p i (c u) -> p c i u", u=2)
+                )
                 z_bf[(nt, a)] = (tile, a - a0)
 
         def quantize_z(nt, a0, a1, offset):
@@ -160,9 +170,9 @@ def tile_list_gmu_silu_scat_kernel(
             nt, h = CHUNKS[c]
             jc = slice(HALF * h, HALF * (h + 1))
             ncols = slice(P * nt, P * (nt + 1))
-            hv = psum.tile([P, BLOCKS, P], F32, name=f"hv{c}", offset=BANK * 0)
-            ht = psum.tile([P, BLOCKS, P], F32, name=f"ht{c}", offset=BANK * (4 if c == 1 else 1))
-            z = psum.tile([P, HALF], F32, name=f"z{c}", offset=BANK * (6 if c == 1 else 2))
+            hv = psum.tile([P, BLOCKS, P], F32, name=f"hv{c}", offset=BANK * HV_BANK)
+            ht = psum.tile([P, BLOCKS, P], F32, name=f"ht{c}", offset=BANK * (BASE_BANKS[0] if c == 1 else HT_BANK))
+            z = psum.tile([P, HALF], F32, name=f"z{c}", offset=BANK * (DIFF_BANKS[0] if c == 1 else Z_BANK))
             for blk in range(BLOCKS):
                 nc.tensor.matmul_mx(
                     out=ht[:, blk, :], lhsT=tw[h][:, P * blk : P * (blk + 1)].bitcast(FP8X4), lhsT_scale=ts[h][:, P * blk : P * (blk + 1)],
@@ -194,33 +204,28 @@ def tile_list_gmu_silu_scat_kernel(
             st = stage[c]
             av = work.tile([P, BLOCKS, P], F32, name="av", bufs=1)
             at = work.tile([P, BLOCKS, P], F32, name="at", bufs=1)
-            wav = reuse.tile([P, BLOCKS, P], F32, name=f"wav{c}", align_bytes=64, offset=WAV_AT + 2048 * c)
+            wav = reuse.tile([P, BLOCKS, P], F32, name=f"wav{c}", align_bytes=64, offset=WAV_AT + TILE_BYTES * c)
             wat = work.tile([P, BLOCKS, P], F32, name="wat")
-            th = reuse.tile([P, HALF], F32, name=f"th{c}", align_bytes=64, offset=TH_AT + 4096 * c + 512)
-
-            def tanh():
-                col = J // P + nt
-                nc.scalar.activation(out=th[:], in_=st["z"][:], func=ACT.Tanh, bias=halves[:, col : col + 1], scale=0.5)
-
+            th = reuse.tile([P, HALF], F32, name=f"th{c}", align_bytes=64, offset=TH_AT + 2 * TILE_BYTES * c + HALF)
             sides = [(st["ht"], at, wat, neg_half_w), (st["hv"], av, wav, halves)]
             if c == 1:
                 sides = sides[::-1]
             for bank, act, weighted, factor in sides:
                 nc.scalar.activation(out=act[:], in_=bank[:], func=ACT.Silu)
                 if c == 0 and act is at:
-                    nc.scalar.activation(out=neg_half_w[:], in_=turned[:, 0, 0 : J // P], func=ACT.Copy, scale=-0.5)
-                    nc.scalar.activation(out=halves[:], in_=turned[:, 0, 0 : J // P + TILES], func=ACT.Copy, scale=0.5)
-            for side, (bank, act, weighted, factor) in enumerate(sides):
+                    nc.scalar.activation(out=neg_half_w[:], in_=turned[:, 0, 0:W_COLS], func=ACT.Copy, scale=-0.5)
+                    nc.scalar.activation(out=halves[:], in_=turned[:, 0, 0 : W_COLS + TILES], func=ACT.Copy, scale=0.5)
+            for bank, act, weighted, factor in sides:
                 for blk in range(BLOCKS):
                     col = BLOCKS * h + blk
                     nc.scalar.activation(out=weighted[:, blk, :], in_=act[:, blk, :], func=ACT.Copy, scale=factor[:, col : col + 1])
-            tanh()
+            nc.scalar.activation(out=th[:], in_=st["z"][:], func=ACT.Tanh, bias=halves[:, W_COLS + nt : W_COLS + nt + 1], scale=0.5)
             st.update({"wav": wav, "wat": wat, "th": th})
 
         def turn(c):
             st = stage[c]
-            base = psum.tile([P, BLOCKS, P], F32, name=f"base{c}", offset=BANK * (4 + c % 2))
-            diff = psum.tile([P, BLOCKS, P], F32, name=f"diff{c}", offset=BANK * (6 + c % 2))
+            base = psum.tile([P, BLOCKS, P], F32, name=f"base{c}", offset=BANK * BASE_BANKS[c % 2])
+            diff = psum.tile([P, BLOCKS, P], F32, name=f"diff{c}", offset=BANK * DIFF_BANKS[c % 2])
             for blk in range(BLOCKS):
                 nc.tensor.transpose(base[:, blk, :], st["wat"][:, blk, :], ident[:])
             for blk in range(BLOCKS):
@@ -250,40 +255,40 @@ def tile_list_gmu_silu_scat_kernel(
         gather_ts(0)
         gather_t(0)
         nc.vector.tensor_copy(vs0[:], tabs[:].indirect(list1[:]))
-        windows.append(reuse.tile([P, T], F32, name="window1", offset=SPARE_AT))
+        windows.append(reuse.tile([P, T], F32, name="window1", offset=TABS_AT))
         nc.gpsimd.memset(windows[1][:], 0.0)
-        load_z(0, P, (0, 1, 2))
-        nc.sync.dma_start(out=vs1[0:112, :].bitcast(I32), in_=vs0[4:116, :].bitcast(I32))
-        load_z(P, 2 * P, (0, 1, 2))
+        load_z(0, P)
+        nc.sync.dma_start(out=vs1[0:PLANE_ROWS, :].bitcast(I32), in_=vs0[4 : 4 + PLANE_ROWS, :].bitcast(I32))
+        load_z(P, 2 * P)
         load_wv(P, N)
-        load_z(2 * P, N, (0, 1, 2))
+        load_z(2 * P, N)
         for h in range(2):
             gather_v(h)
         for h in range(2):
             part_v(h)
-        cast_z(nc.scalar.copy, 0, 0, 3, ROUNDED_AT)
-        turned = psum.tile([P, BLOCKS, P], F32, name="turned", offset=BANK * 5)
+        cast_z(nc.scalar.copy, 0, 0, Z_PASSES, ROUNDED_AT)
+        turned = psum.tile([P, BLOCKS, P], F32, name="turned", offset=BANK * BASE_BANKS[1])
         nc.tensor.transpose(turned[:, 0, :], rows[:], ident[:])
         for a0, a1 in PARTS:
-            quantize_z(0, a0, a1, 40960 + HALF * a0)
-        ts.append(reuse.tile([P, HALF], U8, name="ts1", align_bytes=64, offset=RAW_AT + 2048))
-        tw.append(reuse.tile([P, HALF], U32, name="tw1", align_bytes=64, offset=RAW_AT + 4096))
+            quantize_z(0, a0, a1, CODES_AT + PACK * P * a0)
+        ts.append(reuse.tile([P, HALF], U8, name="ts1", align_bytes=64, offset=RAW_AT + TILE_BYTES))
+        tw.append(reuse.tile([P, HALF], U32, name="tw1", align_bytes=64, offset=RAW_AT + 2 * TILE_BYTES))
         gather_ts(1)
         gather_t(1)
-        cast_z(nc.vector.tensor_copy, 1, 0, 3, ROUNDED_AT + 5 * HALF)
+        cast_z(nc.vector.tensor_copy, 1, 0, Z_PASSES, ROUNDED_AT + ROUNDED_BYTES - HALF)
         products(0)
         activations(0)
         turn(0)
-        last = len(CHUNKS) - 1
         for c in range(len(CHUNKS)):
+            nt, h = CHUNKS[c]
             unload(c)
             gate(c)
-            if c < 6:
-                quantize_z(1 + c // 2, *PARTS[c % 2], WAV_AT + 2048 * c)
-            if c < last:
+            if nt + 1 < TILES:
+                quantize_z(nt + 1, *PARTS[h], WAV_AT + TILE_BYTES * c)
+            if c + 1 < len(CHUNKS):
                 products(c + 1)
                 activations(c + 1)
                 turn(c + 1)
-            if c < 4:
-                cast_z(nc.scalar.copy, 2 + c // 2, *PARTS[c % 2], TH_AT + 4096 * c + 2048)
+            if nt + 2 < TILES:
+                cast_z(nc.scalar.copy, nt + 2, *PARTS[h], TH_AT + 2 * TILE_BYTES * c + TILE_BYTES)
             scatter(c)

@@ -21,27 +21,27 @@ P = 128
 PACK = 4
 PASS = P * PACK
 Z_PASSES = (K + L) // PASS
-QUADRANTS = 4
+QUAD = 32
+ROWS = 4
+SECOND = 16
 HALF = 512
 BLOCKS = HALF // P
 LIST_COLS = HALF // 16
 TILES = N // P
 W_COLS = J // P
 CHUNKS = [(nt, h) for nt in range(TILES) for h in range(J // HALF)]
-PARTS = ((0, 2), (2, 3))
-PLANE_ROWS = 32 * (QUADRANTS - 1) + 4
+PLANE_ROWS = QUAD * 3 + ROWS
 
 TILE_BYTES = 4 * HALF
-ROUNDED_BYTES = 2 * PACK * P * Z_PASSES
 RAW_AT = 0
-TH_AT = 8192
-CODES_AT = 40960
-WAV_AT = 49152
-ROUNDED_AT = 65536
-TABS_AT = 73728
+WAV_AT = 8192
+SLOT = 3 * TILE_BYTES
+ACT_AT = WAV_AT + SLOT * len(CHUNKS)
+TH_AT = ACT_AT + 2 * TILE_BYTES
+TABS_AT = TH_AT + TILE_BYTES
 
 BANK = 2048
-HV_BANK, HT_BANK, Z_BANK = 0, 1, 2
+HV_BANK, HT_BANK, Z_BANK, ROWS_BANK = 0, 1, 2, 3
 BASE_BANKS, DIFF_BANKS = (4, 5), (6, 7)
 
 
@@ -66,20 +66,23 @@ def tile_list_gmu_silu_scat_kernel(
         wvs = keep.tile([P, 2, N], U8, name="wvs", align_bytes=64)
         wts = keep.tile([P, N], U8, name="wts", align_bytes=64)
         wtw = keep.tile([P, 2 * N], U8, name="wtw", align_bytes=64)
-        rows = keep.tile([P, P], F32, name="rows")
+        w_rows = keep.tile([P, P], F32, name="w_rows")
+        b_rows = reuse.tile([P, P], F32, name="b_rows", align_bytes=64, offset=RAW_AT + 3 * TILE_BYTES)
+        half_b = keep.tile([P, TILES], F32, name="half_b")
         ident = keep.tile([P, P], F32, name="ident")
-        halves = keep.tile([P, W_COLS + TILES], F32, name="halves")
+        half_w = keep.tile([P, W_COLS], F32, name="half_w")
         neg_half_w = keep.tile([P, W_COLS], F32, name="neg_half_w")
         windows = [keep.tile([P, T], F32, name="window0")]
 
-        nc.gpsimd.memset(tabs[:].bitcast(I32), 0)
+        nc.vector.memset(tabs[:].bitcast(I32), 0)
         nc.vector.memset(tab2s[:].bitcast(I32), 0)
         nc.vector.memset(wts[:].bitcast(I32), 0)
-        nc.vector.memset(rows[:], 0.0)
         nc.vector.memset(wvs[:].rearrange("p a n -> p (a n)").bitcast(I32), 0)
         nc.vector.memset(vs1[:].bitcast(I32), 0)
         nc.vector.memset(windows[0][:], 0.0)
+        nc.gpsimd.memset(w_rows[:], 0.0)
         make_identity(nc, ident[:])
+        nc.gpsimd.memset(b_rows[:], 0.0)
 
         z_raw = {}
         wv_cols = {}
@@ -90,59 +93,35 @@ def tile_list_gmu_silu_scat_kernel(
             for nt in range(n0 // P, n1 // P):
                 wv_cols[nt] = tile[:, :, P * nt - n0 : P * (nt + 1) - n0]
 
-        def load_z(n0, n1):
-            for a in range(Z_PASSES):
-                if n0 == 0:
-                    tile = reuse.tile([P, PACK, P], F32, name=f"z_raw{a}_{n0}", align_bytes=64, offset=RAW_AT + TILE_BYTES * a)
-                else:
-                    tile = keep.tile([P, PACK, n1 - n0], F32, name=f"z_raw{a}_{n0}")
-                src = zv[PASS * a : PASS * (a + 1), n0:n1] if a < K // PASS else zt[:, n0:n1]
-                nc.sync.dma_start(out=tile[:], in_=src.rearrange("(p i) n -> p i n", i=PACK))
-                for nt in range(n0 // P, n1 // P):
-                    z_raw[(nt, a)] = tile[:, :, P * nt - n0 : P * (nt + 1) - n0]
+        def load_z(n0, n1, a):
+            if n0 == 0:
+                tile = reuse.tile([P, PACK, P], F32, name=f"z_raw{a}_{n0}", align_bytes=64, offset=RAW_AT + TILE_BYTES * a)
+            else:
+                tile = keep.tile([P, PACK, n1 - n0], F32, name=f"z_raw{a}_{n0}")
+            src = zv[PASS * a : PASS * (a + 1), n0:n1] if a < K // PASS else zt[:, n0:n1]
+            nc.sync.dma_start(out=tile[:], in_=src.rearrange("(p i) n -> p i n", i=PACK))
+            for nt in range(n0 // P, n1 // P):
+                z_raw[(nt, a)] = tile[:, :, P * nt - n0 : P * (nt + 1) - n0]
 
-        nc.sync.dma_start(list2[:], offs2)
-        nc.sync.dma_start(list1[:], offs)
-        nc.sync.dma_start(out=tab2w[:].bitcast(I32), in_=tab2_words[0].rearrange("p t i -> p (t i)").bitcast(I32))
-        for q in range(QUADRANTS):
-            nc.sync.dma_start(out=tabs[32 * q : 32 * q + 8, :].bitcast(I32), in_=tab_scales[:, 4 * q : 4 * q + 4, :].bitcast(I32))
-        nc.sync.dma_start(out=tabw[:].bitcast(I32), in_=tab_words[0].rearrange("p t i -> p (t i)").bitcast(I32))
-        nc.sync.dma_start(out=wtw[:].bitcast(I32), in_=wt_words[0].bitcast(I32))
-        for q in range(QUADRANTS):
-            nc.scalar.dma_start(out=tab2s[32 * q : 32 * q + 4, :].bitcast(I32), in_=tab2_scales[0, 4 * q : 4 * q + 4, :].bitcast(I32))
-        for q in range(QUADRANTS):
-            nc.scalar.dma_start(out=wts[32 * q : 32 * q + 4, :].bitcast(I32), in_=wt_scales[0, 4 * q : 4 * q + 4, :].bitcast(I32))
-        for q in range(QUADRANTS):
-            nc.scalar.dma_start(
-                out=wvs[32 * q : 32 * q + 4, :, :].bitcast(I32),
-                in_=wv_scales[:, 4 * q : 4 * q + 4, :].rearrange("a r n -> r a n").bitcast(I32),
-            )
-        load_wv(0, P)
-        nc.sync.dma_start(out=rows[0:W_COLS, :], in_=wgo[0].rearrange("(r c) -> r c", c=P))
-        nc.sync.dma_start(out=rows[W_COLS : W_COLS + TILES, :], in_=b.rearrange("(r c) -> r c", c=P))
+        def load_plane_row(tile, scales, r):
+            nc.sync.dma_start(out=tile[r:P:QUAD].bitcast(I32), in_=scales[r : 4 * ROWS : ROWS].bitcast(I32))
 
         z_codes = {}
         z_scales = [keep.tile([P, Z_PASSES, P], U8, name=f"z_scales{nt}", align_bytes=64) for nt in range(TILES)]
         z_bf = {}
 
-        def cast_z(engine_copy, nt, a0, a1, offset):
-            tile = reuse.tile([P, a1 - a0, P, PACK], BF16, name=f"z_bf{nt}_{a0}", align_bytes=64, offset=offset)
-            for a in range(a0, a1):
-                engine_copy(
-                    tile[:, a - a0, :, :].rearrange("p (c u) i -> p c i u", u=2), z_raw[(nt, a)].rearrange("p i (c u) -> p c i u", u=2)
-                )
-                z_bf[(nt, a)] = (tile, a - a0)
+        def cast_z(engine_copy, nt, a):
+            engine_copy(
+                z_bf[nt][:, a, :, :].rearrange("p (c u) i -> p c i u", u=2), z_raw[(nt, a)].rearrange("p i (c u) -> p c i u", u=2)
+            )
 
-        def quantize_z(nt, a0, a1, offset):
-            codes = reuse.tile([P, a1 - a0, P], U32, name=f"z_codes{nt}_{a0}", align_bytes=64, offset=offset)
-            tile, first = z_bf[(nt, a0)]
+        def quantize_z(nt, codes):
             nc.vector.quantize_mx(
                 out=codes[:].rearrange("p s n -> p (s n)").bitcast(FP8X4),
-                scales=z_scales[nt][:, a0:a1, :].rearrange("p s n -> p (s n)"),
-                in_=tile[:, first : first + a1 - a0, :, :].rearrange("p s n i -> p (s n i)"),
+                scales=z_scales[nt][:].rearrange("p s n -> p (s n)"),
+                in_=z_bf[nt][:].rearrange("p s n i -> p (s n i)"),
             )
-            for a in range(a0, a1):
-                z_codes[(nt, a)] = codes[:, a - a0, :]
+            z_codes[nt] = codes
 
         vw = [keep.tile([P, 2, 2 * HALF], U8, name=f"vw{h}", align_bytes=64) for h in range(2)]
         tw = [keep.tile([P, HALF], U32, name="tw0", align_bytes=64)]
@@ -152,90 +131,104 @@ def tile_list_gmu_silu_scat_kernel(
         def list_half(tile, h):
             return tile[:, LIST_COLS * h : LIST_COLS * (h + 1)]
 
-        def gather_v(h):
-            nc.vector.tensor_copy(pairs[h][:], tabw[:].indirect(list_half(list1, h)))
+        def gather(dst, table, offsets):
+            nc.vector.tensor_copy(dst[:], table[:].indirect(offsets))
 
         def part_v(h):
             nc.vector.tensor_copy(vw[h][:].bitcast(U16), pairs[h][:].bitcast(U16).rearrange("p (j d) -> p d j", d=2))
 
-        def gather_t(h):
-            nc.vector.tensor_copy(tw[h][:], tab2w[:].indirect(list_half(list2, h)))
+        stage = {c: {} for c in range(len(CHUNKS))}
 
-        def gather_ts(h):
-            nc.vector.tensor_copy(ts[h][:], tab2s[:].indirect(list_half(list2, h)))
-
-        stage = {}
-
-        def products(c):
+        def product_ht(c):
             nt, h = CHUNKS[c]
-            jc = slice(HALF * h, HALF * (h + 1))
-            ncols = slice(P * nt, P * (nt + 1))
-            hv = psum.tile([P, BLOCKS, P], F32, name=f"hv{c}", offset=BANK * HV_BANK)
-            ht = psum.tile([P, BLOCKS, P], F32, name=f"ht{c}", offset=BANK * (BASE_BANKS[0] if c == 1 else HT_BANK))
-            z = psum.tile([P, HALF], F32, name=f"z{c}", offset=BANK * (DIFF_BANKS[0] if c == 1 else Z_BANK))
+            ht = psum.tile([P, BLOCKS, P], F32, name=f"ht{c}", offset=BANK * (Z_BANK if c == 1 else HT_BANK if c in (0, 4, 6) else ROWS_BANK))
             for blk in range(BLOCKS):
                 nc.tensor.matmul_mx(
                     out=ht[:, blk, :], lhsT=tw[h][:, P * blk : P * (blk + 1)].bitcast(FP8X4), lhsT_scale=ts[h][:, P * blk : P * (blk + 1)],
-                    rhs=wtw[:, 2 * P * nt : 2 * P * (nt + 1)].bitcast(FP4X4), rhs_scale=wts[:, ncols], start=True, stop=True,
+                    rhs=wtw[:, 2 * P * nt : 2 * P * (nt + 1)].bitcast(FP4X4), rhs_scale=wts[:, P * nt : P * (nt + 1)], start=True, stop=True,
                 )
+            stage[c]["ht"] = ht
+
+        def product_hv(c):
+            nt, h = CHUNKS[c]
+            hv = psum.tile([P, BLOCKS, P], F32, name=f"hv{c}", offset=BANK * (BASE_BANKS[0] if c == 1 else HV_BANK))
             for a, plane in enumerate((vs0, vs1)):
                 for blk in range(BLOCKS):
                     j0 = HALF * h + P * blk
                     nc.tensor.matmul_mx(
                         out=hv[:, blk, :], lhsT=vw[h][:, a, 2 * P * blk : 2 * P * (blk + 1)].bitcast(FP4X4), lhsT_scale=plane[:, j0 : j0 + P],
-                        rhs=wv_cols[nt][:, a, :].bitcast(FP8X4), rhs_scale=wvs[:, a, ncols],
+                        rhs=wv_cols[nt][:, a, :].bitcast(FP8X4), rhs_scale=wvs[:, a, P * nt : P * (nt + 1)],
                         start=(a == 0 and blk == 0), stop=(a == 1 and blk == BLOCKS - 1),
                     )
+            stage[c]["hv"] = hv
+
+        def product_z(c):
+            nt, h = CHUNKS[c]
+            jc = slice(HALF * h, HALF * (h + 1))
+            z = psum.tile([P, HALF], F32, name=f"z{c}", offset=BANK * (DIFF_BANKS[0] if c == 1 else Z_BANK))
             moving = [
                 (vw[h][:, 0, :].bitcast(FP4X4), vs0[:, jc]),
                 (vw[h][:, 1, :].bitcast(FP4X4), vs1[:, jc]),
                 (tw[h][:].bitcast(FP8X4), ts[h][:]),
             ]
-            for a in (0, 2, 1):
-                codes, scales = moving[a]
+            for a, (codes, scales) in enumerate(moving):
                 nc.tensor.matmul_mx(
-                    out=z[:], lhsT=z_codes[(nt, a)].bitcast(FP8X4), lhsT_scale=z_scales[nt][:, a, :],
-                    rhs=codes, rhs_scale=scales, start=(a == 0), stop=(a == 1),
+                    out=z[:], lhsT=z_codes[nt][:, a, :].bitcast(FP8X4), lhsT_scale=z_scales[nt][:, a, :],
+                    rhs=codes, rhs_scale=scales, start=(a == 0), stop=(a == Z_PASSES - 1),
                 )
-            stage[c] = {"hv": hv, "ht": ht, "z": z}
+            stage[c]["z"] = z
 
-        def activations(c):
-            nt, h = CHUNKS[c]
-            st = stage[c]
-            av = work.tile([P, BLOCKS, P], F32, name="av", bufs=1)
-            at = work.tile([P, BLOCKS, P], F32, name="at", bufs=1)
-            wav = reuse.tile([P, BLOCKS, P], F32, name=f"wav{c}", align_bytes=64, offset=WAV_AT + TILE_BYTES * c)
-            wat = work.tile([P, BLOCKS, P], F32, name="wat")
-            th = reuse.tile([P, HALF], F32, name=f"th{c}", align_bytes=64, offset=TH_AT + 2 * TILE_BYTES * c + HALF)
-            sides = [(st["ht"], at, wat, neg_half_w), (st["hv"], av, wav, halves)]
-            if c == 1:
-                sides = sides[::-1]
-            for bank, act, weighted, factor in sides:
-                nc.scalar.activation(out=act[:], in_=bank[:], func=ACT.Silu)
-                if c == 0 and act is at:
-                    nc.scalar.activation(out=neg_half_w[:], in_=turned[:, 0, 0:W_COLS], func=ACT.Copy, scale=-0.5)
-                    nc.scalar.activation(out=halves[:], in_=turned[:, 0, 0 : W_COLS + TILES], func=ACT.Copy, scale=0.5)
-            for bank, act, weighted, factor in sides:
-                for blk in range(BLOCKS):
-                    col = BLOCKS * h + blk
-                    nc.scalar.activation(out=weighted[:, blk, :], in_=act[:, blk, :], func=ACT.Copy, scale=factor[:, col : col + 1])
-            nc.scalar.activation(out=th[:], in_=st["z"][:], func=ACT.Tanh, bias=halves[:, W_COLS + nt : W_COLS + nt + 1], scale=0.5)
-            st.update({"wav": wav, "wat": wat, "th": th})
+        def silu(c, side):
+            act = reuse.tile([P, BLOCKS, P], F32, name=f"a{side}{c}", offset=TH_AT if (c, side) == (1, "v") else ACT_AT + TILE_BYTES * (side == "t"))
+            nc.scalar.activation(out=act[:], in_=stage[c]["h" + side][:], func=ACT.Silu)
+            stage[c]["a" + side] = act
 
-        def turn(c):
+        def weigh(c, side):
+            h = CHUNKS[c][1]
+            if side == "v":
+                weighted = reuse.tile([P, BLOCKS, P], F32, name=f"wav{c}", align_bytes=64, offset=WAV_AT + SLOT * c + TILE_BYTES)
+                factor = half_w
+            else:
+                weighted = work.tile([P, BLOCKS, P], F32, name="wat")
+                factor = neg_half_w
+            for blk in range(BLOCKS):
+                col = BLOCKS * h + blk
+                nc.scalar.activation(out=weighted[:, blk, :], in_=stage[c]["a" + side][:, blk, :], func=ACT.Copy, scale=factor[:, col : col + 1])
+            stage[c]["wa" + side] = weighted
+
+        def tanh(c):
+            nt = CHUNKS[c][0]
+            if c == 0:
+                th = reuse.tile([P, HALF], F32, name="th0", offset=TH_AT)
+            else:
+                th = work.tile([P, HALF], F32, name="th")
+            nc.scalar.activation(out=th[:], in_=stage[c]["z"][:], func=ACT.Tanh, bias=half_b[:, nt : nt + 1], scale=0.5)
+            stage[c]["th"] = th
+
+        def turn_base(c):
             st = stage[c]
-            base = psum.tile([P, BLOCKS, P], F32, name=f"base{c}", offset=BANK * BASE_BANKS[c % 2])
-            diff = psum.tile([P, BLOCKS, P], F32, name=f"diff{c}", offset=BANK * DIFF_BANKS[c % 2])
+            st["base"] = psum.tile([P, BLOCKS, P], F32, name=f"base{c}", offset=BANK * (HV_BANK if c == 0 else BASE_BANKS[c % 2]))
             for blk in range(BLOCKS):
-                nc.tensor.transpose(base[:, blk, :], st["wat"][:, blk, :], ident[:])
+                nc.tensor.transpose(st["base"][:, blk, :], st["wat"][:, blk, :], ident[:])
+
+        def turn_t(c):
+            st = stage[c]
+            st["diff"] = psum.tile([P, BLOCKS, P], F32, name=f"diff{c}", offset=BANK * DIFF_BANKS[c % 2])
             for blk in range(BLOCKS):
-                nc.tensor.matmul(diff[:, blk, :], st["wat"][:, blk, :], ident[:], start=True, stop=False, is_transpose=True)
-                nc.tensor.matmul(diff[:, blk, :], st["wav"][:, blk, :], ident[:], start=False, stop=True, is_transpose=True)
-            st.update({"base": base, "diff": diff})
+                nc.tensor.matmul(st["diff"][:, blk, :], st["wat"][:, blk, :], ident[:], start=(blk == 0), stop=False, is_transpose=True)
+
+        def turn_v(c):
+            st = stage[c]
+            order = list(range(BLOCKS))[::-1] if c == 0 else list(range(BLOCKS))
+            for blk in order:
+                nc.tensor.matmul(st["diff"][:, blk, :], st["wav"][:, blk, :], ident[:], start=False, stop=(blk == order[-1]), is_transpose=True)
 
         def unload(c):
             st = stage[c]
-            base_sb = work.tile([P, HALF], F32, name="base_sb")
+            if c == 0:
+                base_sb = reuse.tile([P, HALF], F32, name="base_sb0", offset=WAV_AT + 3 * TILE_BYTES // 2)
+            else:
+                base_sb = work.tile([P, HALF], F32, name="base_sb")
             nc.scalar.activation(out=base_sb[:], in_=st["base"][:].rearrange("p b j -> p (b j)"), func=ACT.Copy, scale=-2.0)
             st["base_sb"] = base_sb
 
@@ -252,43 +245,97 @@ def tile_list_gmu_silu_scat_kernel(
             if h == 1:
                 nc.sync.dma_start(out=out[P * nt : P * (nt + 1), :], in_=window[:])
 
-        gather_ts(0)
-        gather_t(0)
-        nc.vector.tensor_copy(vs0[:], tabs[:].indirect(list1[:]))
+        nc.sync.dma_start(list1[:], offs)
+        tab_rows = tab_scales.rearrange("a (q r) t -> r q a t", r=ROWS)
+        for r in range(ROWS):
+            nc.sync.dma_start(out=tabs[r:P:SECOND, :].bitcast(I32), in_=tab_rows[r].bitcast(I32))
+        nc.sync.dma_start(list2[:], offs2)
+        nc.sync.dma_start(out=w_rows[0:W_COLS, :], in_=wgo[0].rearrange("(r c) -> r c", c=P))
+        nc.sync.dma_start(out=tab2w[:].bitcast(I32), in_=tab2_words[0].rearrange("p t i -> p (t i)").bitcast(I32))
+        for r in range(ROWS):
+            load_plane_row(tab2s, tab2_scales[0], r)
+        nc.sync.dma_start(out=wtw[:].bitcast(I32), in_=wt_words[0].bitcast(I32))
+        nc.sync.dma_start(out=tabw[:].bitcast(I32), in_=tab_words[0].rearrange("p t i -> p (t i)").bitcast(I32))
+        gather(vs0, tabs, list1[:])
         windows.append(reuse.tile([P, T], F32, name="window1", offset=TABS_AT))
         nc.gpsimd.memset(windows[1][:], 0.0)
-        load_z(0, P)
-        nc.sync.dma_start(out=vs1[0:PLANE_ROWS, :].bitcast(I32), in_=vs0[4 : 4 + PLANE_ROWS, :].bitcast(I32))
-        load_z(P, 2 * P)
+        for r in range(ROWS):
+            load_plane_row(wts, wt_scales[0], r)
+        load_z(0, P, 0)
+        nc.sync.dma_start(out=vs1[0:PLANE_ROWS, :].bitcast(I32), in_=vs0[SECOND : SECOND + PLANE_ROWS, :].bitcast(I32))
+        load_z(0, P, 1)
+        load_wv(0, P)
+        for r in range(ROWS):
+            load_plane_row(wvs, wv_scales.rearrange("a r n -> r a n"), r)
+        load_z(0, P, 2)
+        nc.sync.dma_start(out=b_rows[0:TILES, :], in_=b.rearrange("(r c) -> r c", c=P))
+        for a in range(Z_PASSES):
+            load_z(P, 2 * P, a)
         load_wv(P, N)
-        load_z(2 * P, N)
+        for a in range(Z_PASSES):
+            load_z(2 * P, N, a)
+
+        w_turned = psum.tile([P, P], F32, name="w_turned", offset=BANK * ROWS_BANK)
+        nc.tensor.transpose(w_turned[:], w_rows[:], ident[:])
+        nc.vector.tensor_scalar_mul(neg_half_w[:], w_turned[:, 0:W_COLS], -0.5)
+        nc.vector.tensor_scalar_mul(half_w[:], w_turned[:, 0:W_COLS], 0.5)
+        gather(tw[0], tab2w, list_half(list2, 0))
+        gather(ts[0], tab2s, list_half(list2, 0))
         for h in range(2):
-            gather_v(h)
+            gather(pairs[h], tabw, list_half(list1, h))
         for h in range(2):
             part_v(h)
-        cast_z(nc.scalar.copy, 0, 0, Z_PASSES, ROUNDED_AT)
-        turned = psum.tile([P, BLOCKS, P], F32, name="turned", offset=BANK * BASE_BANKS[1])
-        nc.tensor.transpose(turned[:, 0, :], rows[:], ident[:])
-        for a0, a1 in PARTS:
-            quantize_z(0, a0, a1, CODES_AT + PACK * P * a0)
-        ts.append(reuse.tile([P, HALF], U8, name="ts1", align_bytes=64, offset=RAW_AT + TILE_BYTES))
-        tw.append(reuse.tile([P, HALF], U32, name="tw1", align_bytes=64, offset=RAW_AT + 2 * TILE_BYTES))
-        gather_ts(1)
-        gather_t(1)
-        cast_z(nc.vector.tensor_copy, 1, 0, Z_PASSES, ROUNDED_AT + ROUNDED_BYTES - HALF)
-        products(0)
-        activations(0)
-        turn(0)
+
+        product_ht(0)
+        silu(0, "t")
+        weigh(0, "t")
+        turn_t(0)
+        z_bf[0] = keep.tile([P, Z_PASSES, P, PACK], BF16, name="z_bf0", align_bytes=64)
+        for a in range(Z_PASSES):
+            cast_z(nc.scalar.copy, 0, a)
+        tw.append(reuse.tile([P, HALF], U32, name="tw1", align_bytes=64, offset=RAW_AT))
+        gather(tw[1], tab2w, list_half(list2, 1))
+        quantize_z(0, keep.tile([P, Z_PASSES, P], U32, name="z_codes0", align_bytes=64))
+        product_hv(0)
+        silu(0, "v")
+        weigh(0, "v")
+        product_z(0)
+        turn_v(0)
+        b_turned = psum.tile([P, P], F32, name="b_turned", offset=BANK * BASE_BANKS[1])
+        nc.tensor.transpose(b_turned[:], b_rows[:], ident[:])
+        ts.append(reuse.tile([P, HALF], U8, name="ts1", align_bytes=64, offset=RAW_AT + 3 * TILE_BYTES))
+        gather(ts[1], tab2s, list_half(list2, 1))
+        nc.scalar.activation(out=half_b[:], in_=b_turned[:, 0:TILES], func=ACT.Copy, scale=0.5)
+        tanh(0)
+        turn_base(0)
+        unload(0)
+
         for c in range(len(CHUNKS)):
             nt, h = CHUNKS[c]
-            unload(c)
+            slot = WAV_AT + SLOT * c
             gate(c)
             if nt + 1 < TILES:
-                quantize_z(nt + 1, *PARTS[h], WAV_AT + TILE_BYTES * c)
-            if c + 1 < len(CHUNKS):
-                products(c + 1)
-                activations(c + 1)
-                turn(c + 1)
-            if nt + 2 < TILES:
-                cast_z(nc.scalar.copy, nt + 2, *PARTS[h], TH_AT + 2 * TILE_BYTES * c + TILE_BYTES)
+                if h == 0:
+                    z_bf[nt + 1] = reuse.tile([P, Z_PASSES, P, PACK], BF16, name=f"z_bf{nt + 1}", align_bytes=64, offset=slot)
+                    cast_z(nc.vector.tensor_copy, nt + 1, 0)
+                else:
+                    quantize_z(nt + 1, reuse.tile([P, Z_PASSES, P], U32, name=f"z_codes{nt + 1}", align_bytes=64, offset=slot + TILE_BYTES))
             scatter(c)
+            n = c + 1
+            if n < len(CHUNKS):
+                sides = "vt" if n == 1 else "tv"
+                for side in sides:
+                    (product_hv if side == "v" else product_ht)(n)
+                product_z(n)
+                for side in sides:
+                    silu(n, side)
+                for side in sides:
+                    weigh(n, side)
+                turn_base(n)
+                turn_t(n)
+                turn_v(n)
+                tanh(n)
+                unload(n)
+                if h == 0 and nt + 1 < TILES:
+                    for a in range(1, Z_PASSES):
+                        cast_z(nc.scalar.copy, nt + 1, a)

@@ -246,15 +246,16 @@ def tile_list_gmu_silu_scat_kernel(
                 nc.sync.dma_start(out=out[P * nt : P * (nt + 1), :], in_=window[:])
 
         nc.sync.dma_start(list1[:], offs)
+        nc.sync.dma_start(out=wtw[:].bitcast(I32), in_=wt_words[0].bitcast(I32))
+        load_wv(0, P)
         tab_rows = tab_scales.rearrange("a (q r) t -> r q a t", r=ROWS)
         for r in range(ROWS):
             nc.sync.dma_start(out=tabs[r:P:SECOND, :].bitcast(I32), in_=tab_rows[r].bitcast(I32))
-        nc.sync.dma_start(list2[:], offs2)
-        nc.sync.dma_start(out=w_rows[0:W_COLS, :], in_=wgo[0].rearrange("(r c) -> r c", c=P))
         nc.sync.dma_start(out=tab2w[:].bitcast(I32), in_=tab2_words[0].rearrange("p t i -> p (t i)").bitcast(I32))
+        nc.sync.dma_start(list2[:], offs2)
         for r in range(ROWS):
             load_plane_row(tab2s, tab2_scales[0], r)
-        nc.sync.dma_start(out=wtw[:].bitcast(I32), in_=wt_words[0].bitcast(I32))
+        nc.sync.dma_start(out=w_rows[0:W_COLS, :], in_=wgo[0].rearrange("(r c) -> r c", c=P))
         nc.sync.dma_start(out=tabw[:].bitcast(I32), in_=tab_words[0].rearrange("p t i -> p (t i)").bitcast(I32))
         gather(vs0, tabs, list1[:])
         windows.append(reuse.tile([P, T], F32, name="window1", offset=TABS_AT))
@@ -264,7 +265,6 @@ def tile_list_gmu_silu_scat_kernel(
         load_z(0, P, 0)
         nc.sync.dma_start(out=vs1[0:PLANE_ROWS, :].bitcast(I32), in_=vs0[SECOND : SECOND + PLANE_ROWS, :].bitcast(I32))
         load_z(0, P, 1)
-        load_wv(0, P)
         for r in range(ROWS):
             load_plane_row(wvs, wv_scales.rearrange("a r n -> r a n"), r)
         load_z(0, P, 2)

@@ -34,15 +34,17 @@ PLANE_ROWS = QUAD * 3 + ROWS
 
 TILE_BYTES = 4 * HALF
 RAW_AT = 0
-WAV_AT = 8192
+LAST_RAW_AT = RAW_AT + 4096
+WAV_AT = 12288
 SLOT = 3 * TILE_BYTES
 ACT_AT = WAV_AT + SLOT * len(CHUNKS)
-TH_AT = ACT_AT + 2 * TILE_BYTES
-TABS_AT = TH_AT + TILE_BYTES
+W_ROWS_AT = ACT_AT + 3 * TILE_BYTES
+TABS_AT = W_ROWS_AT + 2 * TILE_BYTES
 
 BANK = 2048
-HV_BANK, HT_BANK, Z_BANK, ROWS_BANK = 0, 1, 2, 3
-BASE_BANKS, DIFF_BANKS = (4, 5), (6, 7)
+HV_BANK, Z_BANK, BASE_BANK = 0, 2, 4
+HT_BANKS = (1, HV_BANK, 3, 3, 5, 3, 1, 5)
+DIFF_BANKS = (6, 7)
 
 
 def tile_list_gmu_silu_scat_kernel(
@@ -66,8 +68,8 @@ def tile_list_gmu_silu_scat_kernel(
         wvs = keep.tile([P, 2, N], U8, name="wvs", align_bytes=64)
         wts = keep.tile([P, N], U8, name="wts", align_bytes=64)
         wtw = keep.tile([P, 2 * N], U8, name="wtw", align_bytes=64)
-        w_rows = keep.tile([P, P], F32, name="w_rows")
-        b_rows = reuse.tile([P, P], F32, name="b_rows", align_bytes=64, offset=RAW_AT + 3 * TILE_BYTES)
+        w_rows = reuse.tile([P, P], F32, name="w_rows", align_bytes=64, offset=W_ROWS_AT)
+        b_rows = reuse.tile([P, P], F32, name="b_rows", align_bytes=64, offset=WAV_AT)
         half_b = keep.tile([P, TILES], F32, name="half_b")
         ident = keep.tile([P, P], F32, name="ident")
         half_w = keep.tile([P, W_COLS], F32, name="half_w")
@@ -115,33 +117,33 @@ def tile_list_gmu_silu_scat_kernel(
                 z_bf[nt][:, a, :, :].rearrange("p (c u) i -> p c i u", u=2), z_raw[(nt, a)].rearrange("p i (c u) -> p c i u", u=2)
             )
 
-        def quantize_z(nt, codes):
+        def quantize_z(nt, codes, a0=0, a1=Z_PASSES):
             nc.vector.quantize_mx(
-                out=codes[:].rearrange("p s n -> p (s n)").bitcast(FP8X4),
-                scales=z_scales[nt][:].rearrange("p s n -> p (s n)"),
-                in_=z_bf[nt][:].rearrange("p s n i -> p (s n i)"),
+                out=codes[:, a0:a1, :].rearrange("p s n -> p (s n)").bitcast(FP8X4),
+                scales=z_scales[nt][:, a0:a1, :].rearrange("p s n -> p (s n)"),
+                in_=z_bf[nt][:, a0:a1, :, :].rearrange("p s n i -> p (s n i)"),
             )
             z_codes[nt] = codes
 
-        vw = [keep.tile([P, 2, 2 * HALF], U8, name=f"vw{h}", align_bytes=64) for h in range(2)]
+        vw = [keep.tile([P, 2, 2 * HALF], U8, name="vw0", align_bytes=64)]
         tw = [keep.tile([P, HALF], U32, name="tw0", align_bytes=64)]
         ts = [keep.tile([P, HALF], U8, name="ts0", align_bytes=64)]
-        pairs = [keep.tile([P, HALF], U32, name=f"pairs{h}", align_bytes=64) for h in range(2)]
+        pairs = [keep.tile([P, HALF], U32, name="pairs0", align_bytes=64)]
 
         def list_half(tile, h):
             return tile[:, LIST_COLS * h : LIST_COLS * (h + 1)]
 
         def gather(dst, table, offsets):
-            nc.vector.tensor_copy(dst[:], table[:].indirect(offsets))
+            nc.vector.tensor_copy(dst, table[:].indirect(offsets))
 
-        def part_v(h):
-            nc.vector.tensor_copy(vw[h][:].bitcast(U16), pairs[h][:].bitcast(U16).rearrange("p (j d) -> p d j", d=2))
+        def part_v(h, j0, j1):
+            nc.vector.tensor_copy(vw[h][:].bitcast(U16)[:, :, j0:j1], pairs[h][:, j0:j1].bitcast(U16).rearrange("p (j d) -> p d j", d=2))
 
         stage = {c: {} for c in range(len(CHUNKS))}
 
         def product_ht(c):
             nt, h = CHUNKS[c]
-            ht = psum.tile([P, BLOCKS, P], F32, name=f"ht{c}", offset=BANK * (Z_BANK if c == 1 else HT_BANK if c in (0, 4, 6) else ROWS_BANK))
+            ht = psum.tile([P, BLOCKS, P], F32, name=f"ht{c}", offset=BANK * HT_BANKS[c])
             for blk in range(BLOCKS):
                 nc.tensor.matmul_mx(
                     out=ht[:, blk, :], lhsT=tw[h][:, P * blk : P * (blk + 1)].bitcast(FP8X4), lhsT_scale=ts[h][:, P * blk : P * (blk + 1)],
@@ -151,7 +153,7 @@ def tile_list_gmu_silu_scat_kernel(
 
         def product_hv(c):
             nt, h = CHUNKS[c]
-            hv = psum.tile([P, BLOCKS, P], F32, name=f"hv{c}", offset=BANK * (BASE_BANKS[0] if c == 1 else HV_BANK))
+            hv = psum.tile([P, BLOCKS, P], F32, name=f"hv{c}", offset=BANK * (Z_BANK if c == 1 else HV_BANK))
             for a, plane in enumerate((vs0, vs1)):
                 for blk in range(BLOCKS):
                     j0 = HALF * h + P * blk
@@ -165,7 +167,7 @@ def tile_list_gmu_silu_scat_kernel(
         def product_z(c):
             nt, h = CHUNKS[c]
             jc = slice(HALF * h, HALF * (h + 1))
-            z = psum.tile([P, HALF], F32, name=f"z{c}", offset=BANK * (DIFF_BANKS[0] if c == 1 else Z_BANK))
+            z = psum.tile([P, HALF], F32, name=f"z{c}", offset=BANK * (HV_BANK if c == 0 else DIFF_BANKS[0] if c == 1 else Z_BANK))
             moving = [
                 (vw[h][:, 0, :].bitcast(FP4X4), vs0[:, jc]),
                 (vw[h][:, 1, :].bitcast(FP4X4), vs1[:, jc]),
@@ -179,14 +181,14 @@ def tile_list_gmu_silu_scat_kernel(
             stage[c]["z"] = z
 
         def silu(c, side):
-            act = reuse.tile([P, BLOCKS, P], F32, name=f"a{side}{c}", offset=TH_AT if (c, side) == (1, "v") else ACT_AT + TILE_BYTES * (side == "t"))
+            act = reuse.tile([P, BLOCKS, P], F32, name=f"a{side}{c}", offset=ACT_AT + TILE_BYTES * (side == "t"))
             nc.scalar.activation(out=act[:], in_=stage[c]["h" + side][:], func=ACT.Silu)
             stage[c]["a" + side] = act
 
         def weigh(c, side):
             h = CHUNKS[c][1]
             if side == "v":
-                weighted = reuse.tile([P, BLOCKS, P], F32, name=f"wav{c}", align_bytes=64, offset=WAV_AT + SLOT * c + TILE_BYTES)
+                weighted = reuse.tile([P, BLOCKS, P], F32, name=f"wav{c}", align_bytes=64, offset=LAST_RAW_AT + 1024 if c == 0 else WAV_AT + SLOT * c + TILE_BYTES)
                 factor = half_w
             else:
                 weighted = work.tile([P, BLOCKS, P], F32, name="wat")
@@ -198,16 +200,13 @@ def tile_list_gmu_silu_scat_kernel(
 
         def tanh(c):
             nt = CHUNKS[c][0]
-            if c == 0:
-                th = reuse.tile([P, HALF], F32, name="th0", offset=TH_AT)
-            else:
-                th = work.tile([P, HALF], F32, name="th")
+            th = work.tile([P, HALF], F32, name="th")
             nc.scalar.activation(out=th[:], in_=stage[c]["z"][:], func=ACT.Tanh, bias=half_b[:, nt : nt + 1], scale=0.5)
             stage[c]["th"] = th
 
         def turn_base(c):
             st = stage[c]
-            st["base"] = psum.tile([P, BLOCKS, P], F32, name=f"base{c}", offset=BANK * (HV_BANK if c == 0 else BASE_BANKS[c % 2]))
+            st["base"] = psum.tile([P, BLOCKS, P], F32, name=f"base{c}", offset=BANK * BASE_BANK)
             for blk in range(BLOCKS):
                 nc.tensor.transpose(st["base"][:, blk, :], st["wat"][:, blk, :], ident[:])
 
@@ -219,16 +218,21 @@ def tile_list_gmu_silu_scat_kernel(
 
         def turn_v(c):
             st = stage[c]
+            for blk in range(BLOCKS):
+                nc.tensor.matmul(st["diff"][:, blk, :], st["wav"][:, blk, :], ident[:], start=False, stop=(blk == BLOCKS - 1), is_transpose=True)
+
+        def turn_v_first(c):
+            st = stage[c]
+            st["diff"] = psum.tile([P, BLOCKS, P], F32, name=f"diff{c}", offset=BANK * DIFF_BANKS[c % 2])
             order = list(range(BLOCKS))[::-1] if c == 0 else list(range(BLOCKS))
-            for blk in order:
-                nc.tensor.matmul(st["diff"][:, blk, :], st["wav"][:, blk, :], ident[:], start=False, stop=(blk == order[-1]), is_transpose=True)
+            for side in "vt":
+                for blk in order:
+                    first, final = (side, blk) == ("v", order[0]), (side, blk) == ("t", order[-1])
+                    nc.tensor.matmul(st["diff"][:, blk, :], st["wa" + side][:, blk, :], ident[:], start=first, stop=final, is_transpose=True)
 
         def unload(c):
             st = stage[c]
-            if c == 0:
-                base_sb = reuse.tile([P, HALF], F32, name="base_sb0", offset=WAV_AT + 3 * TILE_BYTES // 2)
-            else:
-                base_sb = work.tile([P, HALF], F32, name="base_sb")
+            base_sb = work.tile([P, HALF], F32, name="base_sb")
             nc.scalar.activation(out=base_sb[:], in_=st["base"][:].rearrange("p b j -> p (b j)"), func=ACT.Copy, scale=-2.0)
             st["base_sb"] = base_sb
 
@@ -255,56 +259,63 @@ def tile_list_gmu_silu_scat_kernel(
         nc.sync.dma_start(list2[:], offs2)
         for r in range(ROWS):
             load_plane_row(tab2s, tab2_scales[0], r)
-        nc.sync.dma_start(out=w_rows[0:W_COLS, :], in_=wgo[0].rearrange("(r c) -> r c", c=P))
+        load_plane_row(wts, wt_scales[0], 0)
         nc.sync.dma_start(out=tabw[:].bitcast(I32), in_=tab_words[0].rearrange("p t i -> p (t i)").bitcast(I32))
-        gather(vs0, tabs, list1[:])
+        nc.sync.dma_start(out=w_rows[0:W_COLS, :], in_=wgo[0].rearrange("(r c) -> r c", c=P))
+        gather(vs0[:], tabs, list1[:])
         windows.append(reuse.tile([P, T], F32, name="window1", offset=TABS_AT))
         nc.gpsimd.memset(windows[1][:], 0.0)
-        for r in range(ROWS):
+        for r in range(1, ROWS):
             load_plane_row(wts, wt_scales[0], r)
         load_z(0, P, 0)
-        nc.sync.dma_start(out=vs1[0:PLANE_ROWS, :].bitcast(I32), in_=vs0[SECOND : SECOND + PLANE_ROWS, :].bitcast(I32))
         load_z(0, P, 1)
+        nc.sync.dma_start(out=vs1[0:PLANE_ROWS, :].bitcast(I32), in_=vs0[SECOND : SECOND + PLANE_ROWS, :].bitcast(I32))
         for r in range(ROWS):
             load_plane_row(wvs, wv_scales.rearrange("a r n -> r a n"), r)
-        load_z(0, P, 2)
         nc.sync.dma_start(out=b_rows[0:TILES, :], in_=b.rearrange("(r c) -> r c", c=P))
+        load_z(0, P, 2)
         for a in range(Z_PASSES):
             load_z(P, 2 * P, a)
         load_wv(P, N)
         for a in range(Z_PASSES):
             load_z(2 * P, N, a)
 
-        w_turned = psum.tile([P, P], F32, name="w_turned", offset=BANK * ROWS_BANK)
+        gather(tw[0][:], tab2w, list_half(list2, 0))
+        gather(ts[0][:], tab2s, list_half(list2, 0))
+        quarter = HALF // 2
+        for u in range(2):
+            gather(pairs[0][:, quarter * u : quarter * (u + 1)], tabw, list1[:, quarter // 16 * u : quarter // 16 * (u + 1)])
+        for u in range(2):
+            part_v(0, quarter * u, quarter * (u + 1))
+        w_turned = psum.tile([P, P], F32, name="w_turned", offset=BANK * BASE_BANK)
         nc.tensor.transpose(w_turned[:], w_rows[:], ident[:])
         nc.vector.tensor_scalar_mul(neg_half_w[:], w_turned[:, 0:W_COLS], -0.5)
         nc.vector.tensor_scalar_mul(half_w[:], w_turned[:, 0:W_COLS], 0.5)
-        gather(tw[0], tab2w, list_half(list2, 0))
-        gather(ts[0], tab2s, list_half(list2, 0))
-        for h in range(2):
-            gather(pairs[h], tabw, list_half(list1, h))
-        for h in range(2):
-            part_v(h)
+        pairs.append(reuse.tile([P, HALF], U32, name="pairs1", align_bytes=64, offset=W_ROWS_AT + 256 - TILE_BYTES))
+        gather(pairs[1][:], tabw, list_half(list1, 1))
+        tw.append(reuse.tile([P, HALF], U32, name="tw1", align_bytes=64, offset=W_ROWS_AT + 256))
+        gather(tw[1][:], tab2w, list_half(list2, 1))
 
         product_ht(0)
         silu(0, "t")
         weigh(0, "t")
-        turn_t(0)
         z_bf[0] = keep.tile([P, Z_PASSES, P, PACK], BF16, name="z_bf0", align_bytes=64)
         for a in range(Z_PASSES):
             cast_z(nc.scalar.copy, 0, a)
-        tw.append(reuse.tile([P, HALF], U32, name="tw1", align_bytes=64, offset=RAW_AT))
-        gather(tw[1], tab2w, list_half(list2, 1))
-        quantize_z(0, keep.tile([P, Z_PASSES, P], U32, name="z_codes0", align_bytes=64))
+        first_codes = keep.tile([P, Z_PASSES, P], U32, name="z_codes0", align_bytes=64)
+        quantize_z(0, first_codes, 0, Z_PASSES - 1)
+        quantize_z(0, first_codes, Z_PASSES - 1, Z_PASSES)
+        vw.append(reuse.tile([P, 2, 2 * HALF], U8, name="vw1", align_bytes=64, offset=LAST_RAW_AT + 512 - TILE_BYTES))
+        part_v(1, 0, HALF)
         product_hv(0)
         silu(0, "v")
         weigh(0, "v")
         product_z(0)
-        turn_v(0)
-        b_turned = psum.tile([P, P], F32, name="b_turned", offset=BANK * BASE_BANKS[1])
+        turn_v_first(0)
+        b_turned = psum.tile([P, P], F32, name="b_turned", offset=BANK * BASE_BANK)
         nc.tensor.transpose(b_turned[:], b_rows[:], ident[:])
-        ts.append(reuse.tile([P, HALF], U8, name="ts1", align_bytes=64, offset=RAW_AT + 3 * TILE_BYTES))
-        gather(ts[1], tab2s, list_half(list2, 1))
+        ts.append(reuse.tile([P, HALF], U8, name="ts1", align_bytes=64, offset=LAST_RAW_AT + 512))
+        gather(ts[1][:], tab2s, list_half(list2, 1))
         nc.scalar.activation(out=half_b[:], in_=b_turned[:, 0:TILES], func=ACT.Copy, scale=0.5)
         tanh(0)
         turn_base(0)
@@ -316,7 +327,7 @@ def tile_list_gmu_silu_scat_kernel(
             gate(c)
             if nt + 1 < TILES:
                 if h == 0:
-                    z_bf[nt + 1] = reuse.tile([P, Z_PASSES, P, PACK], BF16, name=f"z_bf{nt + 1}", align_bytes=64, offset=slot)
+                    z_bf[nt + 1] = reuse.tile([P, Z_PASSES, P, PACK], BF16, name=f"z_bf{nt + 1}", align_bytes=64, offset=LAST_RAW_AT + 2560 if c == 0 else slot)
                     cast_z(nc.vector.tensor_copy, nt + 1, 0)
                 else:
                     quantize_z(nt + 1, reuse.tile([P, Z_PASSES, P], U32, name=f"z_codes{nt + 1}", align_bytes=64, offset=slot + TILE_BYTES))
@@ -331,11 +342,15 @@ def tile_list_gmu_silu_scat_kernel(
                     silu(n, side)
                 for side in sides:
                     weigh(n, side)
-                turn_base(n)
-                turn_t(n)
-                turn_v(n)
+                if n == 1:
+                    turn_v_first(n)
+                    turn_base(n)
+                else:
+                    turn_base(n)
+                    turn_t(n)
+                    turn_v(n)
                 tanh(n)
-                unload(n)
                 if h == 0 and nt + 1 < TILES:
                     for a in range(1, Z_PASSES):
                         cast_z(nc.scalar.copy, nt + 1, a)
+                unload(n)

@@ -38,8 +38,7 @@ LAST_RAW_AT = RAW_AT + 4096
 WAV_AT = 12288
 SLOT = 3 * TILE_BYTES
 ACT_AT = WAV_AT + SLOT * len(CHUNKS)
-W_ROWS_AT = ACT_AT + 3 * TILE_BYTES
-TABS_AT = W_ROWS_AT + 2 * TILE_BYTES
+TABS_AT = ACT_AT + 2 * TILE_BYTES
 
 BANK = 2048
 HV_BANK, Z_BANK, BASE_BANK = 0, 2, 4
@@ -68,7 +67,7 @@ def tile_list_gmu_silu_scat_kernel(
         wvs = keep.tile([P, 2, N], U8, name="wvs", align_bytes=64)
         wts = keep.tile([P, N], U8, name="wts", align_bytes=64)
         wtw = keep.tile([P, 2 * N], U8, name="wtw", align_bytes=64)
-        w_rows = reuse.tile([P, P], F32, name="w_rows", align_bytes=64, offset=W_ROWS_AT)
+        w_rows = keep.tile([P, P], F32, name="w_rows")
         b_rows = reuse.tile([P, P], F32, name="b_rows", align_bytes=64, offset=WAV_AT)
         half_b = keep.tile([P, TILES], F32, name="half_b")
         ident = keep.tile([P, P], F32, name="ident")
@@ -125,10 +124,10 @@ def tile_list_gmu_silu_scat_kernel(
             )
             z_codes[nt] = codes
 
-        vw = [keep.tile([P, 2, 2 * HALF], U8, name="vw0", align_bytes=64)]
+        vw = [keep.tile([P, 2, 2 * HALF], U8, name=f"vw{h}", align_bytes=64) for h in range(2)]
         tw = [keep.tile([P, HALF], U32, name="tw0", align_bytes=64)]
         ts = [keep.tile([P, HALF], U8, name="ts0", align_bytes=64)]
-        pairs = [keep.tile([P, HALF], U32, name="pairs0", align_bytes=64)]
+        pairs = [keep.tile([P, HALF], U32, name=f"pairs{h}", align_bytes=64) for h in range(2)]
 
         def list_half(tile, h):
             return tile[:, LIST_COLS * h : LIST_COLS * (h + 1)]
@@ -251,25 +250,26 @@ def tile_list_gmu_silu_scat_kernel(
 
         nc.sync.dma_start(list1[:], offs)
         nc.sync.dma_start(out=wtw[:].bitcast(I32), in_=wt_words[0].bitcast(I32))
-        load_wv(0, P)
+        nc.sync.dma_start(list2[:], offs2)
         tab_rows = tab_scales.rearrange("a (q r) t -> r q a t", r=ROWS)
         for r in range(ROWS):
             nc.sync.dma_start(out=tabs[r:P:SECOND, :].bitcast(I32), in_=tab_rows[r].bitcast(I32))
         nc.sync.dma_start(out=tab2w[:].bitcast(I32), in_=tab2_words[0].rearrange("p t i -> p (t i)").bitcast(I32))
-        nc.sync.dma_start(list2[:], offs2)
         for r in range(ROWS):
             load_plane_row(tab2s, tab2_scales[0], r)
-        load_plane_row(wts, wt_scales[0], 0)
+        for r in range(2):
+            load_plane_row(wts, wt_scales[0], r)
         nc.sync.dma_start(out=tabw[:].bitcast(I32), in_=tab_words[0].rearrange("p t i -> p (t i)").bitcast(I32))
-        nc.sync.dma_start(out=w_rows[0:W_COLS, :], in_=wgo[0].rearrange("(r c) -> r c", c=P))
         gather(vs0[:], tabs, list1[:])
         windows.append(reuse.tile([P, T], F32, name="window1", offset=TABS_AT))
         nc.gpsimd.memset(windows[1][:], 0.0)
-        for r in range(1, ROWS):
+        for r in range(2, ROWS):
             load_plane_row(wts, wt_scales[0], r)
+        nc.sync.dma_start(out=w_rows[0:W_COLS, :], in_=wgo[0].rearrange("(r c) -> r c", c=P))
         load_z(0, P, 0)
-        load_z(0, P, 1)
+        load_wv(0, P)
         nc.sync.dma_start(out=vs1[0:PLANE_ROWS, :].bitcast(I32), in_=vs0[SECOND : SECOND + PLANE_ROWS, :].bitcast(I32))
+        load_z(0, P, 1)
         for r in range(ROWS):
             load_plane_row(wvs, wv_scales.rearrange("a r n -> r a n"), r)
         nc.sync.dma_start(out=b_rows[0:TILES, :], in_=b.rearrange("(r c) -> r c", c=P))
@@ -282,31 +282,26 @@ def tile_list_gmu_silu_scat_kernel(
 
         gather(tw[0][:], tab2w, list_half(list2, 0))
         gather(ts[0][:], tab2s, list_half(list2, 0))
-        quarter = HALF // 2
-        for u in range(2):
-            gather(pairs[0][:, quarter * u : quarter * (u + 1)], tabw, list1[:, quarter // 16 * u : quarter // 16 * (u + 1)])
-        for u in range(2):
-            part_v(0, quarter * u, quarter * (u + 1))
-        w_turned = psum.tile([P, P], F32, name="w_turned", offset=BANK * BASE_BANK)
-        nc.tensor.transpose(w_turned[:], w_rows[:], ident[:])
-        nc.vector.tensor_scalar_mul(neg_half_w[:], w_turned[:, 0:W_COLS], -0.5)
-        nc.vector.tensor_scalar_mul(half_w[:], w_turned[:, 0:W_COLS], 0.5)
-        pairs.append(reuse.tile([P, HALF], U32, name="pairs1", align_bytes=64, offset=W_ROWS_AT + 256 - TILE_BYTES))
-        gather(pairs[1][:], tabw, list_half(list1, 1))
-        tw.append(reuse.tile([P, HALF], U32, name="tw1", align_bytes=64, offset=W_ROWS_AT + 256))
-        gather(tw[1][:], tab2w, list_half(list2, 1))
+        for h in range(2):
+            gather(pairs[h][:], tabw, list_half(list1, h))
+        for h in range(2):
+            part_v(h, 0, HALF)
 
         product_ht(0)
         silu(0, "t")
+        w_turned = psum.tile([P, P], F32, name="w_turned", offset=BANK * BASE_BANK)
+        nc.tensor.transpose(w_turned[:], w_rows[:], ident[:])
+        nc.scalar.activation(out=neg_half_w[:], in_=w_turned[:, 0:W_COLS], func=ACT.Copy, scale=-0.5)
+        nc.scalar.activation(out=half_w[:], in_=w_turned[:, 0:W_COLS], func=ACT.Copy, scale=0.5)
         weigh(0, "t")
         z_bf[0] = keep.tile([P, Z_PASSES, P, PACK], BF16, name="z_bf0", align_bytes=64)
         for a in range(Z_PASSES):
             cast_z(nc.scalar.copy, 0, a)
+        tw.append(reuse.tile([P, HALF], U32, name="tw1", align_bytes=64, offset=RAW_AT))
+        gather(tw[1][:], tab2w, list_half(list2, 1))
         first_codes = keep.tile([P, Z_PASSES, P], U32, name="z_codes0", align_bytes=64)
         quantize_z(0, first_codes, 0, Z_PASSES - 1)
         quantize_z(0, first_codes, Z_PASSES - 1, Z_PASSES)
-        vw.append(reuse.tile([P, 2, 2 * HALF], U8, name="vw1", align_bytes=64, offset=LAST_RAW_AT + 512 - TILE_BYTES))
-        part_v(1, 0, HALF)
         product_hv(0)
         silu(0, "v")
         weigh(0, "v")

@@ -70,7 +70,6 @@ def tile_list_gmu_silu_scat_kernel(
         w_rows = keep.tile([P, P], F32, name="w_rows")
         b_rows = reuse.tile([P, P], F32, name="b_rows", align_bytes=64, offset=WAV_AT)
         half_b = keep.tile([P, TILES], F32, name="half_b")
-        ident = keep.tile([P, P], F32, name="ident")
         half_w = keep.tile([P, W_COLS], F32, name="half_w")
         neg_half_w = keep.tile([P, W_COLS], F32, name="neg_half_w")
         windows = [keep.tile([P, T], F32, name="window0")]
@@ -81,9 +80,8 @@ def tile_list_gmu_silu_scat_kernel(
         nc.vector.memset(wvs[:].rearrange("p a n -> p (a n)").bitcast(I32), 0)
         nc.vector.memset(vs1[:].bitcast(I32), 0)
         nc.vector.memset(windows[0][:], 0.0)
-        nc.gpsimd.memset(w_rows[:], 0.0)
-        make_identity(nc, ident[:])
-        nc.gpsimd.memset(b_rows[:], 0.0)
+        nc.vector.memset(w_rows[:], 0.0)
+        nc.vector.memset(b_rows[:], 0.0)
 
         z_raw = {}
         wv_cols = {}
@@ -261,7 +259,9 @@ def tile_list_gmu_silu_scat_kernel(
             load_plane_row(wts, wt_scales[0], r)
         nc.sync.dma_start(out=tabw[:].bitcast(I32), in_=tab_words[0].rearrange("p t i -> p (t i)").bitcast(I32))
         gather(vs0[:], tabs, list1[:])
-        windows.append(reuse.tile([P, T], F32, name="window1", offset=TABS_AT))
+        ident = reuse.tile([P, P], F32, name="ident", offset=TABS_AT)
+        make_identity(nc, ident[:])
+        windows.append(reuse.tile([P, T], F32, name="window1", offset=TABS_AT + 4 * P))
         nc.gpsimd.memset(windows[1][:], 0.0)
         for r in range(2, ROWS):
             load_plane_row(wts, wt_scales[0], r)

from contextlib import ExitStack

import concourse.mybir as mybir
from concourse.masks import make_identity

K, L, N, T, J = 1024, 512, 512, 2048, 1024
FLOPS = 2 * 2 * (K + L) * N * J

F32 = mybir.dt.float32
BF16 = mybir.dt.bfloat16
I32 = mybir.dt.int32
U32 = mybir.dt.uint32
U16 = mybir.dt.uint16
U8 = mybir.dt.uint8
FP8X4 = mybir.dt.float8_e4m3fn_x4
FP4X4 = mybir.dt.float4_e2m1fn_x4
ACT = mybir.ActivationFunctionType
ALU = mybir.AluOpType

P = 128
PACK = 4
PASS = P * PACK
Z_PASSES = (K + L) // PASS
QUAD = 32
ROWS = 4
SECOND = 16
HALF = 512
BLOCKS = HALF // P
LIST_COLS = HALF // 16
TILES = N // P
W_COLS = J // P
CHUNKS = [(nt, h) for nt in range(TILES) for h in range(J // HALF)]
PLANE_ROWS = QUAD * 3 + ROWS

TILE_BYTES = 4 * HALF
RAW_AT = 0
LAST_RAW_AT = RAW_AT + 4096
WAV_AT = 12288
SLOT = 3 * TILE_BYTES
ACT_AT = WAV_AT + SLOT * len(CHUNKS)
TABS_AT = ACT_AT + 2 * TILE_BYTES

BANK = 2048
HV_BANK, Z_BANK, BASE_BANK = 0, 2, 4
HT_BANKS = (1, HV_BANK, 3, 3, 5, 3, 1, 5)
DIFF_BANKS = (6, 7)


def tile_list_gmu_silu_scat_kernel(
    tc, tab_words, tab_scales, tab2_words, tab2_scales, zv, zt, b, wv_words, wv_scales, wt_words, wt_scales, wgo, offs, offs2, out
):
    nc = tc.nc
    with ExitStack() as ctx:
        keep = ctx.enter_context(tc.tile_pool(name="keep", bufs=1))
        reuse = ctx.enter_context(tc.tile_pool(name="reuse", bufs=1))
        work = ctx.enter_context(tc.tile_pool(name="work", bufs=3))
        psum = ctx.enter_context(tc.psum_pool(name="psum", bufs=1))

        list1 = keep.tile([P, J // 16], U16, name="list1")
        list2 = keep.tile([P, J // 16], U16, name="list2")
        tabw = keep.tile([P, T], U32, name="tabw")
        tab2w = keep.tile([P, T], U32, name="tab2w")
        tabs = reuse.tile([P, T], U8, name="tabs", offset=TABS_AT)
        tab2s = keep.tile([P, T], U8, name="tab2s")
        vs0 = keep.tile([P, J], U8, name="vs0", align_bytes=64)
        vs1 = keep.tile([P, J], U8, name="vs1", align_bytes=64)
        wvs = keep.tile([P, 2, N], U8, name="wvs", align_bytes=64)
        wts = keep.tile([P, N], U8, name="wts", align_bytes=64)
        wtw = keep.tile([P, 2 * N], U8, name="wtw", align_bytes=64)
        w_rows = keep.tile([P, P], F32, name="w_rows")
        b_rows = reuse.tile([P, P], F32, name="b_rows", align_bytes=64, offset=WAV_AT)
        half_b = keep.tile([P, TILES], F32, name="half_b")
        half_w = keep.tile([P, W_COLS], F32, name="half_w")
        neg_half_w = keep.tile([P, W_COLS], F32, name="neg_half_w")
        windows = [keep.tile([P, T], F32, name="window0")]

        nc.vector.memset(tabs[:].bitcast(I32), 0)
        nc.vector.memset(tab2s[:].bitcast(I32), 0)
        nc.vector.memset(wts[:].bitcast(I32), 0)
        nc.vector.memset(wvs[:].rearrange("p a n -> p (a n)").bitcast(I32), 0)
        nc.vector.memset(vs1[:].bitcast(I32), 0)
        nc.vector.memset(windows[0][:], 0.0)
        nc.vector.memset(w_rows[:], 0.0)
        nc.vector.memset(b_rows[:], 0.0)

        z_raw = {}
        wv_cols = {}

        def load_wv(n0, n1):
            tile = keep.tile([P, 2, n1 - n0], U32, name=f"wvw{n0}", align_bytes=64)
            nc.sync.dma_start(out=tile[:].bitcast(I32), in_=wv_words[:, :, n0:n1, :].rearrange("a p n i -> p a (n i)").bitcast(I32))
            for nt in range(n0 // P, n1 // P):
                wv_cols[nt] = tile[:, :, P * nt - n0 : P * (nt + 1) - n0]

        def load_z(n0, n1, a):
            if n0 == 0:
                tile = reuse.tile([P, PACK, P], F32, name=f"z_raw{a}_{n0}", align_bytes=64, offset=RAW_AT + TILE_BYTES * a)
            else:
                tile = keep.tile([P, PACK, n1 - n0], F32, name=f"z_raw{a}_{n0}")
            src = zv[PASS * a : PASS * (a + 1), n0:n1] if a < K // PASS else zt[:, n0:n1]
            nc.sync.dma_start(out=tile[:], in_=src.rearrange("(p i) n -> p i n", i=PACK))
            for nt in range(n0 // P, n1 // P):
                z_raw[(nt, a)] = tile[:, :, P * nt - n0 : P * (nt + 1) - n0]

        def load_plane_row(tile, scales, r):
            nc.sync.dma_start(out=tile[r:P:QUAD].bitcast(I32), in_=scales[r : 4 * ROWS : ROWS].bitcast(I32))

        z_codes = {}
        z_scales = [keep.tile([P, Z_PASSES, P], U8, name=f"z_scales{nt}", align_bytes=64) for nt in range(TILES)]
        z_bf = {}

        def cast_z(engine_copy, nt, a):
            engine_copy(
                z_bf[nt][:, a, :, :].rearrange("p (c u) i -> p c i u", u=2), z_raw[(nt, a)].rearrange("p i (c u) -> p c i u", u=2)
            )

        def quantize_z(nt, codes, a0=0, a1=Z_PASSES):
            nc.vector.quantize_mx(
                out=codes[:, a0:a1, :].rearrange("p s n -> p (s n)").bitcast(FP8X4),
                scales=z_scales[nt][:, a0:a1, :].rearrange("p s n -> p (s n)"),
                in_=z_bf[nt][:, a0:a1, :, :].rearrange("p s n i -> p (s n i)"),
            )
            z_codes[nt] = codes

        vw = [keep.tile([P, 2, 2 * HALF], U8, name=f"vw{h}", align_bytes=64) for h in range(2)]
        tw = [keep.tile([P, HALF], U32, name="tw0", align_bytes=64)]
        ts = [keep.tile([P, HALF], U8, name="ts0", align_bytes=64)]
        pairs = [keep.tile([P, HALF], U32, name=f"pairs{h}", align_bytes=64) for h in range(2)]

        def list_half(tile, h):
            return tile[:, LIST_COLS * h : LIST_COLS * (h + 1)]

        def gather(dst, table, offsets):
            nc.vector.tensor_copy(dst, table[:].indirect(offsets))

        def part_v(h, j0, j1):
            nc.vector.tensor_copy(vw[h][:].bitcast(U16)[:, :, j0:j1], pairs[h][:, j0:j1].bitcast(U16).rearrange("p (j d) -> p d j", d=2))

        stage = {c: {} for c in range(len(CHUNKS))}

        def product_ht(c):
            nt, h = CHUNKS[c]
            ht = psum.tile([P, BLOCKS, P], F32, name=f"ht{c}", offset=BANK * HT_BANKS[c])
            for blk in range(BLOCKS):
                nc.tensor.matmul_mx(
                    out=ht[:, blk, :], lhsT=tw[h][:, P * blk : P * (blk + 1)].bitcast(FP8X4), lhsT_scale=ts[h][:, P * blk : P * (blk + 1)],
                    rhs=wtw[:, 2 * P * nt : 2 * P * (nt + 1)].bitcast(FP4X4), rhs_scale=wts[:, P * nt : P * (nt + 1)], start=True, stop=True,
                )
            stage[c]["ht"] = ht

        def product_hv(c):
            nt, h = CHUNKS[c]
            hv = psum.tile([P, BLOCKS, P], F32, name=f"hv{c}", offset=BANK * (Z_BANK if c == 1 else HV_BANK))
            for a, plane in enumerate((vs0, vs1)):
                for blk in range(BLOCKS):
                    j0 = HALF * h + P * blk
                    nc.tensor.matmul_mx(
                        out=hv[:, blk, :], lhsT=vw[h][:, a, 2 * P * blk : 2 * P * (blk + 1)].bitcast(FP4X4), lhsT_scale=plane[:, j0 : j0 + P],
                        rhs=wv_cols[nt][:, a, :].bitcast(FP8X4), rhs_scale=wvs[:, a, P * nt : P * (nt + 1)],
                        start=(a == 0 and blk == 0), stop=(a == 1 and blk == BLOCKS - 1),
                    )
            stage[c]["hv"] = hv

        def product_z(c):
            nt, h = CHUNKS[c]
            jc = slice(HALF * h, HALF * (h + 1))
            z = psum.tile([P, HALF], F32, name=f"z{c}", offset=BANK * (HV_BANK if c == 0 else DIFF_BANKS[0] if c == 1 else Z_BANK))
            moving = [
                (vw[h][:, 0, :].bitcast(FP4X4), vs0[:, jc]),
                (vw[h][:, 1, :].bitcast(FP4X4), vs1[:, jc]),
                (tw[h][:].bitcast(FP8X4), ts[h][:]),
            ]
            for a, (codes, scales) in enumerate(moving):
                nc.tensor.matmul_mx(
                    out=z[:], lhsT=z_codes[nt][:, a, :].bitcast(FP8X4), lhsT_scale=z_scales[nt][:, a, :],
                    rhs=codes, rhs_scale=scales, start=(a == 0), stop=(a == Z_PASSES - 1),
                )
            stage[c]["z"] = z

        def silu(c, side):
            act = reuse.tile([P, BLOCKS, P], F32, name=f"a{side}{c}", offset=ACT_AT + TILE_BYTES * (side == "t"))
            nc.scalar.activation(out=act[:], in_=stage[c]["h" + side][:], func=ACT.Silu)
            stage[c]["a" + side] = act

        def weigh(c, side):
            h = CHUNKS[c][1]
            if side == "v":
                weighted = reuse.tile([P, BLOCKS, P], F32, name=f"wav{c}", align_bytes=64, offset=LAST_RAW_AT + 1024 if c == 0 else WAV_AT + SLOT * c + TILE_BYTES)
                factor = half_w
            else:
                weighted = work.tile([P, BLOCKS, P], F32, name="wat")
                factor = neg_half_w
            for blk in range(BLOCKS):
                col = BLOCKS * h + blk
                nc.scalar.activation(out=weighted[:, blk, :], in_=stage[c]["a" + side][:, blk, :], func=ACT.Copy, scale=factor[:, col : col + 1])
            stage[c]["wa" + side] = weighted

        def tanh(c):
            nt = CHUNKS[c][0]
            th = work.tile([P, HALF], F32, name="th")
            nc.scalar.activation(out=th[:], in_=stage[c]["z"][:], func=ACT.Tanh, bias=half_b[:, nt : nt + 1], scale=0.5)
            stage[c]["th"] = th

        def turn_base(c):
            st = stage[c]
            st["base"] = psum.tile([P, BLOCKS, P], F32, name=f"base{c}", offset=BANK * BASE_BANK)
            for blk in range(BLOCKS):
                nc.tensor.transpose(st["base"][:, blk, :], st["wat"][:, blk, :], ident[:])

        def turn_t(c):
            st = stage[c]
            st["diff"] = psum.tile([P, BLOCKS, P], F32, name=f"diff{c}", offset=BANK * DIFF_BANKS[c % 2])
            for blk in range(BLOCKS):
                nc.tensor.matmul(st["diff"][:, blk, :], st["wat"][:, blk, :], ident[:], start=(blk == 0), stop=False, is_transpose=True)

        def turn_v(c):
            st = stage[c]
            for blk in range(BLOCKS):
                nc.tensor.matmul(st["diff"][:, blk, :], st["wav"][:, blk, :], ident[:], start=False, stop=(blk == BLOCKS - 1), is_transpose=True)

        def turn_v_first(c):
            st = stage[c]
            st["diff"] = psum.tile([P, BLOCKS, P], F32, name=f"diff{c}", offset=BANK * DIFF_BANKS[c % 2])
            order = list(range(BLOCKS))[::-1] if c == 0 else list(range(BLOCKS))
            for side in "vt":
                for blk in order:
                    first, final = (side, blk) == ("v", order[0]), (side, blk) == ("t", order[-1])
                    nc.tensor.matmul(st["diff"][:, blk, :], st["wa" + side][:, blk, :], ident[:], start=first, stop=final, is_transpose=True)

        def unload(c):
            st = stage[c]
            base_sb = work.tile([P, HALF], F32, name="base_sb")
            nc.scalar.activation(out=base_sb[:], in_=st["base"][:].rearrange("p b j -> p (b j)"), func=ACT.Copy, scale=-2.0)
            st["base_sb"] = base_sb

        def gate(c):
            st = stage[c]
            gated = work.tile([P, HALF], F32, name="gated")
            nc.vector.scalar_tensor_tensor(gated[:], st["th"][:], 1.0, st["diff"][:].rearrange("p b j -> p (b j)"), ALU.add, ALU.mult)
            st["gated"] = gated

        def scatter(c):
            nt, h = CHUNKS[c]
            window = windows[nt % 2]
            nc.vector.tensor_tensor(window[:].indirect(list_half(list1, h)), stage[c]["gated"][:], stage[c]["base_sb"][:], ALU.add)
            if h == 1:
                nc.sync.dma_start(out=out[P * nt : P * (nt + 1), :], in_=window[:])

        nc.sync.dma_start(list1[:], offs)
        nc.sync.dma_start(out=wtw[:].bitcast(I32), in_=wt_words[0].bitcast(I32))
        nc.sync.dma_start(list2[:], offs2)
        tab_rows = tab_scales.rearrange("a (q r) t -> r q a t", r=ROWS)
        for r in range(ROWS):
            nc.sync.dma_start(out=tabs[r:P:SECOND, :].bitcast(I32), in_=tab_rows[r].bitcast(I32))
        nc.sync.dma_start(out=tab2w[:].bitcast(I32), in_=tab2_words[0].rearrange("p t i -> p (t i)").bitcast(I32))
        for r in range(ROWS):
            load_plane_row(tab2s, tab2_scales[0], r)
        for r in range(2):
            load_plane_row(wts, wt_scales[0], r)
        nc.sync.dma_start(out=tabw[:].bitcast(I32), in_=tab_words[0].rearrange("p t i -> p (t i)").bitcast(I32))
        gather(vs0[:], tabs, list1[:])
        ident = reuse.tile([P, P], F32, name="ident", offset=TABS_AT)
        make_identity(nc, ident[:])
        windows.append(reuse.tile([P, T], F32, name="window1", offset=TABS_AT + 4 * P))
        nc.gpsimd.memset(windows[1][:], 0.0)
        for r in range(2, ROWS):
            load_plane_row(wts, wt_scales[0], r)
        nc.sync.dma_start(out=w_rows[0:W_COLS, :], in_=wgo[0].rearrange("(r c) -> r c", c=P))
        load_z(0, P, 0)
        load_wv(0, P)
        nc.sync.dma_start(out=vs1[0:PLANE_ROWS, :].bitcast(I32), in_=vs0[SECOND : SECOND + PLANE_ROWS, :].bitcast(I32))
        load_z(0, P, 1)
        for r in range(ROWS):
            load_plane_row(wvs, wv_scales.rearrange("a r n -> r a n"), r)
        nc.sync.dma_start(out=b_rows[0:TILES, :], in_=b.rearrange("(r c) -> r c", c=P))
        load_z(0, P, 2)
        for a in range(Z_PASSES):
            load_z(P, 2 * P, a)
        load_wv(P, N)
        for a in range(Z_PASSES):
            load_z(2 * P, N, a)

        gather(tw[0][:], tab2w, list_half(list2, 0))
        gather(ts[0][:], tab2s, list_half(list2, 0))
        for h in range(2):
            gather(pairs[h][:], tabw, list_half(list1, h))
        for h in range(2):
            part_v(h, 0, HALF)

        product_ht(0)
        silu(0, "t")
        w_turned = psum.tile([P, P], F32, name="w_turned", offset=BANK * BASE_BANK)
        nc.tensor.transpose(w_turned[:], w_rows[:], ident[:])
        nc.scalar.activation(out=neg_half_w[:], in_=w_turned[:, 0:W_COLS], func=ACT.Copy, scale=-0.5)
        nc.scalar.activation(out=half_w[:], in_=w_turned[:, 0:W_COLS], func=ACT.Copy, scale=0.5)
        weigh(0, "t")
        z_bf[0] = keep.tile([P, Z_PASSES, P, PACK], BF16, name="z_bf0", align_bytes=64)
        for a in range(Z_PASSES):
            cast_z(nc.scalar.copy, 0, a)
        tw.append(reuse.tile([P, HALF], U32, name="tw1", align_bytes=64, offset=RAW_AT))
        gather(tw[1][:], tab2w, list_half(list2, 1))
        first_codes = keep.tile([P, Z_PASSES, P], U32, name="z_codes0", align_bytes=64)
        quantize_z(0, first_codes, 0, Z_PASSES - 1)
        quantize_z(0, first_codes, Z_PASSES - 1, Z_PASSES)
        product_hv(0)
        silu(0, "v")
        weigh(0, "v")
        product_z(0)
        turn_v_first(0)
        b_turned = psum.tile([P, P], F32, name="b_turned", offset=BANK * BASE_BANK)
        nc.tensor.transpose(b_turned[:], b_rows[:], ident[:])
        ts.append(reuse.tile([P, HALF], U8, name="ts1", align_bytes=64, offset=LAST_RAW_AT + 512))
        gather(ts[1][:], tab2s, list_half(list2, 1))
        nc.scalar.activation(out=half_b[:], in_=b_turned[:, 0:TILES], func=ACT.Copy, scale=0.5)
        tanh(0)
        turn_base(0)
        unload(0)

        for c in range(len(CHUNKS)):
            nt, h = CHUNKS[c]
            slot = WAV_AT + SLOT * c
            gate(c)
            if nt + 1 < TILES:
                if h == 0:
                    z_bf[nt + 1] = reuse.tile([P, Z_PASSES, P, PACK], BF16, name=f"z_bf{nt + 1}", align_bytes=64, offset=LAST_RAW_AT + 2560 if c == 0 else slot)
                    cast_z(nc.vector.tensor_copy, nt + 1, 0)
                else:
                    quantize_z(nt + 1, reuse.tile([P, Z_PASSES, P], U32, name=f"z_codes{nt + 1}", align_bytes=64, offset=slot + TILE_BYTES))
            scatter(c)
            n = c + 1
            if n < len(CHUNKS):
                sides = "vt" if n == 1 else "tv"
                for side in sides:
                    (product_hv if side == "v" else product_ht)(n)
                product_z(n)
                for side in sides:
                    silu(n, side)
                for side in sides:
                    weigh(n, side)
                if n == 1:
                    turn_v_first(n)
                    turn_base(n)
                else:
                    turn_base(n)
                    turn_t(n)
                    turn_v(n)
                tanh(n)
                if h == 0 and nt + 1 < TILES:
                    for a in range(1, Z_PASSES):
                        cast_z(nc.scalar.copy, nt + 1, a)
                unload(n)
